import numpy as np, ml_dtypes
CORES = [35,38,43,46]
N = 4
import mx_ref
BF = ml_dtypes.bfloat16
def f(rng, *shape):
    return mx_ref.flush((rng.standard_normal(shape, dtype=np.float32) * np.exp2(rng.integers(-2, 3, shape[:-1] + (1,)))).astype(BF))
def wide(rng, *shape, cols=0):
    v = rng.standard_normal(shape, dtype=np.float32) * np.exp2(rng.integers(-12, 13, shape)).astype(np.float32)
    if cols: v *= np.repeat(np.exp2(rng.integers(-cols, cols + 1, shape[:-2] + (1, shape[-1] // 4))) * (rng.random(shape[:-2] + (1, shape[-1] // 4)) > 0.0625), 4, axis=-1).astype(np.float32)
    return mx_ref.flush(v.astype(BF))
T, NB, CH, BW = 512, 4, 128, 128
def scores(x, u):
    return np.stack([mx_ref.matmul(mx_ref.quantize(u[s]), mx_ref.quantize(x[s]))[0] for s in range(N)]) + np.float32(0.0)
def dealt(rng, d, place):
    v = d["x"].reshape(N, 128, T, 4).transpose(0, 2, 1, 3).reshape(N * T, 128, 4)
    g = np.argsort(-scores(d["x"], d["u"]).reshape(-1), kind="stable")
    e = np.stack([g[rng.permutation(place[s])] for s in range(N)])
    return np.ascontiguousarray(v[e].transpose(0, 2, 1, 3)).reshape(N, 128, 4 * T)
def setup_inputs(rng):
    u = np.zeros((N, 128, 512), BF); u[:, :, :4] = f(rng, 128, 4)
    return {"x": f(rng, N, 128, 4 * T), "u": u, "w": f(rng, N, 128, 512 * NB)}
def setup_inputs_ties(rng):
    d = setup_inputs(rng); d["u"][:, 64:] = 0; few = f(rng, 64, 24).reshape(64, 6, 4)
    for s in range(N):
        e = rng.permutation(np.concatenate([np.arange(6), rng.choice(6, T - 6, p=rng.dirichlet(np.ones(6)))]))
        d["x"][s, :64] = few[:, e].reshape(64, -1)
    return d
def setup_inputs_blocks(rng):
    d = setup_inputs(rng); d["x"] = dealt(rng, d, np.arange(N * T).reshape(N, T)[rng.permutation(N)]); return d
def setup_inputs_alternate(rng):
    d = setup_inputs(rng); d["x"] = dealt(rng, d, np.arange(N * T).reshape(T, N).T[rng.permutation(N)]); return d
def setup_inputs_zeros(rng):
    d = setup_inputs(rng); d["u"][:, 64:] = 0
    for s in rng.permutation(N)[:N // 2]: d["x"][s, :64] = 0
    return d
def setup_inputs_spread(rng):
    d = setup_inputs(rng); k = np.where(rng.permutation(N) < N // 2, np.float32(2.0 ** -20), np.float32(2.0 ** 7))
    d["x"] = mx_ref.flush((wide(rng, N, 128, 4 * T, cols=8).astype(np.float32) * k[:, None, None]).astype(BF))
    d["u"] = (d["u"].astype(np.float32) * np.float32(2 ** 24)).astype(BF); return d
def check_inputs(d):
    b = []; u = np.asarray(d["u"]).astype(np.float32)
    for r in range(N):
        if (u[r][:, 4:] != 0).any() or (u[r] != u[0]).any(): b.append("u")
    return b
def reference(x, u, w):
    score = scores(x, u)
    order = [np.argsort(-score[s], kind="stable") for s in range(N)]
    y = np.zeros((N, 128, T), np.float32); ids = np.zeros((N, 2, T), np.float32)
    for d in range(N):
        runs = [order[s][CH * d:CH * d + CH] for s in range(N)]
        rank = np.repeat(np.arange(N), CH); col = np.concatenate(runs)
        m = np.argsort(-score[rank, col], kind="stable")
        rank, col = rank[m], col[m]
        ids[d, 0], ids[d, 1] = rank, col
        t = np.ascontiguousarray(x.reshape(N, 128, T, 4)[rank, :, col].transpose(1, 0, 2)).reshape(128, 4 * T)
        for k in range(NB):
            W = mx_ref.quantize(np.ascontiguousarray(w[d][:, 512 * k:512 * k + 512]))
            y[d][:, BW * k:BW * k + BW] = mx_ref.matmul(W, mx_ref.quantize(np.ascontiguousarray(t[:, 4 * BW * k:4 * BW * k + 4 * BW])))
    return {"y": y, "ids": ids}

@@ -1,0 +1,392 @@
+from concourse.bass import DstId, RemoteDMATransfer
+from concourse.mybir import dt, AluOpType as A, ActivationFunctionType as F
+
+N, CH = 4, 128
+X4 = "float8_e4m3fn_x4"
+
+
+def _sb(n, d):
+    return ("sbuf", [128, n], d)
+
+
+SCRATCH = {
+    "xt": _sb(2048, "bfloat16"), "wt": _sb(2048, "bfloat16"), "ut": _sb(512, "bfloat16"),
+    "xq": _sb(512, X4), "xs": _sb(512, "uint8"), "wq": _sb(512, X4), "ws": _sb(512, "uint8"),
+    "uq": _sb(128, X4), "us": _sb(128, "uint8"), "ubq": _sb(128, X4), "ubs": _sb(128, "uint8"),
+    "sq": _sb(384, X4), "sp": _sb(384, "uint8"), "lq": _sb(512, X4), "lp": _sb(512, "uint8"),
+    "fq": _sb(512, X4), "fp": _sb(512, "uint8"),
+    "zoff": _sb(8, "uint16"), "half": _sb(128, "bfloat16"), "tri": _sb(128, "bfloat16"), "ip": _sb(2, "int32"),
+    "r3": _sb(2, "int32"), "p15": _sb(2, "int32"), "p12": _sb(2, "int32"), "p96": _sb(2, "int32"),
+    "p16": _sb(2, "int32"), "p31": _sb(2, "int32"), "corr0": _sb(2, "float32"), "corr": _sb(2, "float32"),
+    "corw0": _sb(2, "float32"), "corw": _sb(2, "float32"), "quad": _sb(2, "float32"), "tok0": _sb(2, "float32"),
+    "tok": _sb(2, "float32"), "k4": _sb(8, "int32"), "plq": _sb(8, "uint16"), "lo": _sb(2, "float32"),
+    "hi": _sb(2, "float32"), "pcol": _sb(2, "float32"), "ibias": _sb(2, "float32"), "bl32": _sb(32, "int32"),
+    "bl": _sb(32, "uint16"),
+    "de": _sb(16, "int32"), "de2": _sb(16, "int32"), "da": _sb(16, "bfloat16"), "db": _sb(16, "bfloat16"),
+    "d0": _sb(512, "bfloat16"), "dg": _sb(32, "int32"), "dg2": _sb(32, "int32"), "dga": _sb(32, "bfloat16"),
+    "dgb": _sb(32, "bfloat16"), "d4": _sb(32, "bfloat16"), "zz": _sb(136, "bfloat16"),
+    "idv0": _sb(128, "bfloat16"), "idv": _sb(128, "bfloat16"),
+    "ss": _sb(512, "float32"), "vc": _sb(4, "float32"), "sg": _sb(512, "bfloat16"), "sgb": _sb(768, "bfloat16"),
+    "cb": _sb(2080, "bfloat16"), "es": _sb(768, "bfloat16"), "z1": _sb(544, "bfloat16"),
+    "sl": _sb(128, "float32"), "so": _sb(512, "float32"), "tr": _sb(512, "float32"), "v16": _sb(16, "float32"),
+    "rs": _sb(16, "float32"), "r1": _sb(16, "float32"), "rr": _sb(16, "float32"), "bx": _sb(512, "float32"),
+    "sb": _sb(512, "float32"), "v1": _sb(4, "float32"), "sg2": _sb(768, "bfloat16"), "c2": _sb(1600, "bfloat16"),
+    "z2": _sb(800, "bfloat16"), "li": _sb(32, "uint16"), "ia": _sb(16, "bfloat16"), "ib": _sb(16, "bfloat16"),
+    "inn": _sb(512, "bfloat16"), "iw": _sb(512, "bfloat16"), "q2": _sb(8, "uint16"), "gid": _sb(128, "float32"),
+    "ysb": _sb(512, "float32"),
+    "ps": ("psum", [128, 4096], "float32"),
+}
+for _k in ("1", "2"):
+    SCRATCH.update({"pt" + _k: _sb(32, "bfloat16"), "pg" + _k: _sb(32, "float16"), "pw" + _k: _sb(8, "uint16"),
+                    "wi" + _k: _sb(512, "bfloat16"), "wx" + _k: _sb(512, "float16"), "ge" + _k: _sb(32, "float16"),
+                    "gm" + _k: _sb(32, "float16"), "lw" + _k: _sb(32, "uint16")})
+SEMAPHORES = ["v", "a", "t", "q", "du", "dx0", "dx1", "dx2", "dx3", "dw", "dst",
+              "rem_s", "rem_c", "rem_p", "rem_i", "loc"]
+
+
+def _routes(core, cores, topo):
+    far = [c for c in cores if c != core and topo.chip(c) != topo.chip(core)]
+    near = [c for c in cores if c != core and topo.chip(c) == topo.chip(core)]
+    out, used = {}, set()
+    for i, c in enumerate(far):
+        e = topo.engines(core, c)
+        k = 1
+        while 2 * k * len(far) <= len(e):
+            k *= 2
+        out[c] = e[i * k:i * k + k]
+        used.update(out[c])
+    for i, c in enumerate(near):
+        e = [n for n in topo.engines(core, c) if n not in used]
+        k = 1
+        while 2 * k * len(near) <= len(e):
+            k *= 2
+        out[c] = e[i * k:i * k + k]
+    return out
+
+
+def rank_program(g, core, T, topo):
+    rank = T.rank_of(core)
+    if rank is None:
+        return
+    cores = T.cores
+    others = [d for d in range(N) if d != rank]
+    routes = _routes(core, cores, topo)
+    FEW = 4
+
+    def arrive(sem):
+        n = [len(_routes(c, cores, topo)[core]) for c in cores if c != core]
+        return (sem, sum(min(k, FEW) for k in n) if sem == "rem_s" else sum(n))
+
+    U32, U8 = dt.uint32, dt.uint8
+
+    V = {"q": g.vector, "sem": "v", "n": 0, "seen": {}}
+    S = {"q": g.scalar, "sem": "a", "n": 0, "seen": {}}
+    P = {"q": g.tensor, "sem": "t", "n": 0, "seen": {}}
+    G = {"q": g, "sem": "q", "n": 0, "seen": {}}
+    Y = {"q": g.sync, "sem": None, "n": 0, "seen": {}}
+    dmas = {}
+
+    def need(E, deps):
+        for s, n in deps:
+            if E["seen"].get(s, 0) < n:
+                E["q"].wait_ge(T.sem[s], n)
+                E["seen"][s] = n
+
+    def op(E, deps, call, *a, **k):
+        need(E, deps)
+        call(*a, **k).then_inc(T.sem[E["sem"]], 1)
+        E["n"] += 1
+        return (E["sem"], E["n"])
+
+    def dma(E, deps, out, in_, sem):
+        need(E, deps)
+        E["q"].dma_start(out, in_).then_inc(T.sem[sem], 16)
+        dmas[sem] = dmas.get(sem, 0) + 16
+        return (sem, dmas[sem])
+
+    def send(deps, pieces, sem):
+        need(G, deps)
+        tr = []
+        for d, src, dst in pieces:
+            rid, pid, _ = topo.addr(cores[d])
+            engines = routes[cores[d]][:FEW] if sem == "rem_s" else routes[cores[d]]
+            tr.append(RemoteDMATransfer(dst_ids=[DstId(rid=rid, pnc=pid)],
+                                        dma_engine_mask=sum(1 << e for e in engines),
+                                        remote_sem=T.sem[sem], src=src, dst=dst))
+            dmas["loc"] = dmas.get("loc", 0) + len(engines)
+        g.remote_dma_fused(tr, local_sem=T.sem.loc)
+
+    vec, act, pe = g.vector, g.scalar.activation, g.tensor.matmul_mx
+    cp, ts, tt, scan = vec.tensor_copy, vec.tensor_scalar, vec.tensor_tensor, vec.tensor_tensor_scan
+
+    def r(c, w=128):
+        return slice(w * c, w * c + w)
+
+    def iota(out, pattern, base, mult, small=True):
+        return op(G, [], g.iota, out, pattern, base, mult, allow_small_or_imprecise_dtypes=small)
+
+    dx = [None] * 4
+    dx[0] = dma(Y, [], T.xt[:, r(0, 512)], T.x[:, r(0, 512)], "dx0")
+    du = dma(S, [], T.ut[:, 0:8], T.u[:, 0:8], "du")
+    for c in (1, 2, 3):
+        dx[c] = dma(S if c & 1 else Y, [], T.xt[:, r(c, 512)], T.x[:, r(c, 512)], "dx%d" % c)
+    dw = dma(Y, [], T.wt[:], T.w[:], "dw")
+
+    k_ip = iota(T.ip[:], [[0, 2]], 0, 1, False)
+    k_de = iota(T.de[:], [[1, 16]], 2048, -1, False)
+    k_dg = iota(T.dg[:], [[4, 32]], 2051, -1, False)
+    k_k4 = iota(T.k4[:], [[4, 8]], 0, 0, False)
+    mh = op(V, [], vec.memset, T.half[:], 0.5)
+    m0 = op(V, [], vec.memset, T.ut[:, 8:512], 0.0)
+    mz = op(V, [], vec.memset, T.zoff[:], 0)
+    k_tri = op(G, [mh], g.affine_select, T.tri[:], T.half[:], [[-1, 128]], A.is_gt, -0.5, 0, 1)
+    k_i0 = iota(T.idv0[:], [[4, 8], [1, 4], [128, 4]], -256, 0)
+    for c in range(4):
+        iota(T.cb[:, 520 * c + 512:520 * c + 520], [[0, 8]], 0, 0)
+    k_zz = iota(T.zz[:], [[0, 136]], 0, 0)
+    mw1 = iota(T.wi1[:], [[0, 512]], -512, 0)
+    k_bl = iota(T.bl32[:], [[1, 16], [0, 2]], 0, 0, False)
+    for s in range(N):
+        for b in (192, 392):
+            iota(T.c2[:, 400 * s + b:400 * s + b + 8], [[0, 8]], 0, 0)
+    k_pc = iota(T.pcol[:], [[0, 2]], -256, 1)
+    mi = iota(T.inn[:], [[1, 4], [0, 128]], 0, 0)
+    a96 = op(V, [k_ip], ts, T.p96[:], T.ip[:], 96, None, A.bitwise_and)
+    a3 = op(V, [k_ip], ts, T.r3[:], T.ip[:], 3, None, A.bitwise_and)
+    a15 = op(V, [k_ip], ts, T.p15[:], T.ip[:], 15, None, A.bitwise_and)
+    a12 = op(V, [k_ip], ts, T.p12[:], T.ip[:], 12, None, A.bitwise_and)
+    k_qd = op(V, [a96], ts, T.quad[:], T.p96[:], 1, None, A.mult)
+    ade = op(V, [k_de], ts, T.de2[:], T.de[:], 15, None, A.bitwise_and)
+    adg = op(V, [k_dg], ts, T.dg2[:], T.dg[:], 12, None, A.bitwise_and)
+    k_c0 = op(V, [a15], ts, T.corr0[:], T.p15[:], 15, 1024, A.is_lt, A.mult)
+    k_w0 = op(V, [a12], ts, T.corw0[:], T.p12[:], 12, 1024, A.is_lt, A.mult)
+    for i in range(4):
+        ms = op(S, [mh], act, T.so[:, r(i)], T.half[:], F.Copy, 0.0, -1e29)
+    k_id = op(S, [k_i0, k_qd], act, T.idv[:], T.idv0[:], F.Identity, T.quad[:, 0:1])
+
+    qu = op(V, [m0, du], vec.quantize_mx, T.uq[:], T.us[:], T.ut[:])
+    ub = op(V, [qu, mz], cp, T.ubq[:, 0:128].bitcast(U32), T.uq[:, 0:128].bitcast(U32).indirect(T.zoff[:, 0:8]))
+    ubs = op(S, [qu, mz], act, T.ubs[:, 0:128], T.us[:, 0:128].indirect(T.zoff[:, 0:8]), F.Copy)
+
+    qx, pv, psc, vcol, sc, sgn = [None] * 4, [None] * 4, [None] * 4, [None] * 4, [None] * 4, [None] * 4
+    sgb = {}
+
+    def quant(c):
+        qx[c] = op(V, [dx[c]], vec.quantize_mx, T.xq[:, r(c)], T.xs[:, r(c)], T.xt[:, r(c, 512)])
+        b = 512 * (4 + c)
+        pv[c] = op(P, [qx[c], qu], pe, T.ps[:, b:b + 128], T.xq[:, r(c)], T.xs[:, r(c)], T.uq[:], T.us[:], True, True)
+        b = 512 * c
+        psc[c] = op(P, [ub, ubs], pe, T.ps[:, b:b + 128], T.ubq[:], T.ubs[:], T.xq[:, r(c)], T.xs[:, r(c)], True, True)
+
+    def cb(c, a, b):
+        return T.cb[:, 520 * c + a:520 * c + b]
+
+    def at_b(c, e):
+        return r(c * (c - 1) // 2 + e)
+
+    def work_a(c):
+        row = T.ps[:, 512 * c:512 * c + 128]
+        vcol[c] = op(V, [pv[c]], cp, T.vc[:, c:c + 1], T.ps[:, 512 * (4 + c):512 * (4 + c) + 1])
+        for e in range(c):
+            sgb[c, e] = op(S, [psc[c], vcol[e]], act, T.sgb[:, at_b(c, e)], row, F.Sign, T.vc[:, e:e + 1], -1.0)
+        sgn[c] = op(S, [psc[c], vcol[c]], act, T.sg[:, r(c)], row, F.Sign, T.vc[:, c:c + 1], -1.0)
+        sc[c] = op(S, [], act, T.ss[:, r(c)], row, F.Copy)
+        if c:
+            return op(V, [vcol[c], sc[c - 1]], ts, cb(c, 0, 128 * c), T.ss[:, 0:128 * c], T.vc[:, c:c + 1], None, A.is_ge)
+
+    def work_b(c, e):
+        return op(V, [sgb[c, e]], ts, cb(e, 128 * c, 128 * c + 128), T.sgb[:, at_b(c, e)], 0.0, None, A.is_lt)
+
+    def work_d(c):
+        return op(V, [sgn[c], k_tri], tt, cb(c, 128 * c, 128 * c + 128), T.sg[:, r(c)], T.tri[:], A.is_lt)
+
+    def early(c, dep):
+        return op(V, [dep], scan, T.es[:, r(c, 192)], cb(c, 0, 192), cb(c, 192, 384), -256.0, A.add, A.add)
+
+    def late(c, dep):
+        return op(V, dep + [k_zz], scan, T.z1[:, c:544:4], cb(c, 384, 520), T.zz[:, 0:136],
+                  T.es[:, 192 * c + 191:192 * c + 192], A.add, A.add)
+
+    quant(0)
+    quant(1)
+    k_ga = op(V, [adg], ts, T.dga[:], T.dg2[:], 0, -4096, A.is_equal, A.mult)
+    k_gb = op(V, [adg], ts, T.dgb[:], T.dg2[:], 4, 1024, A.is_equal, A.mult)
+    k_da = op(V, [ade], ts, T.da[:], T.de2[:], 0, -4096, A.is_equal, A.mult)
+    k_db = op(V, [ade], ts, T.db[:], T.de2[:], 1, 1024, A.is_equal, A.mult)
+    k_t0 = op(V, [k_qd], ts, T.tok0[:], T.r3[:], 128, T.quad[:, 0:1], A.mult, A.add)
+    work_a(0)
+    k_d4 = op(V, [k_ga, k_gb], tt, T.d4[:], T.dga[:], T.dgb[:], A.add)
+    k_d0 = op(V, [k_da, k_db], tt, T.d0[:, 0:16], T.da[:], T.db[:], A.add)
+    k_co = op(V, [k_c0], ts, T.corr[:], T.corr0[:], 256, None, A.subtract)
+    k_cw = op(V, [k_w0], ts, T.corw[:], T.corw0[:], 256, None, A.subtract)
+    k_tk = op(V, [k_t0], ts, T.tok[:], T.p12[:], 0.25, T.tok0[:, 0:1], A.mult, A.add)
+    work_d(0)
+    k_pl = op(V, [k_tk, k_k4], ts, T.plq[:], T.k4[:], T.tok[:, 0:1], None, A.add)
+    quant(2)
+    work_a(1)
+    work_b(1, 0)
+    work_d(1)
+    work_a(2)
+    quant(3)
+    b0 = work_b(2, 0)
+    b1 = work_b(2, 1)
+    b2 = work_d(2)
+    e0 = early(0, b0)
+    e1 = early(1, b1)
+    e2 = early(2, b2)
+    w3 = work_a(3)
+    b0 = work_b(3, 0)
+    b1 = work_b(3, 1)
+    b2 = work_b(3, 2)
+    e3 = early(3, w3)
+    b3 = work_d(3)
+    late(0, [b0, e0])
+    late(1, [b1, e1])
+    late(2, [b2, e2])
+    fin = late(3, [b3, e3])
+    sl = op(S, [k_pl, sc[3]], act, T.sl[:, 0:128], T.ss[:, 0:512].indirect(T.plq[:, 0:8]), F.Copy)
+    kd = k_d0
+    for n in (16, 32, 64, 128, 256):
+        kd = op(S, [kd], act, T.d0[:, n:2 * n], T.d0[:, 0:n], F.Copy)
+    for i in range(4):
+        mw2 = op(S, [mh], act, T.wi2[:, r(i)], T.half[:], F.Copy, 0.0, -1024.0)
+
+    def offsets(fin, z, k, fill=None):
+        x = op(V, [fin], vec.transpose, T["pt" + k][:], z)
+        if fill:
+            fill()
+        x = op(V, [x, k_d4], scan, T["pg" + k][:], T.d4[:], T["pt" + k][:], 0.0, A.add, A.max)
+        return op(V, [x, k_cw], ts, T["pw" + k][:, 0:8], T["pg" + k][:, 3:32:4], T.corw[:, 0:1], None, A.subtract)
+
+    def scatter(x, k, mw):
+        return op(V, [x, k_id, mw], cp, T["wi" + k][:, 0:512].indirect(T["pw" + k][:, 0:8]), T.idv[:, 0:128])
+
+    def diagonal(x, k):
+        return op(V, [x, kd], scan, T["wx" + k][:], T.d0[:], T["wi" + k][:], 0.0, A.add, A.max)
+
+    def quadrants(x, mid, out, w, src):
+        for a in range(4):
+            p, o = slice(32 * a, 32 * a + 32), slice(32 * (a ^ 1), 32 * (a ^ 1) + 32)
+            y = op(V, x, tt, mid[p, 0:w], src(p), src(o), A.max)
+        for a in range(2):
+            p, o = slice(64 * a, 64 * a + 64), slice(64 * (a ^ 1), 64 * (a ^ 1) + 64)
+            z = op(V, [y], tt, out[p, 0:w], mid[p, 0:w], mid[o, 0:w], A.max)
+        return z
+
+    def number_list(x, k):
+        wx = T["wx" + k]
+        x = quadrants([x], T["ge" + k], T["gm" + k], 32, lambda p: wx[p, 15:512:16])
+        return x, op(V, [x, k_co], ts, T["lw" + k][:, 0:32], T["gm" + k][:, 0:32], T.corr[:, 0:1], None, A.subtract)
+
+    pw = offsets(fin, T.z1[:, 512:544], "1")
+    so = op(V, [pw, sl, ms], cp, T.so[:, 0:512].indirect(T.pw1[:, 0:8]), T.sl[:, 0:128])
+    wi = scatter(pw, "1", mw1)
+    x = op(V, [so], vec.transpose, T.tr[:], T.so[:])
+    wx = diagonal(wi, "1")
+    v16 = op(V, [x], cp, T.v16[:], T.tr[:, 0:512:32])
+    send([v16], [(d, T.v16[:, 4 * d:4 * d + 4], T.rs[:, 4 * rank:4 * rank + 4]) for d in others], "rem_s")
+    rso = op(S, [v16], act, T.rs[:, 4 * rank:4 * rank + 4], T.v16[:, 4 * rank:4 * rank + 4], F.Copy)
+    gm, lw = number_list(wx, "1")
+    send([lw], [(d, T.lw1[:, 8 * d:8 * d + 8], T.li[:, 8 * rank:8 * rank + 8]) for d in others], "rem_i")
+
+    spans = []
+    for i, d in enumerate(others):
+        if spans and spans[-1][1] + spans[-1][2] == d:
+            spans[-1][2] += 1
+        else:
+            spans.append([i, d, 1])
+    for i, d, n in spans:
+        of = T.lw1[:, 8 * d:8 * d + 8 * n]
+        at = slice(128 * i, 128 * i + 128 * n)
+        pq = op(V, [lw], cp, T.sq[:, at].bitcast(U32), T.xq[:, 0:512].bitcast(U32).indirect(of))
+        pp = op(S, [lw], act, T.sp[:, at], T.xs[:, 0:512].indirect(of), F.Copy)
+    send([pq], [(d, T.sq[:, r(i)].bitcast(U8), T.lq[:, r(rank)].bitcast(U8)) for i, d in enumerate(others)], "rem_c")
+    send([pp], [(d, T.sp[:, r(i)], T.lp[:, r(rank)]) for i, d in enumerate(others)], "rem_p")
+
+    of = T.lw1[:, 8 * rank:8 * rank + 8]
+    sbo = op(V, [lw], cp, T.sb[:, r(rank)], T.ss[:, 0:512].indirect(of))
+    k_bl = op(V, [k_bl], cp, T.bl[:], T.bl32[:])
+    oq = op(V, [lw], cp, T.lq[:, r(rank)].bitcast(U32), T.xq[:, 0:512].bitcast(U32).indirect(of))
+    ow = op(S, [lw], act, T.lp[:, r(rank)], T.xs[:, 0:512].indirect(of), F.Copy)
+    lio = op(V, [lw], cp, T.li[:, 8 * rank:8 * rank + 8], of)
+    a16 = op(V, [k_ip], ts, T.p16[:], T.ip[:], 16, None, A.bitwise_and)
+    a31 = op(V, [k_ip], ts, T.p31[:], T.ip[:], 31, None, A.bitwise_and)
+    k_lo = op(V, [a16], ts, T.lo[:], T.p16[:], 16, None, A.is_lt)
+    k_hi = op(V, [a16], ts, T.hi[:], T.p16[:], 16, None, A.is_equal)
+    k_ib = op(V, [a31], ts, T.ibias[:], T.p31[:], 1, 256, A.is_equal, A.mult)
+    qw = op(V, [dw], vec.quantize_mx, T.wq[:], T.ws[:], T.wt[:])
+
+    rr = quadrants([arrive("rem_s"), rso], T.r1, T.rr, 16, lambda p: T.rs[p, 0:16])
+    sx = others[2]
+    bx = {sx: op(S, [rr, k_bl], act, T.bx[:, r(sx)], T.rr[:, 0:16].indirect(T.bl[:, 8 * sx:8 * sx + 8]), F.Copy)}
+    for a in range(4):
+        v1 = op(S, [rr], act, T.v1[32 * a:32 * a + 32, 0:4], T.rr[32 * a:32 * a + 32, a:16:4], F.Copy)
+    for d in others[:2]:
+        bx[d] = op(V, [rr, k_bl], cp, T.bx[:, r(d)], T.rr[:, 0:16].indirect(T.bl[:, 8 * d:8 * d + 8]))
+    for d in others:
+        tb = op(V, [bx[d]], vec.transpose, T.sb[:, r(d)], T.bx[:, r(d)])
+
+    def seg(s):
+        return [(0, 128 * s, 0, True)] * (s > 0) + [(128 * s + 128, 512, 128 * s, False)] * (s < 3)
+
+    sg2 = {}
+    for s in (2, 3):
+        for lo, hi, at, ge in seg(s):
+            o = 384 * (s - 2) + at
+            sg2[s] = op(S, [v1, tb, sbo], act, T.sg2[:, o:o + hi - lo], T.sb[:, lo:hi], F.Sign, T.v1[:, s:s + 1], -1.0)
+    done = []
+    for s in range(N):
+        for lo, hi, at, ge in seg(s):
+            end = at + hi - lo
+            for b, e in ([(at, 192), (192, end)] if at < 192 < end else [(at, end)]):
+                w = 400 * s + b + 8 * (b >= 192)
+                out = T.c2[:, w:w + e - b]
+                if s < 2:
+                    x = op(V, [v1, tb, sbo], ts, out, T.sb[:, lo + b - at:lo + e - at], T.v1[:, s:s + 1], None,
+                           A.is_ge if ge else A.is_gt)
+                else:
+                    o = 384 * (s - 2)
+                    x = op(V, [sg2[s]], ts, out, T.sg2[:, o + b:o + e], 0.0, None, A.is_le if ge else A.is_lt)
+        done.append(x)
+    for s in range(N):
+        fin2 = op(V, [done[s], k_pc], scan, T.z2[:, s:800:4], T.c2[:, 400 * s:400 * s + 200],
+                  T.c2[:, 400 * s + 200:400 * s + 400], T.pcol[:, 0:1], A.add, A.add)
+
+    ids = []
+
+    def halves():
+        ids.append(op(V, [lio, k_lo, arrive("rem_i")], ts, T.ia[:], T.li[:, 0:32:2], 256, T.lo[:, 0:1], A.subtract, A.mult))
+        ids.append(op(V, [k_hi], ts, T.ib[:], T.li[:, 1:32:2], 256, T.hi[:, 0:1], A.subtract, A.mult))
+
+    x = offsets(fin2, T.z2[:, 768:800], "2", halves)
+    ic = op(V, ids + [mi], tt, T.inn[:, 1:512:32], T.ia[:], T.ib[:], A.add)
+    x = scatter(x, "2", mw2)
+    x = diagonal(x, "2")
+    iw = op(V, [ic], vec.transpose, T.iw[:], T.inn[:])
+    gm, lm = number_list(x, "2")
+
+    def quad_list(a):
+        p = slice(32 * a, 32 * a + 32)
+        return op(V, [gm], ts, T.q2[p, 0:8], T.gm2[p, 8 * a:8 * a + 8], T.corr[p, 0:1], None, A.subtract)
+
+    quad_list(0)
+    quad_list(1)
+    ym = [None] * 4
+    for k in range(4):
+        of = T.lw2[:, 8 * k:8 * k + 8]
+        a = op(V, [lm, oq, arrive("rem_c")], cp, T.fq[:, r(k)].bitcast(U32), T.lq[:, 0:512].bitcast(U32).indirect(of))
+        b = op(S, [lm, ow, arrive("rem_p")], act, T.fp[:, r(k)], T.lp[:, 0:512].indirect(of), F.Copy)
+        ym[k] = op(P, [a, b, qw], pe, T.ps[:, 512 * k:512 * k + 128], T.wq[:, r(k)], T.ws[:, r(k)], T.fq[:, r(k)], T.fp[:, r(k)], True, True)
+    quad_list(2)
+    ql = quad_list(3)
+    for k in range(3):
+        yc = op(S, [ym[k]], act, T.ysb[:, r(k)], T.ps[:, 512 * k:512 * k + 128], F.Copy)
+        dma(Y, [yc], T.y[:, r(k)], T.ysb[:, r(k)], "dst")
+    ig = op(V, [ql, iw, k_ib], ts, T.gid[:, 0:128], T.iw[:, 0:512].indirect(T.q2[:, 0:8]), T.ibias[:, 0:1], None, A.add)
+    for a in range(4):
+        dma(Y, [ig], T.ids[:, r(a)], T.gid[32 * a:32 * a + 2, 0:128], "dst")
+    yc = op(V, [ym[3]], cp, T.ysb[:, r(3)], T.ps[:, 512 * 3:512 * 3 + 128])
+    dma(S, [yc], T.y[:, r(3)], T.ysb[:, r(3)], "dst")
+
+    need(Y, [("dst", dmas["dst"])])
+    need(G, [("loc", dmas["loc"]), ("v", V["n"]), ("a", S["n"]), ("t", P["n"]), ("q", G["n"])])

@@ -15,33 +15,37 @@ SCRATCH = {
     "uq": _sb(128, X4), "us": _sb(128, "uint8"), "ubq": _sb(128, X4), "ubs": _sb(128, "uint8"),
     "sq": _sb(384, X4), "sp": _sb(384, "uint8"), "lq": _sb(512, X4), "lp": _sb(512, "uint8"),
     "fq": _sb(512, X4), "fp": _sb(512, "uint8"),
-    "zoff": _sb(8, "uint16"), "half": _sb(128, "bfloat16"), "tri": _sb(128, "bfloat16"), "ip": _sb(2, "int32"),
-    "r3": _sb(2, "int32"), "p15": _sb(2, "int32"), "p12": _sb(2, "int32"), "p96": _sb(2, "int32"),
-    "p16": _sb(2, "int32"), "p31": _sb(2, "int32"), "corr0": _sb(2, "float32"), "corr": _sb(2, "float32"),
-    "corw0": _sb(2, "float32"), "corw": _sb(2, "float32"), "quad": _sb(2, "float32"), "tok0": _sb(2, "float32"),
-    "tok": _sb(2, "float32"), "k4": _sb(8, "int32"), "plq": _sb(8, "uint16"), "lo": _sb(2, "float32"),
-    "hi": _sb(2, "float32"), "pcol": _sb(2, "float32"), "ibias": _sb(2, "float32"), "bl32": _sb(32, "int32"),
-    "bl": _sb(32, "uint16"),
-    "de": _sb(16, "int32"), "de2": _sb(16, "int32"), "da": _sb(16, "bfloat16"), "db": _sb(16, "bfloat16"),
-    "d0": _sb(512, "bfloat16"), "dg": _sb(32, "int32"), "dg2": _sb(32, "int32"), "dga": _sb(32, "bfloat16"),
-    "dgb": _sb(32, "bfloat16"), "d4": _sb(32, "bfloat16"), "zz": _sb(136, "bfloat16"),
-    "idv0": _sb(128, "bfloat16"), "idv": _sb(128, "bfloat16"),
-    "ss": _sb(512, "float32"), "vc": _sb(4, "float32"), "sg": _sb(512, "bfloat16"), "sgb": _sb(768, "bfloat16"),
-    "cb": _sb(2080, "bfloat16"), "es": _sb(768, "bfloat16"), "z1": _sb(544, "bfloat16"),
-    "sl": _sb(128, "float32"), "so": _sb(512, "float32"), "tr": _sb(512, "float32"), "v16": _sb(16, "float32"),
-    "rs": _sb(16, "float32"), "r1": _sb(16, "float32"), "rr": _sb(16, "float32"), "bx": _sb(512, "float32"),
-    "sb": _sb(512, "float32"), "v1": _sb(4, "float32"), "sg2": _sb(768, "bfloat16"), "c2": _sb(1600, "bfloat16"),
-    "z2": _sb(800, "bfloat16"), "li": _sb(32, "uint16"), "ia": _sb(16, "bfloat16"), "ib": _sb(16, "bfloat16"),
-    "inn": _sb(512, "bfloat16"), "iw": _sb(512, "bfloat16"), "q2": _sb(8, "uint16"), "gid": _sb(128, "float32"),
+    "zoff": _sb(8, "uint16"), "flip": _sb(520, "bfloat16"), "ip": _sb(2, "int32"), "pcol": _sb(2, "float32"),
+    "r3": _sb(2, "int32"), "p15": _sb(2, "int32"), "p112": _sb(2, "int32"),
+    "p16": _sb(2, "int32"), "p5": _sb(2, "int32"), "p7": _sb(2, "int32"), "p48": _sb(2, "int32"),
+    "corr": _sb(2, "float32"), "grp": _sb(2, "float32"), "qn": _sb(2, "float32"),
+    "bnd": _sb(2, "float32"), "k4": _sb(4, "int32"), "plq": _sb(4, "uint16"), "lo": _sb(2, "float32"),
+    "hi": _sb(2, "float32"), "ibias": _sb(2, "float32"), "bl32": _sb(32, "int32"), "bl": _sb(32, "uint16"),
+    "vl": _sb(2, "uint16"), "ql": _sb(2, "uint16"),
+    "de": _sb(64, "int32"), "de2": _sb(64, "int32"), "da": _sb(64, "bfloat16"), "db": _sb(64, "bfloat16"),
+    "d0": _sb(512, "bfloat16"), "idv0": _sb(64, "bfloat16"), "idv": _sb(64, "bfloat16"),
+    "ss": _sb(512, "float32"), "vc": _sb(4, "float32"), "sg": _sb(1024, "bfloat16"), "sgb": _sb(512, "bfloat16"),
+    "acc": _sb(4, "float32"), "eq": _sb(1040, "bfloat16"), "ow": _sb(1040, "bfloat16"),
+    "cb": _sb(1024, "bfloat16"), "z1": _sb(512, "bfloat16"),
+    "sl": _sb(64, "float32"), "so": _sb(512, "float32"), "tr": _sb(512, "float32"), "v16": _sb(12, "float32"),
+    "ia": _sb(16, "bfloat16"), "ib": _sb(16, "bfloat16"), "nb": _sb(16, "float32"),
+    "rs": _sb(16, "float32"), "r1": _sb(16, "float32"), "rr": _sb(16, "float32"), "bx": _sb(384, "float32"),
+    "sb": _sb(512, "float32"), "v1": _sb(16, "float32"), "sg2": _sb(1536, "bfloat16"), "c2": _sb(1536, "bfloat16"),
+    "z2": _sb(768, "bfloat16"), "rn": _sb(16, "float32"),
+    "inn": _sb(512, "bfloat16"), "iw": _sb(512, "bfloat16"), "q2": _sb(16, "uint16"), "gid": _sb(128, "float32"),
     "ysb": _sb(512, "float32"),
     "ps": ("psum", [128, 4096], "float32"),
 }
 for _k in ("1", "2"):
-    SCRATCH.update({"pt" + _k: _sb(32, "bfloat16"), "pg" + _k: _sb(32, "float16"), "pw" + _k: _sb(8, "uint16"),
-                    "wi" + _k: _sb(512, "bfloat16"), "wx" + _k: _sb(512, "float16"), "ge" + _k: _sb(32, "float16"),
-                    "gm" + _k: _sb(32, "float16"), "lw" + _k: _sb(32, "uint16")})
-SEMAPHORES = ["v", "a", "t", "q", "du", "dx0", "dx1", "dx2", "dx3", "dw", "dst",
-              "rem_s", "rem_c", "rem_p", "rem_i", "loc"]
+    SCRATCH.update({"pz" + _k: _sb(4, "uint16"), "wi" + _k: _sb(512, "bfloat16"), "wx" + _k: _sb(512, "float16"),
+                    "et" + _k: _sb(32, "float16"), "eh" + _k: _sb(32, "float16"), "eb" + _k: _sb(32, "float16"),
+                    "ge" + _k: _sb(32, "float32"), "gm" + _k: _sb(32, "float32"), "lw" + _k: _sb(32, "uint16")})
+SEMAPHORES = ["v", "a", "t", "q", "du", "dx0", "dx1", "dw", "dst", "rem_s", "rem_c", "rem_p", "rem_i", "loc"]
+
+WAIT = 215
+CYCLE = 0.83
+LOAD, FIRST, HOP = 1000, 1200, 1200
+OPT = {"twin": 1, "ways": "a"}
 
 
 def _routes(core, cores, topo):
@@ -64,6 +68,25 @@ def _routes(core, cores, topo):
     return out
 
 
+def _arrange(steps):
+    for s in reversed(steps):
+        s["chain"] += s["busy"] + s["late"]
+        for d in s["deps"]:
+            d["chain"] = max(d["chain"], s["chain"] + WAIT)
+        for d in s["after"]:
+            d["chain"] = max(d["chain"], s["chain"])
+    taken = {}
+    for s in sorted(steps, key=lambda s: -s["chain"]):
+        t = max([0] + [d["end"] + WAIT for d in s["deps"]] + [d["at"] + d["busy"] for d in s["after"]])
+        if s["q"]:
+            for a, b, kind in sorted(taken.setdefault(s["q"], [])):
+                if t + s["busy"] + WAIT * (s["kind"] == "across" and kind == "") <= a:
+                    break
+                t = max(t, b + WAIT * (kind == "across" and s["kind"] == ""))
+            taken[s["q"]].append((t, t + s["busy"], s["kind"]))
+        s["at"], s["end"] = t, t + s["busy"] + s["late"]
+
+
 def rank_program(g, core, T, topo):
     rank = T.rank_of(core)
     if rank is None:
@@ -72,40 +95,34 @@ def rank_program(g, core, T, topo):
     others = [d for d in range(N) if d != rank]
     routes = _routes(core, cores, topo)
     FEW = 4
-
-    def arrive(sem):
-        n = [len(_routes(c, cores, topo)[core]) for c in cores if c != core]
-        return (sem, sum(min(k, FEW) for k in n) if sem == "rem_s" else sum(n))
-
     U32, U8 = dt.uint32, dt.uint8
+    queues = {"v": g.vector, "a": g.scalar, "t": g.tensor, "q": g, "y": g.sync}
+    steps, counts = [], {}
 
-    V = {"q": g.vector, "sem": "v", "n": 0, "seen": {}}
-    S = {"q": g.scalar, "sem": "a", "n": 0, "seen": {}}
-    P = {"q": g.tensor, "sem": "t", "n": 0, "seen": {}}
-    G = {"q": g, "sem": "q", "n": 0, "seen": {}}
-    Y = {"q": g.sync, "sem": None, "n": 0, "seen": {}}
-    dmas = {}
+    def step(q, deps, busy, call, late=0, sem=None, after=(), kind=""):
+        s = {"q": q, "deps": list(deps), "after": list(after), "busy": busy, "late": late, "call": call, "sem": sem,
+             "chain": 0, "kind": kind}
+        steps.append(s)
+        return s
 
-    def need(E, deps):
-        for s, n in deps:
-            if E["seen"].get(s, 0) < n:
-                E["q"].wait_ge(T.sem[s], n)
-                E["seen"][s] = n
+    def V(deps, n, call, *a, after=(), kind=""):
+        return step("v", deps, CYCLE * max(n, 64), lambda: call(*a), after=after, kind=kind)
 
-    def op(E, deps, call, *a, **k):
-        need(E, deps)
-        call(*a, **k).then_inc(T.sem[E["sem"]], 1)
-        E["n"] += 1
-        return (E["sem"], E["n"])
+    def S(deps, n, *a, after=(), **k):
+        return step("a", deps, 65 + CYCLE * n, lambda: g.scalar.activation(*a, **k), after=after)
 
-    def dma(E, deps, out, in_, sem):
-        need(E, deps)
-        E["q"].dma_start(out, in_).then_inc(T.sem[sem], 16)
-        dmas[sem] = dmas.get(sem, 0) + 16
-        return (sem, dmas[sem])
+    def P(deps, n, *a):
+        return step("t", deps, CYCLE * (n + 16), lambda: g.tensor.matmul_mx(*a, True, True))
 
-    def send(deps, pieces, sem):
-        need(G, deps)
+    def iota(out, n, pattern, base, mult, small=True, after=()):
+        return step("q", [], 130 + 2 * CYCLE * n,
+                    lambda: g.iota(out, pattern, base, mult, allow_small_or_imprecise_dtypes=small), after=after)
+
+    def dma(q, deps, late, out, in_, sem, after=()):
+        counts[sem] = counts.get(sem, 0) + 16
+        return step(q, deps, 50, lambda: queues[q].dma_start(out, in_), late, (sem, counts[sem]), after)
+
+    def send(deps, pieces, sem, busy, late, after=()):
         tr = []
         for d, src, dst in pieces:
             rid, pid, _ = topo.addr(cores[d])
@@ -113,181 +130,35 @@ def rank_program(g, core, T, topo):
             tr.append(RemoteDMATransfer(dst_ids=[DstId(rid=rid, pnc=pid)],
                                         dma_engine_mask=sum(1 << e for e in engines),
                                         remote_sem=T.sem[sem], src=src, dst=dst))
-            dmas["loc"] = dmas.get("loc", 0) + len(engines)
-        g.remote_dma_fused(tr, local_sem=T.sem.loc)
+            counts["loc"] = counts.get("loc", 0) + len(engines)
+        call = step("q", deps, busy, lambda: g.remote_dma_fused(tr, local_sem=T.sem.loc), sem=("loc", None), after=after)
+        n = [len(_routes(c, cores, topo)[core]) for c in cores if c != core]
+        n = sum(min(k, FEW) for k in n) if sem == "rem_s" else sum(n)
+        return call, step(None, [call], 0, None, late, (sem, n))
 
-    vec, act, pe = g.vector, g.scalar.activation, g.tensor.matmul_mx
+    vec = g.vector
     cp, ts, tt, scan = vec.tensor_copy, vec.tensor_scalar, vec.tensor_tensor, vec.tensor_tensor_scan
+    PICK, PUT = 1.5, 3.0
 
     def r(c, w=128):
         return slice(w * c, w * c + w)
 
-    def iota(out, pattern, base, mult, small=True):
-        return op(G, [], g.iota, out, pattern, base, mult, allow_small_or_imprecise_dtypes=small)
+    def fill(out, n, c, after=()):
+        return V([], n, vec.memset, out, c, after=after, kind="plain")
 
-    dx = [None] * 4
-    dx[0] = dma(Y, [], T.xt[:, r(0, 512)], T.x[:, r(0, 512)], "dx0")
-    du = dma(S, [], T.ut[:, 0:8], T.u[:, 0:8], "du")
-    for c in (1, 2, 3):
-        dx[c] = dma(S if c & 1 else Y, [], T.xt[:, r(c, 512)], T.x[:, r(c, 512)], "dx%d" % c)
-    dw = dma(Y, [], T.wt[:], T.w[:], "dw")
+    def bits(out, src, dep, a, b=None):
+        if b is None:
+            return V([dep], 1, ts, out, src, a, None, A.bitwise_and, kind="plain")
+        return V([dep], 1, ts, out, src, a, b, A.bitwise_and, A.logical_shift_right, kind="plain")
 
-    k_ip = iota(T.ip[:], [[0, 2]], 0, 1, False)
-    k_de = iota(T.de[:], [[1, 16]], 2048, -1, False)
-    k_dg = iota(T.dg[:], [[4, 32]], 2051, -1, False)
-    k_k4 = iota(T.k4[:], [[4, 8]], 0, 0, False)
-    mh = op(V, [], vec.memset, T.half[:], 0.5)
-    m0 = op(V, [], vec.memset, T.ut[:, 8:512], 0.0)
-    mz = op(V, [], vec.memset, T.zoff[:], 0)
-    k_tri = op(G, [mh], g.affine_select, T.tri[:], T.half[:], [[-1, 128]], A.is_gt, -0.5, 0, 1)
-    k_i0 = iota(T.idv0[:], [[4, 8], [1, 4], [128, 4]], -256, 0)
-    for c in range(4):
-        iota(T.cb[:, 520 * c + 512:520 * c + 520], [[0, 8]], 0, 0)
-    k_zz = iota(T.zz[:], [[0, 136]], 0, 0)
-    mw1 = iota(T.wi1[:], [[0, 512]], -512, 0)
-    k_bl = iota(T.bl32[:], [[1, 16], [0, 2]], 0, 0, False)
-    for s in range(N):
-        for b in (192, 392):
-            iota(T.c2[:, 400 * s + b:400 * s + b + 8], [[0, 8]], 0, 0)
-    k_pc = iota(T.pcol[:], [[0, 2]], -256, 1)
-    mi = iota(T.inn[:], [[1, 4], [0, 128]], 0, 0)
-    a96 = op(V, [k_ip], ts, T.p96[:], T.ip[:], 96, None, A.bitwise_and)
-    a3 = op(V, [k_ip], ts, T.r3[:], T.ip[:], 3, None, A.bitwise_and)
-    a15 = op(V, [k_ip], ts, T.p15[:], T.ip[:], 15, None, A.bitwise_and)
-    a12 = op(V, [k_ip], ts, T.p12[:], T.ip[:], 12, None, A.bitwise_and)
-    k_qd = op(V, [a96], ts, T.quad[:], T.p96[:], 1, None, A.mult)
-    ade = op(V, [k_de], ts, T.de2[:], T.de[:], 15, None, A.bitwise_and)
-    adg = op(V, [k_dg], ts, T.dg2[:], T.dg[:], 12, None, A.bitwise_and)
-    k_c0 = op(V, [a15], ts, T.corr0[:], T.p15[:], 15, 1024, A.is_lt, A.mult)
-    k_w0 = op(V, [a12], ts, T.corw0[:], T.p12[:], 12, 1024, A.is_lt, A.mult)
-    for i in range(4):
-        ms = op(S, [mh], act, T.so[:, r(i)], T.half[:], F.Copy, 0.0, -1e29)
-    k_id = op(S, [k_i0, k_qd], act, T.idv[:], T.idv0[:], F.Identity, T.quad[:, 0:1])
+    def pick(deps, n, out, src):
+        return V(deps, 60 + PICK * n, cp, out, src)
 
-    qu = op(V, [m0, du], vec.quantize_mx, T.uq[:], T.us[:], T.ut[:])
-    ub = op(V, [qu, mz], cp, T.ubq[:, 0:128].bitcast(U32), T.uq[:, 0:128].bitcast(U32).indirect(T.zoff[:, 0:8]))
-    ubs = op(S, [qu, mz], act, T.ubs[:, 0:128], T.us[:, 0:128].indirect(T.zoff[:, 0:8]), F.Copy)
+    def quantize(deps, n, *a):
+        return step("v", deps, 12 + 0.88 * n, lambda: vec.quantize_mx(*a))
 
-    qx, pv, psc, vcol, sc, sgn = [None] * 4, [None] * 4, [None] * 4, [None] * 4, [None] * 4, [None] * 4
-    sgb = {}
-
-    def quant(c):
-        qx[c] = op(V, [dx[c]], vec.quantize_mx, T.xq[:, r(c)], T.xs[:, r(c)], T.xt[:, r(c, 512)])
-        b = 512 * (4 + c)
-        pv[c] = op(P, [qx[c], qu], pe, T.ps[:, b:b + 128], T.xq[:, r(c)], T.xs[:, r(c)], T.uq[:], T.us[:], True, True)
-        b = 512 * c
-        psc[c] = op(P, [ub, ubs], pe, T.ps[:, b:b + 128], T.ubq[:], T.ubs[:], T.xq[:, r(c)], T.xs[:, r(c)], True, True)
-
-    def cb(c, a, b):
-        return T.cb[:, 520 * c + a:520 * c + b]
-
-    def at_b(c, e):
-        return r(c * (c - 1) // 2 + e)
-
-    def work_a(c):
-        row = T.ps[:, 512 * c:512 * c + 128]
-        vcol[c] = op(V, [pv[c]], cp, T.vc[:, c:c + 1], T.ps[:, 512 * (4 + c):512 * (4 + c) + 1])
-        for e in range(c):
-            sgb[c, e] = op(S, [psc[c], vcol[e]], act, T.sgb[:, at_b(c, e)], row, F.Sign, T.vc[:, e:e + 1], -1.0)
-        sgn[c] = op(S, [psc[c], vcol[c]], act, T.sg[:, r(c)], row, F.Sign, T.vc[:, c:c + 1], -1.0)
-        sc[c] = op(S, [], act, T.ss[:, r(c)], row, F.Copy)
-        if c:
-            return op(V, [vcol[c], sc[c - 1]], ts, cb(c, 0, 128 * c), T.ss[:, 0:128 * c], T.vc[:, c:c + 1], None, A.is_ge)
-
-    def work_b(c, e):
-        return op(V, [sgb[c, e]], ts, cb(e, 128 * c, 128 * c + 128), T.sgb[:, at_b(c, e)], 0.0, None, A.is_lt)
-
-    def work_d(c):
-        return op(V, [sgn[c], k_tri], tt, cb(c, 128 * c, 128 * c + 128), T.sg[:, r(c)], T.tri[:], A.is_lt)
-
-    def early(c, dep):
-        return op(V, [dep], scan, T.es[:, r(c, 192)], cb(c, 0, 192), cb(c, 192, 384), -256.0, A.add, A.add)
-
-    def late(c, dep):
-        return op(V, dep + [k_zz], scan, T.z1[:, c:544:4], cb(c, 384, 520), T.zz[:, 0:136],
-                  T.es[:, 192 * c + 191:192 * c + 192], A.add, A.add)
-
-    quant(0)
-    quant(1)
-    k_ga = op(V, [adg], ts, T.dga[:], T.dg2[:], 0, -4096, A.is_equal, A.mult)
-    k_gb = op(V, [adg], ts, T.dgb[:], T.dg2[:], 4, 1024, A.is_equal, A.mult)
-    k_da = op(V, [ade], ts, T.da[:], T.de2[:], 0, -4096, A.is_equal, A.mult)
-    k_db = op(V, [ade], ts, T.db[:], T.de2[:], 1, 1024, A.is_equal, A.mult)
-    k_t0 = op(V, [k_qd], ts, T.tok0[:], T.r3[:], 128, T.quad[:, 0:1], A.mult, A.add)
-    work_a(0)
-    k_d4 = op(V, [k_ga, k_gb], tt, T.d4[:], T.dga[:], T.dgb[:], A.add)
-    k_d0 = op(V, [k_da, k_db], tt, T.d0[:, 0:16], T.da[:], T.db[:], A.add)
-    k_co = op(V, [k_c0], ts, T.corr[:], T.corr0[:], 256, None, A.subtract)
-    k_cw = op(V, [k_w0], ts, T.corw[:], T.corw0[:], 256, None, A.subtract)
-    k_tk = op(V, [k_t0], ts, T.tok[:], T.p12[:], 0.25, T.tok0[:, 0:1], A.mult, A.add)
-    work_d(0)
-    k_pl = op(V, [k_tk, k_k4], ts, T.plq[:], T.k4[:], T.tok[:, 0:1], None, A.add)
-    quant(2)
-    work_a(1)
-    work_b(1, 0)
-    work_d(1)
-    work_a(2)
-    quant(3)
-    b0 = work_b(2, 0)
-    b1 = work_b(2, 1)
-    b2 = work_d(2)
-    e0 = early(0, b0)
-    e1 = early(1, b1)
-    e2 = early(2, b2)
-    w3 = work_a(3)
-    b0 = work_b(3, 0)
-    b1 = work_b(3, 1)
-    b2 = work_b(3, 2)
-    e3 = early(3, w3)
-    b3 = work_d(3)
-    late(0, [b0, e0])
-    late(1, [b1, e1])
-    late(2, [b2, e2])
-    fin = late(3, [b3, e3])
-    sl = op(S, [k_pl, sc[3]], act, T.sl[:, 0:128], T.ss[:, 0:512].indirect(T.plq[:, 0:8]), F.Copy)
-    kd = k_d0
-    for n in (16, 32, 64, 128, 256):
-        kd = op(S, [kd], act, T.d0[:, n:2 * n], T.d0[:, 0:n], F.Copy)
-    for i in range(4):
-        mw2 = op(S, [mh], act, T.wi2[:, r(i)], T.half[:], F.Copy, 0.0, -1024.0)
-
-    def offsets(fin, z, k, fill=None):
-        x = op(V, [fin], vec.transpose, T["pt" + k][:], z)
-        if fill:
-            fill()
-        x = op(V, [x, k_d4], scan, T["pg" + k][:], T.d4[:], T["pt" + k][:], 0.0, A.add, A.max)
-        return op(V, [x, k_cw], ts, T["pw" + k][:, 0:8], T["pg" + k][:, 3:32:4], T.corw[:, 0:1], None, A.subtract)
-
-    def scatter(x, k, mw):
-        return op(V, [x, k_id, mw], cp, T["wi" + k][:, 0:512].indirect(T["pw" + k][:, 0:8]), T.idv[:, 0:128])
-
-    def diagonal(x, k):
-        return op(V, [x, kd], scan, T["wx" + k][:], T.d0[:], T["wi" + k][:], 0.0, A.add, A.max)
-
-    def quadrants(x, mid, out, w, src):
-        for a in range(4):
-            p, o = slice(32 * a, 32 * a + 32), slice(32 * (a ^ 1), 32 * (a ^ 1) + 32)
-            y = op(V, x, tt, mid[p, 0:w], src(p), src(o), A.max)
-        for a in range(2):
-            p, o = slice(64 * a, 64 * a + 64), slice(64 * (a ^ 1), 64 * (a ^ 1) + 64)
-            z = op(V, [y], tt, out[p, 0:w], mid[p, 0:w], mid[o, 0:w], A.max)
-        return z
-
-    def number_list(x, k):
-        wx = T["wx" + k]
-        x = quadrants([x], T["ge" + k], T["gm" + k], 32, lambda p: wx[p, 15:512:16])
-        return x, op(V, [x, k_co], ts, T["lw" + k][:, 0:32], T["gm" + k][:, 0:32], T.corr[:, 0:1], None, A.subtract)
-
-    pw = offsets(fin, T.z1[:, 512:544], "1")
-    so = op(V, [pw, sl, ms], cp, T.so[:, 0:512].indirect(T.pw1[:, 0:8]), T.sl[:, 0:128])
-    wi = scatter(pw, "1", mw1)
-    x = op(V, [so], vec.transpose, T.tr[:], T.so[:])
-    wx = diagonal(wi, "1")
-    v16 = op(V, [x], cp, T.v16[:], T.tr[:, 0:512:32])
-    send([v16], [(d, T.v16[:, 4 * d:4 * d + 4], T.rs[:, 4 * rank:4 * rank + 4]) for d in others], "rem_s")
-    rso = op(S, [v16], act, T.rs[:, 4 * rank:4 * rank + 4], T.v16[:, 4 * rank:4 * rank + 4], F.Copy)
-    gm, lw = number_list(wx, "1")
-    send([lw], [(d, T.lw1[:, 8 * d:8 * d + 8], T.li[:, 8 * rank:8 * rank + 8]) for d in others], "rem_i")
+    def bank(b, n=128, a=0):
+        return T.ps[:, 512 * b + a:512 * b + a + n]
 
     spans = []
     for i, d in enumerate(others):
@@ -295,98 +166,215 @@ def rank_program(g, core, T, topo):
             spans[-1][2] += 1
         else:
             spans.append([i, d, 1])
-    for i, d, n in spans:
-        of = T.lw1[:, 8 * d:8 * d + 8 * n]
-        at = slice(128 * i, 128 * i + 128 * n)
-        pq = op(V, [lw], cp, T.sq[:, at].bitcast(U32), T.xq[:, 0:512].bitcast(U32).indirect(of))
-        pp = op(S, [lw], act, T.sp[:, at], T.xs[:, 0:512].indirect(of), F.Copy)
-    send([pq], [(d, T.sq[:, r(i)].bitcast(U8), T.lq[:, r(rank)].bitcast(U8)) for i, d in enumerate(others)], "rem_c")
-    send([pp], [(d, T.sp[:, r(i)], T.lp[:, r(rank)]) for i, d in enumerate(others)], "rem_p")
+
+    du = dma("a", [], LOAD, T.ut[:, 0:8], T.u[:, 0:8], "du")
+    dx = [dma("y", [], LOAD + 600, T.xt[:, r(0, 1024)], T.x[:, r(0, 1024)], "dx0")]
+    dx.append(dma("a", [], LOAD + 1200, T.xt[:, r(1, 1024)], T.x[:, r(1, 1024)], "dx1", after=[du]))
+    dw = dma("y", [], LOAD + 2400, T.wt[:], T.w[:], "dw", after=dx)
+
+    k_de = iota(T.de[:], 64, [[0, 4], [1, 16]], 2048, -1, False)
+    k_ip = iota(T.ip[:], 2, [[0, 2]], 0, 1, False)
+    k_k4 = iota(T.k4[:], 4, [[128, 4]], 0, 1, False)
+    k_pc = iota(T.pcol[:], 2, [[0, 2]], -64, 1)
+    k_i0 = iota(T.idv0[:], 64, [[128, 4], [1, 16]], -256, 0)
+    k_bl = iota(T.bl32[:], 32, [[1, 16], [0, 2]], 0, 0, False)
+    m0 = fill(T.ut[:, 8:512], 252, 0.0)
+    mz = fill(T.zoff[:], 8, 0)
+    mw = {k: fill(T["wi" + k][:], 256, -512.0) for k in "12"}
+    m1 = fill(T.flip[:], 260, 1.0)
+    k_fl = [V([m1], 2, vec.memset, T.flip[:, 256:520:260], 0.5)]
+    for at in (0, 260 + 128):
+        k_fl.append(step("q", [m1], 170 + 2 * CYCLE * 128, lambda at=at: g.affine_select(
+            T.flip[:, at:at + 128], T.flip[:, at:at + 128], [[-1, 128]], A.not_equal, -1.0, 0, 1)))
+    k_eq = fill(T.eq[:, 256:1040:260], 4, 0.0)
+    ade = bits(T.de2[:], T.de[:], k_de, 15)
+    k_da = V([ade], 64, ts, T.da[:], T.de2[:], 0, -4096, A.is_equal, A.mult)
+    k_db = V([ade], 64, ts, T.db[:], T.de2[:], 1, 1024, A.is_equal, A.mult)
+    kd = V([k_da, k_db], 128, tt, T.d0[:, 0:64], T.da[:], T.db[:], A.add)
+    for n in (64, 128, 256):
+        kd = S([kd], n, T.d0[:, n:2 * n], T.d0[:, 0:n], F.Copy)
+    k_co = V([bits(T.p15[:], T.ip[:], k_ip, 15)], 1, ts, T.corr[:, 0:1], T.p15[:, 0:1], 15, 1024, A.is_lt, A.mult)
+    k_cq = V([k_co], 1, ts, T.corr[:, 1:2], T.corr[:, 0:1], 256, None, A.subtract)
+    k_gr = V([bits(T.p112[:], T.ip[:], k_ip, 112)], 1, cp, T.grp[:], T.p112[:])
+    k_id = S([k_i0, k_gr], 64, T.idv[:], T.idv0[:], F.Identity, T.grp[:, 0:1])
+    a16 = bits(T.p16[:], T.ip[:], k_ip, 16)
+    k_lo = V([a16], 1, ts, T.lo[:], T.p16[:], 16, None, A.is_lt)
+    k_hi = V([a16], 1, ts, T.hi[:], T.p16[:], 16, None, A.is_equal)
+    k_pl = V([k_k4], 4, cp, T.plq[:], T.k4[:])
+    k_bl = V([k_bl], 32, cp, T.bl[:], T.bl32[:])
+    k_qn = V([bits(T.p5[:], T.ip[:], k_ip, 96, 5)], 1, cp, T.qn[:], T.p5[:])
+    k_vl = V([bits(T.r3[:], T.ip[:], k_ip, 3), k_qn], 1, ts, T.vl[:], T.r3[:], 4, T.qn[:, 0:1], A.mult, A.add)
+    k_bd = V([bits(T.p48[:], T.ip[:], k_ip, 48, 1)], 1, cp, T.bnd[:], T.p48[:])
+    k_ql = V([bits(T.p7[:], T.ip[:], k_ip, 7), k_bd], 1, ts, T.ql[:], T.p7[:], T.bnd[:, 0:1], None, A.add)
+    k_ib = [fill(T.ibias[0:64, :], 2, 0.0), fill(T.ibias[64:128, :], 2, 256.0)]
+    ms = S([mw["1"]], 512, T.so[:], T.wi1[:], F.Copy, 0.0, 1e26)
+    mn = S([mw["1"]], 512, T.inn[64:128, :], T.wi1[64:128, :], F.Copy)
+
+    qu = quantize([m0, du], 128, T.uq[:], T.us[:], T.ut[:])
+    ub = pick([qu, mz], 128, T.ubq[:, 0:128].bitcast(U32), T.uq[:, 0:128].bitcast(U32).indirect(T.zoff[:, 0:8]))
+    ubs = S([qu, mz], PICK * 128, T.ubs[:, 0:128], T.us[:, 0:128].indirect(T.zoff[:, 0:8]), F.Copy)
+    qw = [quantize([dw], 128, T.wq[:, r(k)], T.ws[:, r(k)], T.wt[:, r(k, 512)]) for k in range(4)]
+
+    pv, vcol, rows, kept, own = [], [], [], [], []
+    for h in range(2):
+        qx = quantize([dx[h]], 256, T.xq[:, r(h, 256)], T.xs[:, r(h, 256)], T.xt[:, r(h, 1024)])
+        for c in (2 * h, 2 * h + 1):
+            pv.append(P([qx, qu], 128, bank(4 + c), T.xq[:, r(c)], T.xs[:, r(c)], T.uq[:], T.us[:]))
+        rows.append(P([qx, ub, ubs], 256, bank(h, 256), T.ubq[:], T.ubs[:], T.xq[:, r(h, 256)], T.xs[:, r(h, 256)]))
+        vcol.append(V(pv[-2:], 2, cp, T.vc[:, r(h, 2)], T.ps[:, 512 * (4 + 2 * h):512 * (6 + 2 * h):512]))
+        kept.append(S([rows[h]], 256, T.ss[:, r(h, 256)], bank(h, 256), F.Copy))
+        for c in (2 * h, 2 * h + 1):
+            x = S([rows[h], vcol[h]], 280, T.sg[:, r(c, 256)], bank(h, 256), F.Sign, T.vc[:, c:c + 1], -1.0,
+                  accum_out=T.acc[:, c:c + 1])
+            x = V([x], 128, ts, T.eq[:, 260 * c:260 * c + 256], T.sg[:, r(c, 256)], 0.0, None, A.is_equal)
+            m = 260 * (c & 1)
+            own.append(V([x, k_eq] + k_fl, 129, scan, T.ow[:, 260 * c:260 * c + 257], T.flip[:, m:m + 257],
+                         T.eq[:, 260 * c:260 * c + 257], T.acc[:, c:c + 1], A.mult, A.subtract))
+    twin = P([rows[1]], 256, bank(2, 256), T.ubq[:], T.ubs[:], T.xq[:, r(1, 256)], T.xs[:, r(1, 256)])
+    pz = []
+    for c in range(4):
+        out = T.cb[:, r(c, 256)]
+        if c >= 2:
+            x = V([pv[c], kept[0]], 256, ts, out, T.ss[:, 0:256], bank(4 + c, 1), 0.5, A.is_ge, A.subtract)
+        elif c < OPT["twin"]:
+            x = V([twin, vcol[0]], 256, ts, out, bank(2, 256), T.vc[:, c:c + 1], 0.5, A.is_gt, A.subtract)
+        else:
+            x = S([rows[1], vcol[0]], 256, T.sgb[:, r(c, 256)], bank(1, 256), F.Sign, T.vc[:, c:c + 1], -1.0)
+            x = V([x], 128, ts, out, T.sgb[:, r(c, 256)], 0.0, 0.5, A.is_lt, A.subtract)
+        x = V([x], 64, scan, T.z1[:, r(c)], T.cb[:, 256 * c:256 * c + 128], T.cb[:, 256 * c + 128:256 * c + 256],
+              256.0 - 128, A.add, A.add)
+        pz.append(V([x, own[c]], 1, ts, T.pz1[:, c:c + 1], T.z1[:, 128 * c + 127:128 * c + 128],
+                    T.ow[:, 260 * c + 256:260 * c + 257], 128, A.add, A.add))
+    sl = S([k_pl] + kept, PICK * 64, T.sl[:], T.ss[:, 0:512].indirect(T.plq[:, 0:4]), F.Copy)
+
+    def quadrants(deps, mid, out, w, src, many):
+        y = V(deps, 2 * w, tt, mid[0:64, 0:w], src[0:64, 0:w], src[64:128, 0:w], A.max, kind="across")
+        return [V([y], 2 * w, tt, out[32 * a:32 * a + 32, 0:w], mid[0:32, 0:w], mid[32:64, 0:w], A.max, kind="across")
+                for a in range(many)]
+
+    def make_list(deps, k, many):
+        wi, wx, et, eh, eb = (T[n + k] for n in ("wi", "wx", "et", "eh", "eb"))
+        x = V(deps + [k_id, mw[k]], 60 + PUT * 64, cp, wi[:, 0:512].indirect(T["pz" + k][:, 0:4]), T.idv[:])
+        x = V([x, kd], 256, scan, wx[:], T.d0[:], wi[:], 0.0, A.add, A.max)
+        x = V([x], 16, vec.transpose, et[:], wx[:, 15:512:16])
+        x = [V([x], 32, tt, eh[:, r(h, 16)], et[:, 0:16], et[:, 16:32], A.max) for h in range(2)]
+        x = V(x, 16, vec.transpose, eb[:], eh[:])
+        gm = quadrants([x], T["ge" + k], T["gm" + k], 32, eb, many)
+        p = slice(0, 32 * many)
+        return gm, [V(gm + [k_co], 32, ts, T["lw" + k][a:a + 32 * many, :], T["gm" + k][p, :], T.corr[p, 0:1], 256,
+                      A.subtract, A.add) for a in range(0, 128, 32 * many)]
+
+    so = V(pz + [sl, ms], 60 + PUT * 64, cp, T.so[:, 0:512].indirect(T.pz1[:, 0:4]), T.sl[:])
+    tr = [V([so], 128 * n, vec.transpose, T.tr[:, 128 * i:128 * (i + n)], T.so[:, 128 * d:128 * (d + n)])
+          for i, d, n in spans]
+    v16 = V(tr, 24, tt, T.v16[:], T.tr[:, 0:384:32], T.tr[:, 16:384:32], A.max)
+    out_s, in_s = send([v16], [(d, T.v16[:, r(i, 4)], T.rs[:, r(rank, 4)]) for i, d in enumerate(others)], "rem_s",
+                       FIRST, HOP)
+    tro = V([so], 128, vec.transpose, T.tr[:, 384:512], T.so[:, r(rank)])
+    rso = V([tro], 8, tt, T.rs[:, r(rank, 4)], T.tr[:, 384:512:32], T.tr[:, 400:512:32], A.max)
+    _, lw = make_list(pz + [ms, mn], "1", 2)
+
+    pq, pp = [], []
+    for i, d in enumerate(others):
+        pq.append(pick(lw, 128, T.sq[:, r(i)].bitcast(U32), T.xq[:, 0:512].bitcast(U32).indirect(T.lw1[:, r(d, 8)])))
+        pp.append(S(lw, PICK * 128, T.sp[:, r(i)], T.xs[:, 0:512].indirect(T.lw1[:, r(d, 8)]), F.Copy))
+    out_c, in_c = send(pq, [(d, T.sq[:, r(i)].bitcast(U8), T.lq[:, r(rank)].bitcast(U8)) for i, d in enumerate(others)],
+                       "rem_c", 200, 2 * HOP, after=[out_s])
+    out_p, in_p = send(pp, [(d, T.sp[:, r(i)], T.lp[:, r(rank)]) for i, d in enumerate(others)], "rem_p", 200, 2 * HOP,
+                       after=[out_s])
+    ia = V(lw + [k_lo], 8, ts, T.ia[:], T.lw1[:, 0:32:2], 256, T.lo[:, 0:1], A.subtract, A.mult)
+    ib = V(lw + [k_hi], 8, ts, T.ib[:], T.lw1[:, 1:32:2], 256, T.hi[:, 0:1], A.subtract, A.mult)
+    nb = V([ia, ib], 32, tt, T.nb[:], T.ia[:], T.ib[:], A.add)
+    out_i, in_i = send([nb], [(d, T.nb[:, r(d, 4)], T.rn[:, r(rank, 4)]) for d in others], "rem_i", 200, 2 * HOP,
+                       after=[out_s])
+    mi = iota(T.iw[0:64, :], 512, [[1, 4], [0, 128]], 0, 0, after=[out_c, out_p, out_i])
 
     of = T.lw1[:, 8 * rank:8 * rank + 8]
-    sbo = op(V, [lw], cp, T.sb[:, r(rank)], T.ss[:, 0:512].indirect(of))
-    k_bl = op(V, [k_bl], cp, T.bl[:], T.bl32[:])
-    oq = op(V, [lw], cp, T.lq[:, r(rank)].bitcast(U32), T.xq[:, 0:512].bitcast(U32).indirect(of))
-    ow = op(S, [lw], act, T.lp[:, r(rank)], T.xs[:, 0:512].indirect(of), F.Copy)
-    lio = op(V, [lw], cp, T.li[:, 8 * rank:8 * rank + 8], of)
-    a16 = op(V, [k_ip], ts, T.p16[:], T.ip[:], 16, None, A.bitwise_and)
-    a31 = op(V, [k_ip], ts, T.p31[:], T.ip[:], 31, None, A.bitwise_and)
-    k_lo = op(V, [a16], ts, T.lo[:], T.p16[:], 16, None, A.is_lt)
-    k_hi = op(V, [a16], ts, T.hi[:], T.p16[:], 16, None, A.is_equal)
-    k_ib = op(V, [a31], ts, T.ibias[:], T.p31[:], 1, 256, A.is_equal, A.mult)
-    qw = op(V, [dw], vec.quantize_mx, T.wq[:], T.ws[:], T.wt[:])
+    have = {rank: S(lw + kept, PICK * 128, T.sb[:, r(rank)], T.ss[:, 0:512].indirect(of), F.Copy)}
+    oq = pick(lw, 128, T.lq[:, r(rank)].bitcast(U32), T.xq[:, 0:512].bitcast(U32).indirect(of))
+    ow = S(lw, PICK * 128, T.lp[:, r(rank)], T.xs[:, 0:512].indirect(of), F.Copy)
+    nbo = S([nb], 4, T.rn[:, r(rank, 4)], T.nb[:, r(rank, 4)], F.Copy)
 
-    rr = quadrants([arrive("rem_s"), rso], T.r1, T.rr, 16, lambda p: T.rs[p, 0:16])
-    sx = others[2]
-    bx = {sx: op(S, [rr, k_bl], act, T.bx[:, r(sx)], T.rr[:, 0:16].indirect(T.bl[:, 8 * sx:8 * sx + 8]), F.Copy)}
-    for a in range(4):
-        v1 = op(S, [rr], act, T.v1[32 * a:32 * a + 32, 0:4], T.rr[32 * a:32 * a + 32, a:16:4], F.Copy)
-    for d in others[:2]:
-        bx[d] = op(V, [rr, k_bl], cp, T.bx[:, r(d)], T.rr[:, 0:16].indirect(T.bl[:, 8 * d:8 * d + 8]))
-    for d in others:
-        tb = op(V, [bx[d]], vec.transpose, T.sb[:, r(d)], T.bx[:, r(d)])
+    rr = quadrants([in_s, rso], T.r1, T.rr, 16, T.rs, 4)
+    v1 = pick(rr + [k_vl], 16, T.v1[:], T.rr[:, 0:16].indirect(T.vl[:, 0:1]))
+    for i, d in enumerate(others):
+        src = T.rr[:, 0:16].indirect(T.bl[:, r(d, 8)])
+        x = S(rr + [k_bl], PICK * 128, T.bx[:, r(i)], src, F.Copy) if i else pick(rr + [k_bl], 128, T.bx[:, r(i)], src)
+        have[d] = V([x], 128, vec.transpose, T.sb[:, r(d)], T.bx[:, r(i)])
 
-    def seg(s):
-        return [(0, 128 * s, 0, True)] * (s > 0) + [(128 * s + 128, 512, 128 * s, False)] * (s < 3)
+    def ways(s):
+        rest = [d for d in range(N) if d != s]
+        parts = []
+        for d in rest:
+            by_s = OPT["by_s"](rank, s, d) if "by_s" in OPT else s == 3 or d == rank
+            if parts and parts[-1][0] + parts[-1][1] == d and parts[-1][2] == by_s and rank not in (d, d - 1):
+                parts[-1][1] += 1
+            else:
+                parts.append([d, 1, by_s])
+        return parts
 
-    sg2 = {}
-    for s in (2, 3):
-        for lo, hi, at, ge in seg(s):
-            o = 384 * (s - 2) + at
-            sg2[s] = op(S, [v1, tb, sbo], act, T.sg2[:, o:o + hi - lo], T.sb[:, lo:hi], F.Sign, T.v1[:, s:s + 1], -1.0)
-    done = []
+    fin = []
     for s in range(N):
-        for lo, hi, at, ge in seg(s):
-            end = at + hi - lo
-            for b, e in ([(at, 192), (192, end)] if at < 192 < end else [(at, end)]):
-                w = 400 * s + b + 8 * (b >= 192)
-                out = T.c2[:, w:w + e - b]
-                if s < 2:
-                    x = op(V, [v1, tb, sbo], ts, out, T.sb[:, lo + b - at:lo + e - at], T.v1[:, s:s + 1], None,
-                           A.is_ge if ge else A.is_gt)
-                else:
-                    o = 384 * (s - 2)
-                    x = op(V, [sg2[s]], ts, out, T.sg2[:, o + b:o + e], 0.0, None, A.is_le if ge else A.is_lt)
-        done.append(x)
-    for s in range(N):
-        fin2 = op(V, [done[s], k_pc], scan, T.z2[:, s:800:4], T.c2[:, 400 * s:400 * s + 200],
-                  T.c2[:, 400 * s + 200:400 * s + 400], T.pcol[:, 0:1], A.add, A.add)
+        done = []
+        for d, n, by_s in ways(s):
+            at = slice(384 * s + 128 * (d - (d > s)), 384 * s + 128 * (d - (d > s) + n))
+            deps, src = [v1] + [have[e] for e in range(d, d + n)], T.sb[:, 128 * d:128 * (d + n)]
+            if by_s:
+                x = S(deps, 128 * n, T.sg2[:, at], src, F.Sign, T.v1[:, s:s + 1], -1.0)
+                x = V([x], 64 * n, ts, T.c2[:, at], T.sg2[:, at], 0.0, 0.5, A.is_le if d < s else A.is_lt, A.subtract)
+            else:
+                x = V(deps, 128 * n, ts, T.c2[:, at], src, T.v1[:, s:s + 1], 0.5, A.is_ge if d < s else A.is_gt,
+                      A.subtract)
+            done.append(x)
+        fin.append(V(done + [k_pc], 96, scan, T.z2[:, r(s, 192)], T.c2[:, 384 * s:384 * s + 192],
+                     T.c2[:, 384 * s + 192:384 * s + 384], T.pcol[:, 0:1], A.add, A.add))
+    pz2 = V(fin, 4, ts, T.pz2[:], T.z2[:, 191:768:192], 256, None, A.add)
+    gm, lm = make_list([pz2], "2", 4)
 
-    ids = []
+    ic = [S([in_i, nbo, mn], 16, T.inn[64:128, h:512:32], T.rn[64:128, :], F.Copy) for h in (0, 16)]
+    iw = V(ic, 256, vec.transpose, T.iw[64:128, :], T.inn[64:128, :])
+    ql = V(gm + [k_ql, k_cq], 60 + PICK * 16, ts, T.q2[:], T.gm2[:, 0:32].indirect(T.ql[:, 0:1]), T.corr[:, 1:2], None,
+           A.subtract)
+    ig = S([ql, iw, mi] + k_ib, PICK * 128, T.gid[:], T.iw[:, 0:512].indirect(T.q2[:, 0:8]), F.Identity,
+           T.ibias[:, 0:1])
+    dma("a", [ig], LOAD, T.ids[:, :], T.gid[0:128:16, :], "dst")
 
-    def halves():
-        ids.append(op(V, [lio, k_lo, arrive("rem_i")], ts, T.ia[:], T.li[:, 0:32:2], 256, T.lo[:, 0:1], A.subtract, A.mult))
-        ids.append(op(V, [k_hi], ts, T.ib[:], T.li[:, 1:32:2], 256, T.hi[:, 0:1], A.subtract, A.mult))
+    for k, n in ((0, 2), (2, 1), (3, 1)):
+        of, at = T.lw2[:, 8 * k:8 * (k + n)], slice(128 * k, 128 * (k + n))
+        a = pick(lm + [oq, in_c], 128 * n, T.fq[:, at].bitcast(U32), T.lq[:, 0:512].bitcast(U32).indirect(of))
+        b = S(lm + [ow, in_p], PICK * 128 * n, T.fp[:, at], T.lp[:, 0:512].indirect(of), F.Copy)
+        for j in range(k, k + n):
+            x = P([a, b, qw[j]], 128, bank(j), T.wq[:, r(j)], T.ws[:, r(j)], T.fq[:, r(j)], T.fp[:, r(j)])
+            x = V([x], 128, cp, T.ysb[:, r(j)], bank(j))
+            dma("y", [x], LOAD + 200, T.y[:, r(j)], T.ysb[:, r(j)], "dst")
 
-    x = offsets(fin2, T.z2[:, 768:800], "2", halves)
-    ic = op(V, ids + [mi], tt, T.inn[:, 1:512:32], T.ia[:], T.ib[:], A.add)
-    x = scatter(x, "2", mw2)
-    x = diagonal(x, "2")
-    iw = op(V, [ic], vec.transpose, T.iw[:], T.inn[:])
-    gm, lm = number_list(x, "2")
+    _arrange(steps)
+    order = {q: sorted((s for s in steps if s["q"] == q), key=lambda s: s["at"]) for q in queues}
+    for q in queues:
+        for s in order[q]:
+            if s["sem"] is None:
+                counts[q] = counts.get(q, 0) + 1
+                s["sem"] = (q, counts[q])
+    for q, E in queues.items():
+        seen = {}
 
-    def quad_list(a):
-        p = slice(32 * a, 32 * a + 32)
-        return op(V, [gm], ts, T.q2[p, 0:8], T.gm2[p, 8 * a:8 * a + 8], T.corr[p, 0:1], None, A.subtract)
+        def need(tokens):
+            for sem, n in tokens:
+                if seen.get(sem, 0) < n:
+                    E.wait_ge(T.sem[sem], n)
+                    seen[sem] = n
 
-    quad_list(0)
-    quad_list(1)
-    ym = [None] * 4
-    for k in range(4):
-        of = T.lw2[:, 8 * k:8 * k + 8]
-        a = op(V, [lm, oq, arrive("rem_c")], cp, T.fq[:, r(k)].bitcast(U32), T.lq[:, 0:512].bitcast(U32).indirect(of))
-        b = op(S, [lm, ow, arrive("rem_p")], act, T.fp[:, r(k)], T.lp[:, 0:512].indirect(of), F.Copy)
-        ym[k] = op(P, [a, b, qw], pe, T.ps[:, 512 * k:512 * k + 128], T.wq[:, r(k)], T.ws[:, r(k)], T.fq[:, r(k)], T.fp[:, r(k)], True, True)
-    quad_list(2)
-    ql = quad_list(3)
-    for k in range(3):
-        yc = op(S, [ym[k]], act, T.ysb[:, r(k)], T.ps[:, 512 * k:512 * k + 128], F.Copy)
-        dma(Y, [yc], T.y[:, r(k)], T.ysb[:, r(k)], "dst")
-    ig = op(V, [ql, iw, k_ib], ts, T.gid[:, 0:128], T.iw[:, 0:512].indirect(T.q2[:, 0:8]), T.ibias[:, 0:1], None, A.add)
-    for a in range(4):
-        dma(Y, [ig], T.ids[:, r(a)], T.gid[32 * a:32 * a + 2, 0:128], "dst")
-    yc = op(V, [ym[3]], cp, T.ysb[:, r(3)], T.ps[:, 512 * 3:512 * 3 + 128])
-    dma(S, [yc], T.y[:, r(3)], T.ysb[:, r(3)], "dst")
-
-    need(Y, [("dst", dmas["dst"])])
-    need(G, [("loc", dmas["loc"]), ("v", V["n"]), ("a", S["n"]), ("t", P["n"]), ("q", G["n"])])
+        across = []
+        for s in order[q]:
+            if s["kind"] == "across":
+                across = [s["sem"]]
+            elif s["kind"] == "":
+                need(across)
+            need(sorted((d["sem"] for d in s["deps"]), key=lambda t: (t[0], -t[1])))
+            done = s["call"]()
+            if s["sem"][1] is not None:
+                done.then_inc(T.sem[s["sem"][0]], 1 if s["sem"][0] == q else 16)
+        if q == "y":
+            need([("dst", counts["dst"])])
+        if q == "q":
+            need([(sem, counts[sem]) for sem in ("loc", "v", "a", "t", "q")])

@@ -15,23 +15,19 @@ SCRATCH = {
     "uq": _sb(128, X4), "us": _sb(128, "uint8"), "ubq": _sb(128, X4), "ubs": _sb(128, "uint8"),
     "sq": _sb(384, X4), "sp": _sb(384, "uint8"), "lq": _sb(512, X4), "lp": _sb(512, "uint8"),
     "fq": _sb(512, X4), "fp": _sb(512, "uint8"),
-    "zoff": _sb(8, "uint16"), "flip": _sb(520, "bfloat16"), "ip": _sb(2, "int32"), "pcol": _sb(2, "float32"),
-    "r3": _sb(2, "int32"), "p15": _sb(2, "int32"), "p112": _sb(2, "int32"),
-    "p16": _sb(2, "int32"), "p5": _sb(2, "int32"), "p7": _sb(2, "int32"), "p48": _sb(2, "int32"),
-    "corr": _sb(2, "float32"), "grp": _sb(2, "float32"), "qn": _sb(2, "float32"),
-    "bnd": _sb(2, "float32"), "k4": _sb(4, "int32"), "plq": _sb(4, "uint16"), "lo": _sb(2, "float32"),
-    "hi": _sb(2, "float32"), "ibias": _sb(2, "float32"), "bl32": _sb(32, "int32"), "bl": _sb(32, "uint16"),
-    "vl": _sb(2, "uint16"), "ql": _sb(2, "uint16"),
-    "de": _sb(64, "int32"), "de2": _sb(64, "int32"), "da": _sb(64, "bfloat16"), "db": _sb(64, "bfloat16"),
-    "d0": _sb(512, "bfloat16"), "idv0": _sb(64, "bfloat16"), "idv": _sb(64, "bfloat16"),
-    "ss": _sb(512, "float32"), "vc": _sb(4, "float32"), "sg": _sb(1024, "bfloat16"), "sgb": _sb(512, "bfloat16"),
-    "acc": _sb(4, "float32"), "eq": _sb(1040, "bfloat16"), "ow": _sb(1040, "bfloat16"),
-    "cb": _sb(1024, "bfloat16"), "z1": _sb(512, "bfloat16"),
-    "sl": _sb(64, "float32"), "so": _sb(512, "float32"), "tr": _sb(512, "float32"), "v16": _sb(12, "float32"),
-    "ia": _sb(16, "bfloat16"), "ib": _sb(16, "bfloat16"), "nb": _sb(16, "float32"),
-    "rs": _sb(16, "float32"), "r1": _sb(16, "float32"), "rr": _sb(16, "float32"), "bx": _sb(384, "float32"),
+    "zoff": _sb(8, "uint16"), "flip": _sb(384, "bfloat16"), "reset": _sb(128, "bfloat16"),
+    "de": _sb(66, "int32"), "de2": _sb(72, "int32"),
+    "da": _sb(64, "bfloat16"), "db": _sb(64, "bfloat16"), "d0": _sb(512, "bfloat16"),
+    "col": _sb(16, "float32"), "lf": _sb(36, "int32"), "lu": _sb(42, "uint16"),
+    "idv0": _sb(64, "bfloat16"), "idv": _sb(64, "bfloat16"),
+    "ss": _sb(512, "float32"), "vc": _sb(4, "float32"), "sg": _sb(1024, "bfloat16"), "sgb": _sb(2048, "bfloat16"),
+    "acc": _sb(4, "float32"), "eq": _sb(1024, "bfloat16"), "ow": _sb(1024, "bfloat16"),
+    "cb": _sb(2048, "bfloat16"), "z1": _sb(1024, "float16"),
+    "sl": _sb(64, "float32"), "so": _sb(512, "float32"), "tr": _sb(512, "float32"), "v16": _sb(16, "float32"),
+    "nb": _sb(16, "float32"),
+    "rs": _sb(16, "float32"), "r1": _sb(16, "float32"), "rr": _sb(64, "float32"), "bx": _sb(384, "float32"),
     "sb": _sb(512, "float32"), "v1": _sb(16, "float32"), "sg2": _sb(1536, "bfloat16"), "c2": _sb(1536, "bfloat16"),
-    "z2": _sb(768, "bfloat16"), "rn": _sb(16, "float32"),
+    "acc2": _sb(4, "float32"), "z2": _sb(768, "bfloat16"), "rn": _sb(16, "float32"),
     "inn": _sb(512, "bfloat16"), "iw": _sb(512, "bfloat16"), "q2": _sb(16, "uint16"), "gid": _sb(128, "float32"),
     "ysb": _sb(512, "float32"),
     "ps": ("psum", [128, 4096], "float32"),
@@ -39,13 +35,20 @@ SCRATCH = {
 for _k in ("1", "2"):
     SCRATCH.update({"pz" + _k: _sb(4, "uint16"), "wi" + _k: _sb(512, "bfloat16"), "wx" + _k: _sb(512, "float16"),
                     "et" + _k: _sb(32, "float16"), "eh" + _k: _sb(32, "float16"), "eb" + _k: _sb(32, "float16"),
-                    "ge" + _k: _sb(32, "float32"), "gm" + _k: _sb(32, "float32"), "lw" + _k: _sb(32, "uint16")})
-SEMAPHORES = ["v", "a", "t", "q", "du", "dx0", "dx1", "dw", "dst", "rem_s", "rem_c", "rem_p", "rem_i", "loc"]
+                    "ge" + _k: _sb(32, "float32"), "gm" + _k: _sb(48, "float32"), "lw" + _k: _sb(32, "uint16")})
+SEMAPHORES = ["v", "a", "t", "q", "du", "dx0", "dx1", "dx2", "dx3", "dw", "dst",
+              "rem_s", "rem_c", "rem_p", "rem_i", "loc"]
 
 WAIT = 215
-CYCLE = 0.83
-LOAD, FIRST, HOP = 1000, 1200, 1200
-OPT = {"twin": 1, "ways": "a"}
+CYCLE, CALL, ACT, SLOW, GSLOW = 0.83, 0, 65, 1.0, 1.0
+SLACK = 0
+LOAD, RATE, FIRST, HOP = 1000, 500, 1100, 1300
+OPT = {"loads": ((0, 1), (1, 2), (2, 3), (3, 4)), "twin": (3,), "many": (2, 2),
+       "sort": (("o", "k", "k", "s"), ("K", "o", "s", "s"), ("K", "K", "o", "t"), ("K", "K", "K", "o")),
+       "ways": "cvvv", "fine": 1, "ycopy": "vvvv",
+       "gather": "vaa", "v1": "v", "bands": ((0, 1), (1, 1), (2, 1), (3, 1)), "st": "yyyy",
+       "order": ("relu ic icb", "nb pp0", "out_i out_c", "put2 iw diag2"),
+       "picks": 0}
 
 
 def _routes(core, cores, topo):
@@ -69,18 +72,26 @@ def _routes(core, cores, topo):
 
 
 def _arrange(steps):
-    for s in reversed(steps):
-        s["chain"] += s["busy"] + s["late"]
+    later = [[] for s in steps]
+    for i, s in enumerate(steps):
+        s["n"] = i
+    for s in steps:
         for d in s["deps"]:
-            d["chain"] = max(d["chain"], s["chain"] + WAIT)
+            later[d["n"]].append((s, WAIT + d["late"]))
         for d in s["after"]:
-            d["chain"] = max(d["chain"], s["chain"])
+            later[d["n"]].append((s, 0))
+
+    def chain(s):
+        if not s["chain"]:
+            s["chain"] = s["busy"] + 1 + max([s["late"]] + [w + chain(n) for n, w in later[s["n"]]])
+        return s["chain"]
+
     taken = {}
-    for s in sorted(steps, key=lambda s: -s["chain"]):
+    for s in sorted(steps, key=lambda s: -chain(s)):
         t = max([0] + [d["end"] + WAIT for d in s["deps"]] + [d["at"] + d["busy"] for d in s["after"]])
         if s["q"]:
             for a, b, kind in sorted(taken.setdefault(s["q"], [])):
-                if t + s["busy"] + WAIT * (s["kind"] == "across" and kind == "") <= a:
+                if t < a and t + s["busy"] - SLACK + WAIT * (s["kind"] == "across" and kind == "") <= a:
                     break
                 t = max(t, b + WAIT * (kind == "across" and s["kind"] == ""))
             taken[s["q"]].append((t, t + s["busy"], s["kind"]))
@@ -97,7 +108,7 @@ def rank_program(g, core, T, topo):
     FEW = 4
     U32, U8 = dt.uint32, dt.uint8
     queues = {"v": g.vector, "a": g.scalar, "t": g.tensor, "q": g, "y": g.sync}
-    steps, counts = [], {}
+    steps, counts, named = [], {}, {}
 
     def step(q, deps, busy, call, late=0, sem=None, after=(), kind=""):
         s = {"q": q, "deps": list(deps), "after": list(after), "busy": busy, "late": late, "call": call, "sem": sem,
@@ -105,17 +116,17 @@ def rank_program(g, core, T, topo):
         steps.append(s)
         return s
 
-    def V(deps, n, call, *a, after=(), kind=""):
-        return step("v", deps, CYCLE * max(n, 64), lambda: call(*a), after=after, kind=kind)
+    def V(deps, n, call, *a, kind=""):
+        return step("v", deps, CALL + CYCLE * max(n, 64), lambda: call(*a), kind=kind)
 
-    def S(deps, n, *a, after=(), **k):
-        return step("a", deps, 65 + CYCLE * n, lambda: g.scalar.activation(*a, **k), after=after)
+    def S(deps, n, *a, fixed=ACT, **k):
+        return step("a", deps, fixed + CYCLE * n, lambda: g.scalar.activation(*a, **k))
 
     def P(deps, n, *a):
-        return step("t", deps, CYCLE * (n + 16), lambda: g.tensor.matmul_mx(*a, True, True))
+        return step("t", deps, SLOW * CYCLE * (n + 16), lambda: g.tensor.matmul_mx(*a, True, True), 120)
 
     def iota(out, n, pattern, base, mult, small=True, after=()):
-        return step("q", [], 130 + 2 * CYCLE * n,
+        return step("q", [], GSLOW * (130 + 2 * CYCLE * n),
                     lambda: g.iota(out, pattern, base, mult, allow_small_or_imprecise_dtypes=small), after=after)
 
     def dma(q, deps, late, out, in_, sem, after=()):
@@ -143,16 +154,13 @@ def rank_program(g, core, T, topo):
     def r(c, w=128):
         return slice(w * c, w * c + w)
 
-    def fill(out, n, c, after=()):
-        return V([], n, vec.memset, out, c, after=after, kind="plain")
+    def by_list(deps, n, call, *a):
+        return step("v", deps, 50 + CYCLE * n, lambda: call(*a))
 
-    def bits(out, src, dep, a, b=None):
-        if b is None:
-            return V([dep], 1, ts, out, src, a, None, A.bitwise_and, kind="plain")
-        return V([dep], 1, ts, out, src, a, b, A.bitwise_and, A.logical_shift_right, kind="plain")
-
-    def pick(deps, n, out, src):
-        return V(deps, 60 + PICK * n, cp, out, src)
+    def pick(q, deps, n, out, src):
+        if q == "v":
+            return by_list(deps, PICK * n, cp, out, src)
+        return S(deps, PICK * n, out, src, F.Copy, fixed=65)
 
     def quantize(deps, n, *a):
         return step("v", deps, 12 + 0.88 * n, lambda: vec.quantize_mx(*a))
@@ -168,84 +176,136 @@ def rank_program(g, core, T, topo):
             spans.append([i, d, 1])
 
     du = dma("a", [], LOAD, T.ut[:, 0:8], T.u[:, 0:8], "du")
-    dx = [dma("y", [], LOAD + 600, T.xt[:, r(0, 1024)], T.x[:, r(0, 1024)], "dx0")]
-    dx.append(dma("a", [], LOAD + 1200, T.xt[:, r(1, 1024)], T.x[:, r(1, 1024)], "dx1", after=[du]))
-    dw = dma("y", [], LOAD + 2400, T.wt[:], T.w[:], "dw", after=dx)
+    dx, last = [], [du]
+    for i, (a, b) in enumerate(OPT["loads"]):
+        last = [dma("ya"[i & 1], [], LOAD + RATE * b, T.xt[:, 512 * a:512 * b], T.x[:, 512 * a:512 * b], "dx%d" % i,
+                    after=last if i else [])]
+        dx.append(last[0])
+    dw = dma("y", [], LOAD + RATE * 8, T.wt[:], T.w[:], "dw", after=dx)
 
-    k_de = iota(T.de[:], 64, [[0, 4], [1, 16]], 2048, -1, False)
-    k_ip = iota(T.ip[:], 2, [[0, 2]], 0, 1, False)
-    k_k4 = iota(T.k4[:], 4, [[128, 4]], 0, 1, False)
-    k_pc = iota(T.pcol[:], 2, [[0, 2]], -64, 1)
-    k_i0 = iota(T.idv0[:], 64, [[128, 4], [1, 16]], -256, 0)
-    k_bl = iota(T.bl32[:], 32, [[1, 16], [0, 2]], 0, 0, False)
+    names = "p mid top bias uncut group twice".split()
+    col = {n: T.col[:, i:i + 1] for i, n in enumerate(names)}
+    k_p = iota(T.de[:, 0:64], 64, [[0, 4], [-1, 16]], 2048, 1, False)
+    made = {n: [V([k_p], 1, ts, col[n], T.de[:, 0:1], 2048 - c, None, A.subtract, kind="plain")]
+            for n, c in (("p", 0), ("mid", -64), ("top", 384)) if n != "top" or OPT["ways"][3] == "c"}
+
+    def fill(out, n, c):
+        return V([], n, vec.memset, out, c, kind="plain")
+
+    def bits(at, a, b):
+        return V([k_p], 1, ts, T.de2[:, at:at + 1], T.de[:, 0:1], a, b, A.bitwise_and, A.logical_shift_right,
+                 kind="plain"), T.de2[:, at:at + 1]
+
     m0 = fill(T.ut[:, 8:512], 252, 0.0)
     mz = fill(T.zoff[:], 8, 0)
-    mw = {k: fill(T["wi" + k][:], 256, -512.0) for k in "12"}
-    m1 = fill(T.flip[:], 260, 1.0)
-    k_fl = [V([m1], 2, vec.memset, T.flip[:, 256:520:260], 0.5)]
-    for at in (0, 260 + 128):
-        k_fl.append(step("q", [m1], 170 + 2 * CYCLE * 128, lambda at=at: g.affine_select(
-            T.flip[:, at:at + 128], T.flip[:, at:at + 128], [[-1, 128]], A.not_equal, -1.0, 0, 1)))
-    k_eq = fill(T.eq[:, 256:1040:260], 4, 0.0)
-    ade = bits(T.de2[:], T.de[:], k_de, 15)
-    k_da = V([ade], 64, ts, T.da[:], T.de2[:], 0, -4096, A.is_equal, A.mult)
-    k_db = V([ade], 64, ts, T.db[:], T.de2[:], 1, 1024, A.is_equal, A.mult)
-    kd = V([k_da, k_db], 128, tt, T.d0[:, 0:64], T.da[:], T.db[:], A.add)
+    low = V([k_p], 64, ts, T.de2[:, 0:64], T.de[:, 0:64], 15, None, A.bitwise_and, kind="plain")
+    p15 = T.de2[:, 0:1]
+    BOOST = 1024
+    x = [V([low], 64, ts, T.da[:], T.de2[:, 0:64], 0, -4 * BOOST, A.is_equal, A.mult),
+         V([low], 64, ts, T.db[:], T.de2[:, 0:64], 15, BOOST, A.is_equal, A.mult)]
+    kd = V(x, 64, tt, T.d0[:, 0:64], T.da[:], T.db[:], A.add)
     for n in (64, 128, 256):
         kd = S([kd], n, T.d0[:, n:2 * n], T.d0[:, 0:n], F.Copy)
-    k_co = V([bits(T.p15[:], T.ip[:], k_ip, 15)], 1, ts, T.corr[:, 0:1], T.p15[:, 0:1], 15, 1024, A.is_lt, A.mult)
-    k_cq = V([k_co], 1, ts, T.corr[:, 1:2], T.corr[:, 0:1], 256, None, A.subtract)
-    k_gr = V([bits(T.p112[:], T.ip[:], k_ip, 112)], 1, cp, T.grp[:], T.p112[:])
-    k_id = S([k_i0, k_gr], 64, T.idv[:], T.idv0[:], F.Identity, T.grp[:, 0:1])
-    a16 = bits(T.p16[:], T.ip[:], k_ip, 16)
-    k_lo = V([a16], 1, ts, T.lo[:], T.p16[:], 16, None, A.is_lt)
-    k_hi = V([a16], 1, ts, T.hi[:], T.p16[:], 16, None, A.is_equal)
-    k_pl = V([k_k4], 4, cp, T.plq[:], T.k4[:])
-    k_bl = V([k_bl], 32, cp, T.bl[:], T.bl32[:])
-    k_qn = V([bits(T.p5[:], T.ip[:], k_ip, 96, 5)], 1, cp, T.qn[:], T.p5[:])
-    k_vl = V([bits(T.r3[:], T.ip[:], k_ip, 3), k_qn], 1, ts, T.vl[:], T.r3[:], 4, T.qn[:, 0:1], A.mult, A.add)
-    k_bd = V([bits(T.p48[:], T.ip[:], k_ip, 48, 1)], 1, cp, T.bnd[:], T.p48[:])
-    k_ql = V([bits(T.p7[:], T.ip[:], k_ip, 7), k_bd], 1, ts, T.ql[:], T.p7[:], T.bnd[:, 0:1], None, A.add)
-    k_ib = [fill(T.ibias[0:64, :], 2, 0.0), fill(T.ibias[64:128, :], 2, 256.0)]
+    made["uncut"] = [V([low], 1, ts, col["uncut"], p15, 15, -BOOST, A.is_lt, A.mult)]
+    made["group"] = [V([low] + made["p"], 1, ts, col["group"], p15, -1, col["p"], A.mult, A.add)]
+    made["twice"] = [V([low], 1, ts, col["twice"], p15, 2, None, A.mult)]
+    made["bias"] = [V(made["p"], 1, ts, col["bias"], col["p"], 64, 256, A.is_ge, A.mult)]
+    uncut64 = T.col[0:64, r(names.index("uncut"), 1)]
+    x = fill(T.flip[:], 192, 1.0)
+    mark = step("q", [x], GSLOW * (170 + 2 * CYCLE * 128), lambda: g.affine_select(
+        T.flip[:, 128:256], T.flip[:, 128:256], [[-1, 128]], A.not_equal, -1.0, 0, 1), after=[k_p])
+    if "d" in "".join("".join(w) for w in OPT["sort"]):
+        k_re = V([mark], 64, ts, T.reset[:], T.flip[:, 128:256], 0.0, None, A.max)
+    k_id = V([iota(T.idv0[:], 64, [[128, 4], [1, 16]], -256, 0, after=[mark])] + made["group"], 32, ts, T.idv[:],
+             T.idv0[:], col["group"], None, A.add)
+    x = [iota(T.lf[:, 0:4], 4, [[128, 4]], 0, 1, False, [mark]),
+         iota(T.lf[:, 4:36], 32, [[1, 16], [0, 2]], 0, 0, False, [mark])]
+    k_lu = V(x, 36, cp, T.lu[:, 0:36], T.lf[:])
+    own_list, wide_list, mine_list, band_list, pair_list = (
+        T.lu[:, 0:4], lambda d: T.lu[:, 4 + 8 * d:12 + 8 * d], T.lu[:, 36:37], T.lu[:, 38:39], T.lu[:, 40:41])
+    two = col["twice"]
+    x, v = bits(66, 96, 5)
+    k_mine = V([x] + made["twice"], 1, ts, mine_list, v, two, two, A.add, A.add)
+    x, v = bits(68, 48, 0)
+    k_band = V([x] + made["twice"], 1, ts, band_list, v, two, 0.5, A.add, A.mult)
+    x, v = bits(70, 16, 4)
+    k_pair = V([x] + made["twice"], 1, ts, pair_list, v, two, None, A.add)
+    mw = {"1": fill(T.wi1[:], 256, -512.0)}
+    mw["2"] = S([mw["1"]], 512, T.wi2[:], T.wi1[:], F.Copy)
+    k_rr = fill(T.rr[:, 16:64], 48, 0.0)
+    k_gm = fill(T.gm2[:, 32:48], 16, 0.0)
     ms = S([mw["1"]], 512, T.so[:], T.wi1[:], F.Copy, 0.0, 1e26)
-    mn = S([mw["1"]], 512, T.inn[64:128, :], T.wi1[64:128, :], F.Copy)
+    mn = S([kd], 512, T.inn[64:128, :], T.d0[64:128, :], F.Copy)
 
     qu = quantize([m0, du], 128, T.uq[:], T.us[:], T.ut[:])
-    ub = pick([qu, mz], 128, T.ubq[:, 0:128].bitcast(U32), T.uq[:, 0:128].bitcast(U32).indirect(T.zoff[:, 0:8]))
-    ubs = S([qu, mz], PICK * 128, T.ubs[:, 0:128], T.us[:, 0:128].indirect(T.zoff[:, 0:8]), F.Copy)
+    ub = pick("v", [qu, mz], 128, T.ubq[:, 0:128].bitcast(U32), T.uq[:, 0:128].bitcast(U32).indirect(T.zoff[:, 0:8]))
+    ubs = pick("a", [qu, mz], 128, T.ubs[:, 0:128], T.us[:, 0:128].indirect(T.zoff[:, 0:8]))
     qw = [quantize([dw], 128, T.wq[:, r(k)], T.ws[:, r(k)], T.wt[:, r(k, 512)]) for k in range(4)]
 
-    pv, vcol, rows, kept, own = [], [], [], [], []
-    for h in range(2):
-        qx = quantize([dx[h]], 256, T.xq[:, r(h, 256)], T.xs[:, r(h, 256)], T.xt[:, r(h, 1024)])
-        for c in (2 * h, 2 * h + 1):
-            pv.append(P([qx, qu], 128, bank(4 + c), T.xq[:, r(c)], T.xs[:, r(c)], T.uq[:], T.us[:]))
-        rows.append(P([qx, ub, ubs], 256, bank(h, 256), T.ubq[:], T.ubs[:], T.xq[:, r(h, 256)], T.xs[:, r(h, 256)]))
-        vcol.append(V(pv[-2:], 2, cp, T.vc[:, r(h, 2)], T.ps[:, 512 * (4 + 2 * h):512 * (6 + 2 * h):512]))
-        kept.append(S([rows[h]], 256, T.ss[:, r(h, 256)], bank(h, 256), F.Copy))
-        for c in (2 * h, 2 * h + 1):
-            x = S([rows[h], vcol[h]], 280, T.sg[:, r(c, 256)], bank(h, 256), F.Sign, T.vc[:, c:c + 1], -1.0,
-                  accum_out=T.acc[:, c:c + 1])
-            x = V([x], 128, ts, T.eq[:, 260 * c:260 * c + 256], T.sg[:, r(c, 256)], 0.0, None, A.is_equal)
-            m = 260 * (c & 1)
-            own.append(V([x, k_eq] + k_fl, 129, scan, T.ow[:, 260 * c:260 * c + 257], T.flip[:, m:m + 257],
-                         T.eq[:, 260 * c:260 * c + 257], T.acc[:, c:c + 1], A.mult, A.subtract))
-    twin = P([rows[1]], 256, bank(2, 256), T.ubq[:], T.ubs[:], T.xq[:, r(1, 256)], T.xs[:, r(1, 256)])
+    stages = OPT["loads"]
+    pv, vcol, rows, kept, twin = {}, {}, [], [], {}
+    for j, (a, b) in enumerate(stages):
+        n, at = 128 * (b - a), slice(128 * a, 128 * b)
+        qx = quantize([dx[j]], n, T.xq[:, at], T.xs[:, at], T.xt[:, 512 * a:512 * b])
+        for c in range(a, b):
+            pv[c] = P([qx, qu], 128, bank(4 + c), T.xq[:, r(c)], T.xs[:, r(c)], T.uq[:], T.us[:])
+        rows.append(P([qx, ub, ubs], n, bank(j, n), T.ubq[:], T.ubs[:], T.xq[:, at], T.xs[:, at]))
+        x = V([pv[c] for c in range(a, b)], 2, cp, T.vc[:, a:b], T.ps[:, 512 * (4 + a):512 * (4 + b):512])
+        vcol.update({c: x for c in range(a, b)})
+        kept.append(S([rows[j]], n, T.ss[:, at], bank(j, n), F.Copy))
+        named.update({"qx%d" % j: qx, "row%d" % j: rows[j], "keep%d" % j: kept[j], "col%d" % j: x})
+        if j in OPT["twin"]:
+            free = len(stages) if len(stages) < 4 else 4
+            twin[j] = P([rows[j]] + [vcol[0]] * (free == 4), n, bank(free, n), T.ubq[:], T.ubs[:], T.xq[:, at],
+                        T.xs[:, at]), free
     pz = []
     for c in range(4):
-        out = T.cb[:, r(c, 256)]
-        if c >= 2:
-            x = V([pv[c], kept[0]], 256, ts, out, T.ss[:, 0:256], bank(4 + c, 1), 0.5, A.is_ge, A.subtract)
-        elif c < OPT["twin"]:
-            x = V([twin, vcol[0]], 256, ts, out, bank(2, 256), T.vc[:, c:c + 1], 0.5, A.is_gt, A.subtract)
-        else:
-            x = S([rows[1], vcol[0]], 256, T.sgb[:, r(c, 256)], bank(1, 256), F.Sign, T.vc[:, c:c + 1], -1.0)
-            x = V([x], 128, ts, out, T.sgb[:, r(c, 256)], 0.0, 0.5, A.is_lt, A.subtract)
-        x = V([x], 64, scan, T.z1[:, r(c)], T.cb[:, 256 * c:256 * c + 128], T.cb[:, 256 * c + 128:256 * c + 256],
-              256.0 - 128, A.add, A.add)
-        pz.append(V([x, own[c]], 1, ts, T.pz1[:, c:c + 1], T.z1[:, 128 * c + 127:128 * c + 128],
-                    T.ow[:, 260 * c + 256:260 * c + 257], 128, A.add, A.add))
-    sl = S([k_pl] + kept, PICK * 64, T.sl[:], T.ss[:, 0:512].indirect(T.plq[:, 0:4]), F.Copy)
+        parts, fill_to = [], 512 * c
+        for j, (a, b) in enumerate(stages):
+            way = OPT["sort"][c][j]
+            runs = [(a, b)]
+            if a <= c < b:
+                lo, hi = {"i": (a, b), "o": (c, c + 1), "d": (c + 1, c + 1)}[way[0]]
+                n, m = 128 * (hi - lo), 128 * (1 + lo - c)
+                if way[0] == "d":
+                    x = V([twin[j][0], pv[c]], 128, ts, T.eq[:, 256 * c:256 * c + 128],
+                          bank(twin[j][1], 128, 128 * (c - a)), bank(4 + c, 1), 2.0, A.is_equal, A.mult)
+                    own = V([x, k_re], 64, scan, T.ow[:, 256 * c:256 * c + 128], T.reset[:],
+                            T.eq[:, 256 * c:256 * c + 128], 0.0, A.mult, A.subtract)
+                    n = 128
+                else:
+                    x = S([rows[j], vcol[c]], n + 24, T.sg[:, 256 * c:256 * c + n], bank(j, n, 128 * (lo - a)), F.Sign,
+                          T.vc[:, c:c + 1], -1.0, accum_out=T.acc[:, c:c + 1])
+                    named["sign%d" % c] = x
+                    x = V([x], n / 2, ts, T.eq[:, 256 * c:256 * c + n], T.sg[:, 256 * c:256 * c + n], 0.0, None,
+                          A.is_equal)
+                    own = V([x, mark], n / 2, scan, T.ow[:, 256 * c:256 * c + n], T.flip[:, m:m + n],
+                            T.eq[:, 256 * c:256 * c + n], T.acc[:, c:c + 1], A.mult, A.subtract)
+                result, first = T.ow[:, 256 * c + n - 1:256 * c + n], float(128 * (hi - lo))
+                runs, way = [(a, lo), (hi, b)], way[1:]
+            for lo, hi in runs:
+                n = 128 * (hi - lo)
+                if n == 0:
+                    continue
+                out, up = T.cb[:, fill_to:fill_to + n], lo > c
+                if way == "s":
+                    y = S([rows[j], vcol[c]], n, T.sgb[:, fill_to:fill_to + n], bank(j, n, 128 * (lo - a)), F.Sign,
+                          T.vc[:, c:c + 1], -1.0)
+                    y = V([y], n / 2, ts, out, T.sgb[:, fill_to:fill_to + n], 0.0, 2.0, A.is_lt if up else A.is_le,
+                          A.mult)
+                else:
+                    dep, src = ((kept[j], T.ss[:, 128 * lo:128 * hi]) if way in "kK" else
+                                (twin[j][0], bank(twin[j][1], n, 128 * (lo - a))))
+                    has, v = (vcol[c], T.vc[:, c:c + 1]) if way in "kt" else (pv[c], bank(4 + c, 1))
+                    y = V([dep, has], n, ts, out, src, v, 2.0, A.is_gt if up else A.is_ge, A.mult)
+                parts.append(y)
+                fill_to += n
+        n = (fill_to - 512 * c) // 2
+        x = V(parts, n / 2, scan, T.z1[:, 256 * c:256 * c + n], T.cb[:, 512 * c:512 * c + n],
+              T.cb[:, 512 * c + n:512 * c + 2 * n], first, A.add, A.add)
+        pz.append(V([x, own], 1, ts, T.pz1[:, c:c + 1], T.z1[:, 256 * c + n - 1:256 * c + n], result, 0.5,
+                    A.add, A.mult))
+    sl = pick("a", [k_lu] + kept, 64, T.sl[:], T.ss[:, 0:512].indirect(own_list))
 
     def quadrants(deps, mid, out, w, src, many):
         y = V(deps, 2 * w, tt, mid[0:64, 0:w], src[0:64, 0:w], src[64:128, 0:w], A.max, kind="across")
@@ -253,101 +313,123 @@ def rank_program(g, core, T, topo):
                 for a in range(many)]
 
     def make_list(deps, k, many):
-        wi, wx, et, eh, eb = (T[n + k] for n in ("wi", "wx", "et", "eh", "eb"))
-        x = V(deps + [k_id, mw[k]], 60 + PUT * 64, cp, wi[:, 0:512].indirect(T["pz" + k][:, 0:4]), T.idv[:])
-        x = V([x, kd], 256, scan, wx[:], T.d0[:], wi[:], 0.0, A.add, A.max)
-        x = V([x], 16, vec.transpose, et[:], wx[:, 15:512:16])
-        x = [V([x], 32, tt, eh[:, r(h, 16)], et[:, 0:16], et[:, 16:32], A.max) for h in range(2)]
-        x = V(x, 16, vec.transpose, eb[:], eh[:])
-        gm = quadrants([x], T["ge" + k], T["gm" + k], 32, eb, many)
-        p = slice(0, 32 * many)
-        return gm, [V(gm + [k_co], 32, ts, T["lw" + k][a:a + 32 * many, :], T["gm" + k][p, :], T.corr[p, 0:1], 256,
-                      A.subtract, A.add) for a in range(0, 128, 32 * many)]
+        wi, wx, et, eh, eb, gm = (T[n + k] for n in ("wi", "wx", "et", "eh", "eb", "gm"))
+        put = by_list(deps + [k_id, mw[k]], PUT * 64, cp, wi[:, 0:512].indirect(T["pz" + k][:, 0:4]), T.idv[:])
+        diag = V([put, kd], 256, scan, wx[:], T.d0[:], wi[:], 0.0, A.add, A.max)
+        turn = V([diag], 16, vec.transpose, et[:], wx[:, 15:512:16])
+        x = [V([turn], 32, tt, eh[:, r(h, 16)], et[:, 0:16], et[:, 16:32], A.max) for h in range(2)]
+        back = V(x, 16, vec.transpose, eb[:], eh[:])
+        named.update({"put" + k: put, "diag" + k: diag, "turn" + k: turn, "max" + k: x[0], "maxb" + k: x[1],
+                      "back" + k: back})
+        x = quadrants([back], T["ge" + k], gm, 32, eb, many)
+        if many == 4:
+            return x, [V(x + made["uncut"], 32, ts, T["lw" + k][:], gm[:, 0:32], col["uncut"], 256, A.add, A.add)]
+        return ([S(x, 32, gm[64:128, 0:32], gm[0:64, 0:32], F.Copy)],
+                [V(x + made["uncut"], 32, ts, T["lw" + k][r(h, 64), :], gm[0:64, 0:32], uncut64, 256, A.add, A.add)
+                 for h in range(2)])
 
-    so = V(pz + [sl, ms], 60 + PUT * 64, cp, T.so[:, 0:512].indirect(T.pz1[:, 0:4]), T.sl[:])
+    so = by_list(pz + [sl, ms], PUT * 64, cp, T.so[:, 0:512].indirect(T.pz1[:, 0:4]), T.sl[:])
     tr = [V([so], 128 * n, vec.transpose, T.tr[:, 128 * i:128 * (i + n)], T.so[:, 128 * d:128 * (d + n)])
           for i, d, n in spans]
-    v16 = V(tr, 24, tt, T.v16[:], T.tr[:, 0:384:32], T.tr[:, 16:384:32], A.max)
+    v16 = V(tr, 24, tt, T.v16[:, 0:12], T.tr[:, 0:384:32], T.tr[:, 16:384:32], A.max)
     out_s, in_s = send([v16], [(d, T.v16[:, r(i, 4)], T.rs[:, r(rank, 4)]) for i, d in enumerate(others)], "rem_s",
                        FIRST, HOP)
     tro = V([so], 128, vec.transpose, T.tr[:, 384:512], T.so[:, r(rank)])
     rso = V([tro], 8, tt, T.rs[:, r(rank, 4)], T.tr[:, 384:512:32], T.tr[:, 400:512:32], A.max)
-    _, lw = make_list(pz + [ms, mn], "1", 2)
+    named.update(so=so, tr=tr[0], trb=tr[-1], v16=v16, tro=tro, rso=rso, sl=sl, ub=ub)
+    named.update({"qw%d" % k: qw[k] for k in range(4)})
+    gm, lw = make_list(pz + [ms, mw["2"]], "1", OPT["many"][0])
 
     pq, pp = [], []
-    for i, d in enumerate(others):
-        pq.append(pick(lw, 128, T.sq[:, r(i)].bitcast(U32), T.xq[:, 0:512].bitcast(U32).indirect(T.lw1[:, r(d, 8)])))
-        pp.append(S(lw, PICK * 128, T.sp[:, r(i)], T.xs[:, 0:512].indirect(T.lw1[:, r(d, 8)]), F.Copy))
+    for i, d, n in spans if OPT["picks"] else [(i, d, 1) for i, d in enumerate(others)]:
+        of, at = T.lw1[:, 8 * d:8 * (d + n)], slice(128 * i, 128 * (i + n))
+        pq.append(pick("v", lw, 128 * n, T.sq[:, at].bitcast(U32), T.xq[:, 0:512].bitcast(U32).indirect(of)))
+        pp.append(pick("a", lw, 128 * n, T.sp[:, at], T.xs[:, 0:512].indirect(of)))
+    nb = S(gm + [k_pair] + made["uncut"], PICK * 16, T.nb[:], T.gm1[:, 0:32].indirect(pair_list), F.Identity,
+           col["uncut"], fixed=65)
+    out_i, in_i = send([nb], [(d, T.nb[:, r(d, 4)], T.rn[:, r(rank, 4)]) for d in others], "rem_i", 200, HOP,
+                       after=[out_s])
     out_c, in_c = send(pq, [(d, T.sq[:, r(i)].bitcast(U8), T.lq[:, r(rank)].bitcast(U8)) for i, d in enumerate(others)],
                        "rem_c", 200, 2 * HOP, after=[out_s])
-    out_p, in_p = send(pp, [(d, T.sp[:, r(i)], T.lp[:, r(rank)]) for i, d in enumerate(others)], "rem_p", 200, 2 * HOP,
-                       after=[out_s])
-    ia = V(lw + [k_lo], 8, ts, T.ia[:], T.lw1[:, 0:32:2], 256, T.lo[:, 0:1], A.subtract, A.mult)
-    ib = V(lw + [k_hi], 8, ts, T.ib[:], T.lw1[:, 1:32:2], 256, T.hi[:, 0:1], A.subtract, A.mult)
-    nb = V([ia, ib], 32, tt, T.nb[:], T.ia[:], T.ib[:], A.add)
-    out_i, in_i = send([nb], [(d, T.nb[:, r(d, 4)], T.rn[:, r(rank, 4)]) for d in others], "rem_i", 200, 2 * HOP,
-                       after=[out_s])
+    out_p, in_p = send(pp, [(d, T.sp[:, r(i)], T.lp[:, r(rank)]) for i, d in enumerate(others)], "rem_p", 200,
+                       2.5 * HOP, after=[out_c])
     mi = iota(T.iw[0:64, :], 512, [[1, 4], [0, 128]], 0, 0, after=[out_c, out_p, out_i])
+    named.update(out_i=out_i, out_c=out_c, out_p=out_p, nb=nb, lw=lw[0], lwb=lw[-1], gm1=gm[0])
+    named.update({"pq%d" % i: x for i, x in enumerate(pq)})
+    named.update({"pp%d" % i: x for i, x in enumerate(pp)})
 
-    of = T.lw1[:, 8 * rank:8 * rank + 8]
-    have = {rank: S(lw + kept, PICK * 128, T.sb[:, r(rank)], T.ss[:, 0:512].indirect(of), F.Copy)}
-    oq = pick(lw, 128, T.lq[:, r(rank)].bitcast(U32), T.xq[:, 0:512].bitcast(U32).indirect(of))
-    ow = S(lw, PICK * 128, T.lp[:, r(rank)], T.xs[:, 0:512].indirect(of), F.Copy)
+    of = T.lw1[:, r(rank, 8)]
+    have = {rank: pick("a", lw + kept, 128, T.sb[:, r(rank)], T.ss[:, 0:512].indirect(of))}
+    oq = pick("v", lw, 128, T.lq[:, r(rank)].bitcast(U32), T.xq[:, 0:512].bitcast(U32).indirect(of))
+    ow = pick("a", lw, 128, T.lp[:, r(rank)], T.xs[:, 0:512].indirect(of))
     nbo = S([nb], 4, T.rn[:, r(rank, 4)], T.nb[:, r(rank, 4)], F.Copy)
 
     rr = quadrants([in_s, rso], T.r1, T.rr, 16, T.rs, 4)
-    v1 = pick(rr + [k_vl], 16, T.v1[:], T.rr[:, 0:16].indirect(T.vl[:, 0:1]))
+    v1 = pick(OPT["v1"], rr + [k_mine, k_rr], 16, T.v1[:], T.rr[:, 0:64].indirect(mine_list))
     for i, d in enumerate(others):
-        src = T.rr[:, 0:16].indirect(T.bl[:, r(d, 8)])
-        x = S(rr + [k_bl], PICK * 128, T.bx[:, r(i)], src, F.Copy) if i else pick(rr + [k_bl], 128, T.bx[:, r(i)], src)
+        x = pick(OPT["gather"][i], rr + [k_lu], 128, T.bx[:, r(i)], T.rr[:, 0:16].indirect(wide_list(d)))
         have[d] = V([x], 128, vec.transpose, T.sb[:, r(d)], T.bx[:, r(i)])
+        named.update({"g%d" % i: x, "t%d" % i: have[d]})
+    named.update(oq=oq, ow=ow, sbo=have[rank], nbo=nbo, l2=rr[3], v1=v1)
 
-    def ways(s):
-        rest = [d for d in range(N) if d != s]
-        parts = []
-        for d in rest:
-            by_s = OPT["by_s"](rank, s, d) if "by_s" in OPT else s == 3 or d == rank
-            if parts and parts[-1][0] + parts[-1][1] == d and parts[-1][2] == by_s and rank not in (d, d - 1):
-                parts[-1][1] += 1
-            else:
-                parts.append([d, 1, by_s])
-        return parts
-
-    fin = []
+    fin, pz2 = {}, []
     for s in range(N):
-        done = []
-        for d, n, by_s in ways(s):
+        way, done, mine = OPT["ways"][s], [], T.v1[:, s:s + 1]
+        parts = [(0, s)] * (s > 0) + [(s + 1, N - 1 - s)] * (s < N - 1)
+        if way == "v" and OPT.get("fine"):
+            parts = [(d, 1) for d in range(N) if d != s]
+        for d, n in parts:
             at = slice(384 * s + 128 * (d - (d > s)), 384 * s + 128 * (d - (d > s) + n))
             deps, src = [v1] + [have[e] for e in range(d, d + n)], T.sb[:, 128 * d:128 * (d + n)]
-            if by_s:
-                x = S(deps, 128 * n, T.sg2[:, at], src, F.Sign, T.v1[:, s:s + 1], -1.0)
-                x = V([x], 64 * n, ts, T.c2[:, at], T.sg2[:, at], 0.0, 0.5, A.is_le if d < s else A.is_lt, A.subtract)
+            if way == "v":
+                x = V(deps, 128 * n, ts, T.c2[:, at], src, mine, 0.5, A.is_ge if d < s else A.is_gt, A.subtract)
             else:
-                x = V(deps, 128 * n, ts, T.c2[:, at], src, T.v1[:, s:s + 1], 0.5, A.is_ge if d < s else A.is_gt,
-                      A.subtract)
+                x = S(deps, 128 * n, T.sg2[:, at], src, F.Sign, mine, -1.0)
+            if way == "s":
+                x = V([x], 64 * n, ts, T.c2[:, at], T.sg2[:, at], 0.0, 0.5, A.is_le if d < s else A.is_lt, A.subtract)
+            if way == "c":
+                k = 1.0 if s else -1.0
+                x = S([x], 128 * n + 24, T.c2[:, at], T.sg2[:, at], F.Relu, 0.0, k, accum_out=T.acc2[:, s:s + 1])
+                named["relu"] = x
+                base = "top" if s else "p"
+                pz2.append(V([x] + made[base], 1, ts, T.pz2[:, s:s + 1], T.acc2[:, s:s + 1], -k, col[base],
+                             A.mult, A.add))
             done.append(x)
-        fin.append(V(done + [k_pc], 96, scan, T.z2[:, r(s, 192)], T.c2[:, 384 * s:384 * s + 192],
-                     T.c2[:, 384 * s + 192:384 * s + 384], T.pcol[:, 0:1], A.add, A.add))
-    pz2 = V(fin, 4, ts, T.pz2[:], T.z2[:, 191:768:192], 256, None, A.add)
-    gm, lm = make_list([pz2], "2", 4)
+        if way != "c":
+            fin[s] = V(done + made["mid"], 96, scan, T.z2[:, r(s, 192)], T.c2[:, 384 * s:384 * s + 192],
+                       T.c2[:, 384 * s + 192:384 * s + 384], col["mid"], A.add, A.add)
+    a, b = min(fin), max(fin) + 1
+    pz2.append(V(list(fin.values()), 4, ts, T.pz2[:, a:b], T.z2[:, 192 * a + 191:192 * b:192], 256, None, A.add))
+    gm, lm = make_list(pz2, "2", OPT["many"][1])
 
     ic = [S([in_i, nbo, mn], 16, T.inn[64:128, h:512:32], T.rn[64:128, :], F.Copy) for h in (0, 16)]
     iw = V(ic, 256, vec.transpose, T.iw[64:128, :], T.inn[64:128, :])
-    ql = V(gm + [k_ql, k_cq], 60 + PICK * 16, ts, T.q2[:], T.gm2[:, 0:32].indirect(T.ql[:, 0:1]), T.corr[:, 1:2], None,
-           A.subtract)
-    ig = S([ql, iw, mi] + k_ib, PICK * 128, T.gid[:], T.iw[:, 0:512].indirect(T.q2[:, 0:8]), F.Identity,
-           T.ibias[:, 0:1])
+    ql = by_list(gm + [k_band, k_gm], PICK * 16, ts, T.q2[:], T.gm2[:, 0:48].indirect(band_list), col["uncut"], 256,
+                 A.add, A.add)
+    ig = S([ql, iw, mi] + made["bias"], PICK * 128, T.gid[:], T.iw[:, 0:512].indirect(T.q2[:, 0:8]), F.Identity,
+           col["bias"], fixed=65)
     dma("a", [ig], LOAD, T.ids[:, :], T.gid[0:128:16, :], "dst")
+    named.update(iw=iw, ql=ql, ig=ig, ic=ic[0], icb=ic[1], lm=lm[0], lmb=lm[-1], pz2=pz2[-1], gm2=gm[0])
 
-    for k, n in ((0, 2), (2, 1), (3, 1)):
+    for k, n in OPT["bands"]:
         of, at = T.lw2[:, 8 * k:8 * (k + n)], slice(128 * k, 128 * (k + n))
-        a = pick(lm + [oq, in_c], 128 * n, T.fq[:, at].bitcast(U32), T.lq[:, 0:512].bitcast(U32).indirect(of))
-        b = S(lm + [ow, in_p], PICK * 128 * n, T.fp[:, at], T.lp[:, 0:512].indirect(of), F.Copy)
+        a = pick("v", lm + [oq, in_c], 128 * n, T.fq[:, at].bitcast(U32), T.lq[:, 0:512].bitcast(U32).indirect(of))
+        b = pick("a", lm + [ow, in_p], 128 * n, T.fp[:, at], T.lp[:, 0:512].indirect(of))
+        named.update({"a%d" % k: a, "b%d" % k: b})
         for j in range(k, k + n):
             x = P([a, b, qw[j]], 128, bank(j), T.wq[:, r(j)], T.ws[:, r(j)], T.fq[:, r(j)], T.fp[:, r(j)])
-            x = V([x], 128, cp, T.ysb[:, r(j)], bank(j))
-            dma("y", [x], LOAD + 200, T.y[:, r(j)], T.ysb[:, r(j)], "dst")
+            if OPT["ycopy"][j] == "v":
+                x = V([x], 128, cp, T.ysb[:, r(j)], bank(j))
+            else:
+                x = S([x], 128, T.ysb[:, r(j)], bank(j), F.Copy)
+            named["y%d" % j] = x
+            dma(OPT["st"][j], [x], LOAD + 200, T.y[:, r(j)], T.ysb[:, r(j)], "dst")
 
+    for rule in OPT["order"]:
+        rule = [named[n] for n in rule.split()]
+        for a, b in zip(rule, rule[1:]):
+            if a is not b:
+                b["after"].append(a)
     _arrange(steps)
     order = {q: sorted((s for s in steps if s["q"] == q), key=lambda s: s["at"]) for q in queues}
     for q in queues:

@@ -3,6 +3,7 @@ from concourse.mybir import dt, AluOpType as A, ActivationFunctionType as F
 
 N, CH = 4, 128
 X4 = "float8_e4m3fn_x4"
+PART, PART2, HALF = 656, 400, 272
 
 
 def _sb(n, d):
@@ -15,40 +16,50 @@ SCRATCH = {
     "uq": _sb(128, X4), "us": _sb(128, "uint8"), "ubq": _sb(128, X4), "ubs": _sb(128, "uint8"),
     "sq": _sb(384, X4), "sp": _sb(384, "uint8"), "lq": _sb(512, X4), "lp": _sb(512, "uint8"),
     "fq": _sb(512, X4), "fp": _sb(512, "uint8"),
-    "zoff": _sb(8, "uint16"), "flip": _sb(384, "bfloat16"), "reset": _sb(128, "bfloat16"),
+    "zoff": _sb(8, "uint16"), "flip": _sb(144, "bfloat16"), "reset": _sb(128, "bfloat16"),
     "de": _sb(66, "int32"), "de2": _sb(72, "int32"),
     "da": _sb(64, "bfloat16"), "db": _sb(64, "bfloat16"), "d0": _sb(512, "bfloat16"),
-    "col": _sb(16, "float32"), "lf": _sb(36, "int32"), "lu": _sb(42, "uint16"),
+    "col": _sb(16, "float32"), "lf": _sb(38, "int32"), "lu": _sb(44, "uint16"),
     "idv0": _sb(64, "bfloat16"), "idv": _sb(64, "bfloat16"),
-    "ss": _sb(512, "float32"), "vc": _sb(4, "float32"), "sg": _sb(1024, "bfloat16"), "sgb": _sb(2048, "bfloat16"),
-    "acc": _sb(4, "float32"), "eq": _sb(1024, "bfloat16"), "ow": _sb(1024, "bfloat16"),
-    "cb": _sb(2048, "bfloat16"), "z1": _sb(1024, "float16"),
-    "sl": _sb(64, "float32"), "so": _sb(512, "float32"), "tr": _sb(512, "float32"), "v16": _sb(16, "float32"),
-    "nb": _sb(16, "float32"),
-    "rs": _sb(16, "float32"), "r1": _sb(16, "float32"), "rr": _sb(64, "float32"), "bx": _sb(384, "float32"),
-    "sb": _sb(512, "float32"), "v1": _sb(16, "float32"), "sg2": _sb(1536, "bfloat16"), "c2": _sb(1536, "bfloat16"),
-    "acc2": _sb(4, "float32"), "z2": _sb(768, "bfloat16"), "rn": _sb(16, "float32"),
-    "inn": _sb(512, "bfloat16"), "iw": _sb(512, "bfloat16"), "q2": _sb(16, "uint16"), "gid": _sb(128, "float32"),
+    "ss": _sb(512, "float32"), "vc": _sb(4, "float32"), "sg": _sb(512, "bfloat16"), "sgb": _sb(2048, "bfloat16"),
+    "acc": _sb(8, "float32"), "eq": _sb(576, "bfloat16"), "sgc": _sb(1152, "bfloat16"),
+    "cb": _sb(4 * PART, "bfloat16"), "t3": _sb(32, "float32"),
+    "sl": _sb(64, "float32"), "so": _sb(512, "float32"), "tr": _sb(384, "float32"),
+    "pa": _sb(24, "float32"), "gm": _sb(32, "float32"), "nb": _sb(16, "float32"), "et": _sb(436, "float16"),
+    "rs": _sb(24, "float32"), "rr": _sb(128, "float32"), "bx": _sb(384, "float32"), "bo": _sb(128, "float32"),
+    "sb": _sb(512, "float32"), "v1": _sb(16, "float32"), "vo": _sb(16, "float32"),
+    "sg2": _sb(4 * PART2, "bfloat16"), "c2": _sb(1536, "bfloat16"),
+    "acc2": _sb(4, "float32"), "rn": _sb(16, "float32"),
+    "inn": _sb(512, "bfloat16"), "iw": _sb(512, "bfloat16"), "gid": _sb(512, "float32"),
     "ysb": _sb(512, "float32"),
     "ps": ("psum", [128, 4096], "float32"),
 }
 for _k in ("1", "2"):
-    SCRATCH.update({"pz" + _k: _sb(4, "uint16"), "wi" + _k: _sb(512, "bfloat16"), "wx" + _k: _sb(512, "float16"),
-                    "et" + _k: _sb(32, "float16"), "eh" + _k: _sb(32, "float16"), "eb" + _k: _sb(32, "float16"),
-                    "ge" + _k: _sb(32, "float32"), "gm" + _k: _sb(48, "float32"), "lw" + _k: _sb(32, "uint16")})
+    SCRATCH.update({"z" + _k: _sb(4 * HALF, "uint16"), "wi" + _k: _sb(512, "bfloat16"), "wx" + _k: _sb(512, "float16"),
+                    "ez" + _k: _sb(288, "uint16"), "lw" + _k: _sb(32, "uint16")})
 SEMAPHORES = ["v", "a", "t", "q", "du", "dx0", "dx1", "dx2", "dx3", "dw", "dst",
               "rem_s", "rem_c", "rem_p", "rem_i", "loc"]
 
 WAIT = 215
 CYCLE, CALL, ACT, SLOW, GSLOW = 0.83, 0, 65, 1.0, 1.0
+ROUNDS = 0
 SLACK = 0
-LOAD, RATE, FIRST, HOP = 1000, 500, 1100, 1300
-OPT = {"loads": ((0, 1), (1, 2), (2, 3), (3, 4)), "twin": (3,), "many": (2, 2),
-       "sort": (("o", "k", "k", "s"), ("K", "o", "s", "s"), ("K", "K", "o", "t"), ("K", "K", "K", "o")),
-       "ways": "cvvv", "fine": 1, "ycopy": "vvvv",
+LOAD, RATE, FIRST, HOP = 1000, 500, 1000, 1300
+OPT = {"loads": ((0, 1), (1, 2), (2, 3), (3, 4)), "twin": (2, 3),
+       "count": (((1, 2, "k"), (2, 3, "t"), (3, 4, "c")), ((0, 1, "K"), (2, 3, "t"), (3, 4, "c")),
+                 ((0, 2, "K"), (3, 4, "t")), ((0, 3, "K"), (3, 4, "T"))), "col": "vvv",
+       "few": 4, "merge": ("aos nbc nac", "noc nac nbc", "aoc boc abc", "aoc boc noc"), "ycopy": "vvvv", "vo": "a", "sl3": "a", "split": 1,
        "gather": "vaa", "v1": "v", "bands": ((0, 1), (1, 1), (2, 1), (3, 1)), "st": "yyyy",
-       "order": ("relu ic icb", "nb pp0", "out_i out_c", "put2 iw diag2"),
-       "picks": 0}
+       "order": (
+           "m0 m1 k_low mz ones half b_quad da db k_group k_et k_etb qu d64 k_etc k_lu qx0 ub k_id qx1 k_twice col0",
+           "col0 b_pair qx2 col1 e10 k_pair qx3 eq0 col2 e01 e20 e02 eq1 e30 own0 eq2 eq3 e33 own1 own2 own3 t3 e23 e12",
+           "e12 z3 z0 z2 z1 k_eight b_mine k_bias so put1 tr trb diag1 low0 low1 low2 turn1a turn1b turn1c turn1d",
+           "turn1d qw0 k_mine join1 joinb1 back1a back1b back1c back1d qw1 gm pqf pqn to oq l2a l2 v1 ga",
+           "ga early tn ta earlyb tb",
+           "za qw2", "zb qw2", "zn qw2", "zo qw2 put2 qw3 diag2 iw turn2a turn2b turn2c turn2d iwb join2",
+           "ms d128 ubs d256 keep0 sign0 keep1 sign1 keep2 sign2 s03 s13 sum0 sum1 sl sl3 d512 keep3 m2 mn",
+           "mn go nb ppf ppn vo nbo gn gb", "ra ic", "rb ic", "rn ic", "ro ic ow",
+           "out_i out_cf out_pf out_cn out_pn")}
 
 
 def _routes(core, cores, topo):
@@ -86,16 +97,28 @@ def _arrange(steps):
             s["chain"] = s["busy"] + 1 + max([s["late"]] + [w + chain(n) for n, w in later[s["n"]]])
         return s["chain"]
 
-    taken = {}
-    for s in sorted(steps, key=lambda s: -chain(s)):
-        t = max([0] + [d["end"] + WAIT for d in s["deps"]] + [d["at"] + d["busy"] for d in s["after"]])
-        if s["q"]:
-            for a, b, kind in sorted(taken.setdefault(s["q"], [])):
-                if t < a and t + s["busy"] - SLACK + WAIT * (s["kind"] == "across" and kind == "") <= a:
-                    break
-                t = max(t, b + WAIT * (kind == "across" and s["kind"] == ""))
-            taken[s["q"]].append((t, t + s["busy"], s["kind"]))
-        s["at"], s["end"] = t, t + s["busy"] + s["late"]
+    def place(key, back):
+        taken, first, second = {}, "" if back else "across", "across" if back else ""
+        for s in sorted(steps, key=key):
+            if back:
+                t = max([s["late"]] + [n["left"] + w for n, w in later[s["n"]]])
+            else:
+                t = max([0] + [d["end"] + WAIT for d in s["deps"]] + [d["at"] + d["busy"] for d in s["after"]])
+            if s["q"]:
+                for a, b, kind in sorted(taken.setdefault(s["q"], [])):
+                    if t < a and t + s["busy"] - SLACK + WAIT * (s["kind"] == first and kind == second) <= a:
+                        break
+                    t = max(t, b + WAIT * (kind == first and s["kind"] == second))
+                taken[s["q"]].append((t, t + s["busy"], s["kind"]))
+            if back:
+                s["left"] = t + s["busy"] + 1
+            else:
+                s["at"], s["end"] = t, t + s["busy"] + s["late"]
+
+    place(lambda s: -chain(s), False)
+    for _ in range(ROUNDS):
+        place(lambda s: (-s["at"] - s["busy"], chain(s)), True)
+        place(lambda s: (-s["left"], -chain(s)), False)
 
 
 def rank_program(g, core, T, topo):
@@ -105,7 +128,7 @@ def rank_program(g, core, T, topo):
     cores = T.cores
     others = [d for d in range(N) if d != rank]
     routes = _routes(core, cores, topo)
-    FEW = 4
+    FEW = OPT["few"]
     U32, U8 = dt.uint32, dt.uint8
     queues = {"v": g.vector, "a": g.scalar, "t": g.tensor, "q": g, "y": g.sync}
     steps, counts, named = [], {}, {}
@@ -138,9 +161,10 @@ def rank_program(g, core, T, topo):
         for d, src, dst in pieces:
             rid, pid, _ = topo.addr(cores[d])
             engines = routes[cores[d]][:FEW] if sem == "rem_s" else routes[cores[d]]
+            sides = dict(srcs=src, dsts=[dst], alu_op=3) if isinstance(src, list) else dict(src=src, dst=dst)
             tr.append(RemoteDMATransfer(dst_ids=[DstId(rid=rid, pnc=pid)],
                                         dma_engine_mask=sum(1 << e for e in engines),
-                                        remote_sem=T.sem[sem], src=src, dst=dst))
+                                        remote_sem=T.sem[sem], **sides))
             counts["loc"] = counts.get("loc", 0) + len(engines)
         call = step("q", deps, busy, lambda: g.remote_dma_fused(tr, local_sem=T.sem.loc), sem=("loc", None), after=after)
         n = [len(_routes(c, cores, topo)[core]) for c in cores if c != core]
@@ -168,6 +192,8 @@ def rank_program(g, core, T, topo):
     def bank(b, n=128, a=0):
         return T.ps[:, 512 * b + a:512 * b + a + n]
 
+    near = [d for d in others if topo.chip(cores[d]) == topo.chip(core)]
+    far = [d for d in others if d not in near]
     spans = []
     for i, d in enumerate(others):
         if spans and spans[-1][1] + spans[-1][2] == d:
@@ -183,11 +209,10 @@ def rank_program(g, core, T, topo):
         dx.append(last[0])
     dw = dma("y", [], LOAD + RATE * 8, T.wt[:], T.w[:], "dw", after=dx)
 
-    names = "p mid top bias uncut group twice".split()
+    names = "p eight bias group twice".split()
     col = {n: T.col[:, i:i + 1] for i, n in enumerate(names)}
     k_p = iota(T.de[:, 0:64], 64, [[0, 4], [-1, 16]], 2048, 1, False)
-    made = {n: [V([k_p], 1, ts, col[n], T.de[:, 0:1], 2048 - c, None, A.subtract, kind="plain")]
-            for n, c in (("p", 0), ("mid", -64), ("top", 384)) if n != "top" or OPT["ways"][3] == "c"}
+    made = {"p": [iota(col["p"], 1, [[0, 1]], 0, 1, after=[k_p])]}
 
     def fill(out, n, c):
         return V([], n, vec.memset, out, c, kind="plain")
@@ -200,221 +225,257 @@ def rank_program(g, core, T, topo):
     mz = fill(T.zoff[:], 8, 0)
     low = V([k_p], 64, ts, T.de2[:, 0:64], T.de[:, 0:64], 15, None, A.bitwise_and, kind="plain")
     p15 = T.de2[:, 0:1]
-    BOOST = 1024
-    x = [V([low], 64, ts, T.da[:], T.de2[:, 0:64], 0, -4 * BOOST, A.is_equal, A.mult),
-         V([low], 64, ts, T.db[:], T.de2[:, 0:64], 15, BOOST, A.is_equal, A.mult)]
-    kd = V(x, 64, tt, T.d0[:, 0:64], T.da[:], T.db[:], A.add)
+    x = [V([low], 64, ts, out[:], T.de2[:, 0:64], at, k, A.is_equal, A.mult)
+         for out, at, k in ((T.da, 0, 768), (T.db, 1, -1280))]
+    kd = V(x, 128, tt, T.d0[:, 0:64], T.da[:], T.db[:], A.add)
+    named.update(m0=m0, mz=mz, da=x[0], db=x[1], d64=kd)
     for n in (64, 128, 256):
-        kd = S([kd], n, T.d0[:, n:2 * n], T.d0[:, 0:n], F.Copy)
-    made["uncut"] = [V([low], 1, ts, col["uncut"], p15, 15, -BOOST, A.is_lt, A.mult)]
+        kd = named["d%d" % (2 * n)] = S([kd], n, T.d0[:, n:2 * n], T.d0[:, 0:n], F.Copy)
     made["group"] = [V([low] + made["p"], 1, ts, col["group"], p15, -1, col["p"], A.mult, A.add)]
     made["twice"] = [V([low], 1, ts, col["twice"], p15, 2, None, A.mult)]
     made["bias"] = [V(made["p"], 1, ts, col["bias"], col["p"], 64, 256, A.is_ge, A.mult)]
-    uncut64 = T.col[0:64, r(names.index("uncut"), 1)]
-    x = fill(T.flip[:], 192, 1.0)
+    x = named["ones"] = fill(T.flip[:, 16:144], 64, 1.0)
+    half = named["half"] = fill(T.flip[:, 15:16], 1, 0.5)
     mark = step("q", [x], GSLOW * (170 + 2 * CYCLE * 128), lambda: g.affine_select(
-        T.flip[:, 128:256], T.flip[:, 128:256], [[-1, 128]], A.not_equal, -1.0, 0, 1), after=[k_p])
-    if "d" in "".join("".join(w) for w in OPT["sort"]):
-        k_re = V([mark], 64, ts, T.reset[:], T.flip[:, 128:256], 0.0, None, A.max)
+        T.flip[:, 16:144], T.flip[:, 16:144], [[-1, 128]], A.not_equal, -1.0, 0, 1), after=[k_p])
     k_id = V([iota(T.idv0[:], 64, [[128, 4], [1, 16]], -256, 0, after=[mark])] + made["group"], 32, ts, T.idv[:],
              T.idv0[:], col["group"], None, A.add)
     x = [iota(T.lf[:, 0:4], 4, [[128, 4]], 0, 1, False, [mark]),
-         iota(T.lf[:, 4:36], 32, [[1, 16], [0, 2]], 0, 0, False, [mark])]
-    k_lu = V(x, 36, cp, T.lu[:, 0:36], T.lf[:])
-    own_list, wide_list, mine_list, band_list, pair_list = (
-        T.lu[:, 0:4], lambda d: T.lu[:, 4 + 8 * d:12 + 8 * d], T.lu[:, 36:37], T.lu[:, 38:39], T.lu[:, 40:41])
-    two = col["twice"]
-    x, v = bits(66, 96, 5)
-    k_mine = V([x] + made["twice"], 1, ts, mine_list, v, two, two, A.add, A.add)
-    x, v = bits(68, 48, 0)
-    k_band = V([x] + made["twice"], 1, ts, band_list, v, two, 0.5, A.add, A.mult)
-    x, v = bits(70, 16, 4)
-    k_pair = V([x] + made["twice"], 1, ts, pair_list, v, two, None, A.add)
-    mw = {"1": fill(T.wi1[:], 256, -512.0)}
-    mw["2"] = S([mw["1"]], 512, T.wi2[:], T.wi1[:], F.Copy)
-    k_rr = fill(T.rr[:, 16:64], 48, 0.0)
-    k_gm = fill(T.gm2[:, 32:48], 16, 0.0)
-    ms = S([mw["1"]], 512, T.so[:], T.wi1[:], F.Copy, 0.0, 1e26)
-    mn = S([kd], 512, T.inn[64:128, :], T.d0[64:128, :], F.Copy)
+         iota(T.lf[:, 4:36], 32, [[2, 16], [0, 2]], 1, 0, False, [mark]),
+         V([k_p], 1, ts, T.lf[:, 36:37], T.de[:, 0:1], 31, None, A.bitwise_and, kind="plain")]
+    k_re = step("q", [mark], GSLOW * (170 + 2 * CYCLE * 128), lambda: g.affine_select(
+        T.reset[:], T.flip[:, 16:144], [[-1, 128]], A.not_equal, 0.0, 0, 1), after=x[:2])
+    k_lu = V(x, 37, cp, T.lu[:, 0:37], T.lf[:, 0:37])
+    named["b_quad"] = x[2]
+    quad_list, mine_list, pair_list = (T.lu[:, n:n + 1] for n in (36, 38, 40))
+    made["eight"] = [V([low], 1, ts, col["eight"], p15, 8, 1, A.mult, A.add)]
+    x, v = bits(66, 96, 4)
+    k_mine = V([x] + made["eight"], 1, ts, mine_list, v, col["eight"], None, A.add)
+    z, v = bits(70, 16, 4)
+    k_pair = V([z] + made["twice"], 1, ts, pair_list, v, col["twice"], None, A.add)
+    named.update({"k_" + n: made[n][0] for n in made})
+    named.update(k_mine=k_mine, k_pair=k_pair, b_mine=x, b_pair=z, k_lu=k_lu, k_id=k_id, k_low=low, k_re=k_re)
+    mw = {"1": fill(T.wi1[:], 256, -256.0)}
+    named["m1"] = mw["1"]
+    ms = S([mw["1"]], 512, T.so[:], T.wi1[:], F.Copy, 0.0, -1e26)
+    k_et = [V([mw["1"]], 72, ts, T.et[0:32, 144:288], T.wi1[0:32, 0:144], 2.0, None, A.mult),
+            V([mw["1"]], 72, ts, T.et[32:64, 144:288], T.wi1[32:64, 0:144], 0.0, None, A.mult)]
+    k_et.append(V(k_et[:1], 1, ts, T.et[0:32, 146:153:2], T.wi1[0:32, 0:4], -3.0, None, A.mult))
+    named.update(k_et=k_et[0], k_etb=k_et[1], k_etc=k_et[2])
+    k_eq = iota(T.eq[:, 15:432:144], 3, [[0, 3]], 0, 0, after=[mark])
+    k_cb = iota(T.cb[:, PART - 1:4 * PART:PART], 4, [[0, 4]], 64, 0, after=[k_re])
+    k_rr = iota(T.rr[:, 24:128], 104, [[0, 104]], 0, 0, after=[k_cb])
+    k_sg = iota(T.sg2[:, PART2 - 1:4 * PART2:PART2], 4, [[0, 4]], 0, -1, after=[k_rr])
+    mi = iota(T.iw[:], 512, [[1, 4], [0, 128]], 0, 0, after=[k_sg])
+    mw["2"] = named["m2"] = S([kd], 512, T.wi2[:], T.d0[:], F.Identity, -256.0, 0.0)
+    mn = named["mn"] = S([kd], 512, T.inn[64:128, :], T.d0[64:128, :], F.Copy)
 
     qu = quantize([m0, du], 128, T.uq[:], T.us[:], T.ut[:])
     ub = pick("v", [qu, mz], 128, T.ubq[:, 0:128].bitcast(U32), T.uq[:, 0:128].bitcast(U32).indirect(T.zoff[:, 0:8]))
     ubs = pick("a", [qu, mz], 128, T.ubs[:, 0:128], T.us[:, 0:128].indirect(T.zoff[:, 0:8]))
     qw = [quantize([dw], 128, T.wq[:, r(k)], T.ws[:, r(k)], T.wt[:, r(k, 512)]) for k in range(4)]
 
-    stages = OPT["loads"]
     pv, vcol, rows, kept, twin = {}, {}, [], [], {}
-    for j, (a, b) in enumerate(stages):
-        n, at = 128 * (b - a), slice(128 * a, 128 * b)
-        qx = quantize([dx[j]], n, T.xq[:, at], T.xs[:, at], T.xt[:, 512 * a:512 * b])
-        for c in range(a, b):
-            pv[c] = P([qx, qu], 128, bank(4 + c), T.xq[:, r(c)], T.xs[:, r(c)], T.uq[:], T.us[:])
-        rows.append(P([qx, ub, ubs], n, bank(j, n), T.ubq[:], T.ubs[:], T.xq[:, at], T.xs[:, at]))
-        x = V([pv[c] for c in range(a, b)], 2, cp, T.vc[:, a:b], T.ps[:, 512 * (4 + a):512 * (4 + b):512])
-        vcol.update({c: x for c in range(a, b)})
-        kept.append(S([rows[j]], n, T.ss[:, at], bank(j, n), F.Copy))
-        named.update({"qx%d" % j: qx, "row%d" % j: rows[j], "keep%d" % j: kept[j], "col%d" % j: x})
-        if j in OPT["twin"]:
-            free = len(stages) if len(stages) < 4 else 4
-            twin[j] = P([rows[j]] + [vcol[0]] * (free == 4), n, bank(free, n), T.ubq[:], T.ubs[:], T.xq[:, at],
-                        T.xs[:, at]), free
+    for c in range(4):
+        qx = quantize([dx[c]], 128, T.xq[:, r(c)], T.xs[:, r(c)], T.xt[:, r(c, 512)])
+        mine = T.xq[:, r(c)], T.xs[:, r(c)]
+        if c < 3:
+            pv[c] = P([qx, qu], 128, bank(4 + c), *mine, T.uq[:], T.us[:])
+            if OPT["col"][c] == "v":
+                vcol[c] = V([pv[c]], 1, cp, T.vc[:, c:c + 1], bank(4 + c, 1))
+            else:
+                vcol[c] = S([pv[c]], 1, T.vc[:, c:c + 1], bank(4 + c, 1), F.Copy)
+            named["col%d" % c] = vcol[c]
+        else:
+            pv[c] = P([qx, ub, ubs], 128, bank(4 + c), *mine, T.ubq[:], T.ubs[:])
+        rows.append(P([qx, ub, ubs], 128, bank(c), T.ubq[:], T.ubs[:], *mine))
+        rows[c]["after"].append(pv[c])
+        kept.append(S([rows[c]], 128, T.ss[:, r(c)], bank(c), F.Copy))
+        named["keep%d" % c] = kept[c]
+        named.update({"qx%d" % c: qx, "row%d" % c: rows[c], "pv%d" % c: pv[c]})
+        if c in OPT["twin"]:
+            twin[c] = P([qx, ub, ubs, vcol[3 - c]], 128, bank(7 - c), T.ubq[:], T.ubs[:], *mine)
+            twin[c]["after"].append(rows[c])
+
+    def ahead(c, lo, hi, way, at):
+        n, up = 128 * (hi - lo), lo > c
+        out = T.cb[:, at:at + n]
+        if way == "s":
+            signs = T.sgb[:, r(4 * c + lo)]
+            y = S([rows[lo], vcol[c]], n, signs, bank(lo), F.Sign, T.vc[:, c:c + 1], -1.0)
+            named["s%d%d" % (c, lo)] = y
+            return V([y], n / 2, ts, out, signs, 0.0, None, A.is_lt if up else A.is_le)
+        dep, src = (kept[lo:hi], T.ss[:, 128 * lo:128 * hi]) if way in "kK" else ([twin[lo]], bank(7 - lo))
+        has, v = (vcol[c], T.vc[:, c:c + 1]) if way in "kt" else (pv[c], bank(4 + c, 1))
+        y = V(dep + [has], n, ts, out, src, v, None, A.is_gt if up else A.is_ge)
+        if way in "KT" and 3 - c in twin:
+            twin[3 - c]["deps"].append(y)
+        return y
+
+    def total(deps, out, c, src, stop, n, first):
+        h = n // 2
+        return V(deps, h / 2, scan, out[:, 4 * (HALF - h) + c:4 * HALF:4], src[:, stop - n:stop - h],
+                 src[:, stop - h:stop], first, A.add, A.add)
+
     pz = []
     for c in range(4):
-        parts, fill_to = [], 512 * c
-        for j, (a, b) in enumerate(stages):
-            way = OPT["sort"][c][j]
-            runs = [(a, b)]
-            if a <= c < b:
-                lo, hi = {"i": (a, b), "o": (c, c + 1), "d": (c + 1, c + 1)}[way[0]]
-                n, m = 128 * (hi - lo), 128 * (1 + lo - c)
-                if way[0] == "d":
-                    x = V([twin[j][0], pv[c]], 128, ts, T.eq[:, 256 * c:256 * c + 128],
-                          bank(twin[j][1], 128, 128 * (c - a)), bank(4 + c, 1), 2.0, A.is_equal, A.mult)
-                    own = V([x, k_re], 64, scan, T.ow[:, 256 * c:256 * c + 128], T.reset[:],
-                            T.eq[:, 256 * c:256 * c + 128], 0.0, A.mult, A.subtract)
-                    n = 128
-                else:
-                    x = S([rows[j], vcol[c]], n + 24, T.sg[:, 256 * c:256 * c + n], bank(j, n, 128 * (lo - a)), F.Sign,
-                          T.vc[:, c:c + 1], -1.0, accum_out=T.acc[:, c:c + 1])
-                    named["sign%d" % c] = x
-                    x = V([x], n / 2, ts, T.eq[:, 256 * c:256 * c + n], T.sg[:, 256 * c:256 * c + n], 0.0, None,
-                          A.is_equal)
-                    own = V([x, mark], n / 2, scan, T.ow[:, 256 * c:256 * c + n], T.flip[:, m:m + n],
-                            T.eq[:, 256 * c:256 * c + n], T.acc[:, c:c + 1], A.mult, A.subtract)
-                result, first = T.ow[:, 256 * c + n - 1:256 * c + n], float(128 * (hi - lo))
-                runs, way = [(a, lo), (hi, b)], way[1:]
-            for lo, hi in runs:
-                n = 128 * (hi - lo)
-                if n == 0:
-                    continue
-                out, up = T.cb[:, fill_to:fill_to + n], lo > c
-                if way == "s":
-                    y = S([rows[j], vcol[c]], n, T.sgb[:, fill_to:fill_to + n], bank(j, n, 128 * (lo - a)), F.Sign,
-                          T.vc[:, c:c + 1], -1.0)
-                    y = V([y], n / 2, ts, out, T.sgb[:, fill_to:fill_to + n], 0.0, 2.0, A.is_lt if up else A.is_le,
-                          A.mult)
-                else:
-                    dep, src = ((kept[j], T.ss[:, 128 * lo:128 * hi]) if way in "kK" else
-                                (twin[j][0], bank(twin[j][1], n, 128 * (lo - a))))
-                    has, v = (vcol[c], T.vc[:, c:c + 1]) if way in "kt" else (pv[c], bank(4 + c, 1))
-                    y = V([dep, has], n, ts, out, src, v, 2.0, A.is_gt if up else A.is_ge, A.mult)
-                parts.append(y)
-                fill_to += n
-        n = (fill_to - 512 * c) // 2
-        x = V(parts, n / 2, scan, T.z1[:, 256 * c:256 * c + n], T.cb[:, 512 * c:512 * c + n],
-              T.cb[:, 512 * c + n:512 * c + 2 * n], first, A.add, A.add)
-        pz.append(V([x, own], 1, ts, T.pz1[:, c:c + 1], T.z1[:, 256 * c + n - 1:256 * c + n], result, 0.5,
-                    A.add, A.mult))
-    sl = pick("a", [k_lu] + kept, 64, T.sl[:], T.ss[:, 0:512].indirect(own_list))
+        ways = OPT["count"][c]
+        n = 128 * sum(hi - lo for lo, hi, way in ways if way != "c")
+        at, e = PART * (c + 1) - 1 - n, 144 * c + 16
+        if c < 3:
+            x = S([rows[c], vcol[c]], 128 + 24, T.sg[:, r(c)], bank(c), F.Sign, T.vc[:, c:c + 1], -1.0,
+                  accum_out=T.acc[:, c:c + 1])
+            named["sign%d" % c] = x
+            x = V([x], 64, ts, T.eq[:, e:e + 128], T.sg[:, r(c)], 0.0, 0.5, A.is_equal, A.mult)
+            own = V([x, mark, half, k_eq], 65, scan, T.cb[:, at - 129:at], T.flip[:, 15:144], T.eq[:, e - 1:e + 128],
+                    T.acc[:, c:c + 1], A.mult, A.subtract)
+            first = 0.0
+        else:
+            x = V([twin[c], pv[c]], 128, ts, T.eq[:, e:e + 128], bank(7 - c), bank(4 + c, 1), None, A.is_equal)
+            own = V([x, k_re], 64, scan, T.cb[:, at - 128:at], T.reset[:], T.eq[:, e:e + 128], 0.0, A.mult, A.subtract)
+            first = -64.0
+        parts = [own, k_cb]
+        named.update({"eq%d" % c: x, "own%d" % c: own})
+        for lo, hi, way in ways:
+            if way != "c":
+                parts.append(ahead(c, lo, hi, way, at))
+                named["e%d%d" % (c, lo)] = parts[-1]
+                at += 128 * (hi - lo)
+        los = [lo for lo, hi, way in ways if way == "c"]
+        if los:
+            x = [S([rows[lo], vcol[c]], 128, T.sgc[:, r(3 * c + i)], bank(lo), F.Sign, T.vc[:, c:c + 1], -1.0)
+                 for i, lo in enumerate(los)]
+            named.update({"s%d%d" % (c, lo): y for lo, y in zip(los, x)})
+            first, signs = T.acc[:, 4 + c:5 + c], T.sgc[:, 384 * c:384 * c + 128 * len(los)]
+            parts.append(S(x, 128 * len(los) + 24, signs, signs, F.Relu, 0.0, -1.0, accum_out=first))
+            named["sum%d" % c] = parts[-1]
+        pz.append(total(parts, T.z1, c, T.cb, PART * (c + 1), n + 2, first))
+        named["z%d" % c] = pz[c]
+    places = [T["z" + k][:, 4 * HALF - 4:4 * HALF] for k in "12"]
+    if OPT["sl3"] == "k":
+        sl = [pick("a", [k_lu] + kept, 64, T.sl[:], T.ss[:, 0:512].indirect(T.lu[:, 0:4]))]
+    else:
+        t3 = V([pv[3]], 32, vec.transpose, T.t3[:], bank(7, 32))
+        sl = [pick("a", [k_lu] + kept[:3], 48, T.sl[:, 0:48], T.ss[:, 0:384].indirect(T.lu[:, 0:3])),
+              pick(OPT["sl3"], [k_lu, t3], 16, T.sl[:, 48:64], T.t3[:, 0:32].indirect(quad_list))]
+        named.update(t3=t3, sl3=sl[1])
+    named["sl"] = sl[0]
 
-    def quadrants(deps, mid, out, w, src, many):
-        y = V(deps, 2 * w, tt, mid[0:64, 0:w], src[0:64, 0:w], src[64:128, 0:w], A.max, kind="across")
-        return [V([y], 2 * w, tt, out[32 * a:32 * a + 32, 0:w], mid[0:32, 0:w], mid[32:64, 0:w], A.max, kind="across")
-                for a in range(many)]
+    def make_list(deps, k, places, free):
+        wi, wx, ez, lw = (T[n + k] for n in ("wi", "wx", "ez", "lw"))
+        put = by_list(deps + [k_id, mw[k]], PUT * 64, cp, wi[:, 0:512].indirect(places), T.idv[:])
+        diag = V([put, kd], 256, scan, wx[:], wi[:], T.d0[:], -2048.0, A.max, A.add)
+        turn = [V([diag] + free, 16, vec.transpose, T.et[0:64, at + 2 * h:at + 2 * h + 288:9], wx[r(h, 64), 15:512:16])
+                for at in (145, 5) for h in range(2)]
+        join = [V(turn, 72, scan, ez[0:32, r(h, 144)], T.et[0:32, 144:288], T.et[32:64, 144:288], 0.0, A.add, A.max,
+                  kind="across") for h in range(2)]
+        back = [V(join, 16, vec.transpose, lw[r(a, 32), :], ez[0:32, 8:288:9]) for a in range(4)]
+        named.update({"put" + k: put, "diag" + k: diag, "join" + k: join[0], "joinb" + k: join[1]})
+        named.update({n + k + "abcd"[a]: x[a] for n, x in (("turn", turn), ("back", back)) for a in range(4)})
+        return back, join
 
-    def make_list(deps, k, many):
-        wi, wx, et, eh, eb, gm = (T[n + k] for n in ("wi", "wx", "et", "eh", "eb", "gm"))
-        put = by_list(deps + [k_id, mw[k]], PUT * 64, cp, wi[:, 0:512].indirect(T["pz" + k][:, 0:4]), T.idv[:])
-        diag = V([put, kd], 256, scan, wx[:], T.d0[:], wi[:], 0.0, A.add, A.max)
-        turn = V([diag], 16, vec.transpose, et[:], wx[:, 15:512:16])
-        x = [V([turn], 32, tt, eh[:, r(h, 16)], et[:, 0:16], et[:, 16:32], A.max) for h in range(2)]
-        back = V(x, 16, vec.transpose, eb[:], eh[:])
-        named.update({"put" + k: put, "diag" + k: diag, "turn" + k: turn, "max" + k: x[0], "maxb" + k: x[1],
-                      "back" + k: back})
-        x = quadrants([back], T["ge" + k], gm, 32, eb, many)
-        if many == 4:
-            return x, [V(x + made["uncut"], 32, ts, T["lw" + k][:], gm[:, 0:32], col["uncut"], 256, A.add, A.add)]
-        return ([S(x, 32, gm[64:128, 0:32], gm[0:64, 0:32], F.Copy)],
-                [V(x + made["uncut"], 32, ts, T["lw" + k][r(h, 64), :], gm[0:64, 0:32], uncut64, 256, A.add, A.add)
-                 for h in range(2)])
-
-    so = by_list(pz + [sl, ms], PUT * 64, cp, T.so[:, 0:512].indirect(T.pz1[:, 0:4]), T.sl[:])
+    so = by_list(pz + sl + [ms], PUT * 64, cp, T.so[:, 0:512].indirect(places[0]), T.sl[:])
     tr = [V([so], 128 * n, vec.transpose, T.tr[:, 128 * i:128 * (i + n)], T.so[:, 128 * d:128 * (d + n)])
           for i, d, n in spans]
-    v16 = V(tr, 24, tt, T.v16[:, 0:12], T.tr[:, 0:384:32], T.tr[:, 16:384:32], A.max)
-    out_s, in_s = send([v16], [(d, T.v16[:, r(i, 4)], T.rs[:, r(rank, 4)]) for i, d in enumerate(others)], "rem_s",
-                       FIRST, HOP)
-    tro = V([so], 128, vec.transpose, T.tr[:, 384:512], T.so[:, r(rank)])
-    rso = V([tro], 8, tt, T.rs[:, r(rank, 4)], T.tr[:, 384:512:32], T.tr[:, 400:512:32], A.max)
-    named.update(so=so, tr=tr[0], trb=tr[-1], v16=v16, tro=tro, rso=rso, sl=sl, ub=ub)
+    low = [V(tr, 24, scan, T.pa[to:to + n, :], T.tr[a:a + n, 0:384:16], T.tr[a + 64:a + 64 + n, 0:384:16], 1e29,
+             A.min, A.min, kind="across") for to, a, n in ((0, 0, 64), (64, 32, 32), (96, 0, 32))]
+    out_s, in_s = send(low, [(d, T.pa[:, r(i, 8)], T.rs[:, r(rank - (rank > d), 8)]) for i, d in enumerate(others)],
+                       "rem_s", FIRST, HOP)
+    named.update(so=so, trb=tr[-1], tr=tr[0], ub=ub, qu=qu, ubs=ubs, ms=ms, out_s=out_s)
+    named.update({"low%d" % k: x for k, x in enumerate(low)})
     named.update({"qw%d" % k: qw[k] for k in range(4)})
-    gm, lw = make_list(pz + [ms, mw["2"]], "1", OPT["many"][0])
+    lw, free = make_list(pz + [ms] + k_et, "1", places[0], k_et)
 
-    pq, pp = [], []
-    for i, d, n in spans if OPT["picks"] else [(i, d, 1) for i, d in enumerate(others)]:
-        of, at = T.lw1[:, 8 * d:8 * (d + n)], slice(128 * i, 128 * (i + n))
-        pq.append(pick("v", lw, 128 * n, T.sq[:, at].bitcast(U32), T.xq[:, 0:512].bitcast(U32).indirect(of)))
-        pp.append(pick("a", lw, 128 * n, T.sp[:, at], T.xs[:, 0:512].indirect(of)))
-    nb = S(gm + [k_pair] + made["uncut"], PICK * 16, T.nb[:], T.gm1[:, 0:32].indirect(pair_list), F.Identity,
-           col["uncut"], fixed=65)
+    pq, pp, in_c, in_p, sent = {}, {}, [], [], [out_s]
+    for n, ds, at in (("f", far, 0), ("n", near, 128 * len(far))):
+        of, at = T.lw1[:, 8 * ds[0]:8 * ds[-1] + 8], slice(at, at + 128 * len(ds))
+        w = 128 * len(ds)
+        pq[n] = pick("v", lw, w, T.sq[:, at].bitcast(U32), T.xq[:, 0:512].bitcast(U32).indirect(of))
+        pp[n] = pick("a", lw, w, T.sp[:, at], T.xs[:, 0:512].indirect(of))
+        named.update({"pq" + n: pq[n], "pp" + n: pp[n]})
+    gm = V(lw, 32, ts, T.gm[:], T.lw1[:], -256, None, A.add)
+    nb = pick("a", [gm, k_pair], 16, T.nb[:], T.gm[:, 0:32].indirect(pair_list))
     out_i, in_i = send([nb], [(d, T.nb[:, r(d, 4)], T.rn[:, r(rank, 4)]) for d in others], "rem_i", 200, HOP,
                        after=[out_s])
-    out_c, in_c = send(pq, [(d, T.sq[:, r(i)].bitcast(U8), T.lq[:, r(rank)].bitcast(U8)) for i, d in enumerate(others)],
-                       "rem_c", 200, 2 * HOP, after=[out_s])
-    out_p, in_p = send(pp, [(d, T.sp[:, r(i)], T.lp[:, r(rank)]) for i, d in enumerate(others)], "rem_p", 200,
-                       2.5 * HOP, after=[out_c])
-    mi = iota(T.iw[0:64, :], 512, [[1, 4], [0, 128]], 0, 0, after=[out_c, out_p, out_i])
-    named.update(out_i=out_i, out_c=out_c, out_p=out_p, nb=nb, lw=lw[0], lwb=lw[-1], gm1=gm[0])
-    named.update({"pq%d" % i: x for i, x in enumerate(pq)})
-    named.update({"pp%d" % i: x for i, x in enumerate(pp)})
+    for ns, hops in ((("f", 2), ("n", 1)) if OPT["split"] else (("fn", 2),)):
+        ds = [(i, d) for i, d in enumerate(far + near) if "fn"[d in near] in ns]
+        a, b = send([pq[n] for n in ns], [(d, T.sq[:, r(i)].bitcast(U8), T.lq[:, r(rank)].bitcast(U8)) for i, d in ds],
+                    "rem_c", 200, hops * HOP, after=sent[-1:])
+        c, e = send([pp[n] for n in ns], [(d, T.sp[:, r(i)], T.lp[:, r(rank)]) for i, d in ds], "rem_p", 200,
+                    (hops + 0.5) * HOP, after=[a])
+        in_c, in_p, sent = in_c + [b], in_p + [e], sent + [a, c]
+        named.update({"out_c" + ns[0]: a, "out_p" + ns[0]: c})
+    named.update(out_i=out_i, nb=nb, gm=gm)
 
     of = T.lw1[:, r(rank, 8)]
     have = {rank: pick("a", lw + kept, 128, T.sb[:, r(rank)], T.ss[:, 0:512].indirect(of))}
+    bo = V([have[rank]], 128, vec.transpose, T.bo[:], T.sb[:, r(rank)])
+    named.update(go=have[rank], to=bo)
+    vo = pick(OPT["vo"], [bo, k_lu], 16, T.vo[:], T.bo[:, 0:128].indirect(T.lu[:, 0:1]))
     oq = pick("v", lw, 128, T.lq[:, r(rank)].bitcast(U32), T.xq[:, 0:512].bitcast(U32).indirect(of))
     ow = pick("a", lw, 128, T.lp[:, r(rank)], T.xs[:, 0:512].indirect(of))
     nbo = S([nb], 4, T.rn[:, r(rank, 4)], T.nb[:, r(rank, 4)], F.Copy)
 
-    rr = quadrants([in_s, rso], T.r1, T.rr, 16, T.rs, 4)
-    v1 = pick(OPT["v1"], rr + [k_mine, k_rr], 16, T.v1[:], T.rr[:, 0:64].indirect(mine_list))
+    rr, whole = [V([in_s], 48, tt, T.rr[r(h, 64), 0:24], T.rs[0:64, :], T.rs[64:128, :], A.min, kind="across")
+                 for h in range(2)], T.rr
+    named["l2a"] = rr[0]
+    v1 = pick(OPT["v1"], rr + [k_mine, k_rr], 16, T.v1[:], whole[:, 0:128].indirect(mine_list))
+    role = dict(zip(far + near + [rank], "abno"))
     for i, d in enumerate(others):
-        x = pick(OPT["gather"][i], rr + [k_lu], 128, T.bx[:, r(i)], T.rr[:, 0:16].indirect(wide_list(d)))
+        x = pick(OPT["gather"]["abn".index(role[d])], rr + [k_lu], 128, T.bx[:, r(i)],
+                 whole[:, 0:24].indirect(T.lu[:, 4 + 8 * i:12 + 8 * i]))
         have[d] = V([x], 128, vec.transpose, T.sb[:, r(d)], T.bx[:, r(i)])
-        named.update({"g%d" % i: x, "t%d" % i: have[d]})
-    named.update(oq=oq, ow=ow, sbo=have[rank], nbo=nbo, l2=rr[3], v1=v1)
+        named.update({"g" + role[d]: x, "t" + role[d]: have[d]})
+    named.update(oq=oq, ow=ow, nbo=nbo, l2=rr[-1], v1=v1, vo=vo)
 
-    fin, pz2 = {}, []
+    who = {n: d for d, n in role.items()}
+    ways = OPT["merge"][rank] if len(OPT["merge"]) == N else OPT["merge"][0]
+    ways = {(who[w[0]], who[w[1]]): w[2] for w in ways.split()}
+    pz2 = []
     for s in range(N):
-        way, done, mine = OPT["ways"][s], [], T.v1[:, s:s + 1]
-        parts = [(0, s)] * (s > 0) + [(s + 1, N - 1 - s)] * (s < N - 1)
-        if way == "v" and OPT.get("fine"):
-            parts = [(d, 1) for d in range(N) if d != s]
-        for d, n in parts:
-            at = slice(384 * s + 128 * (d - (d > s)), 384 * s + 128 * (d - (d > s) + n))
-            deps, src = [v1] + [have[e] for e in range(d, d + n)], T.sb[:, 128 * d:128 * (d + n)]
-            if way == "v":
-                x = V(deps, 128 * n, ts, T.c2[:, at], src, mine, 0.5, A.is_ge if d < s else A.is_gt, A.subtract)
+        has, mine = (vo, T.vo[:, 0:1]) if s == rank else (v1, T.v1[:, r(others.index(s), 1)])
+        ds = [d for d in range(s + 1, N) if ways.get((s, d)) == "c"]
+        here = [d for d in range(N) if d != s and d not in ds]
+        parts, first, end = list(made["p"]), col["p"], PART2 * (s + 1) - 1
+        if ds:
+            at = end - 128 * len(ds)
+            x = [S([has, have[d]], 128, T.sg2[:, at + 128 * i:at + 128 * i + 128], T.sb[:, r(d)], F.Sign, mine, -1.0)
+                 for i, d in enumerate(ds)]
+            named.update({"s" + role[s] + role[d]: y for d, y in zip(ds, x)})
+            first, signs = T.acc2[:, s:s + 1], T.sg2[:, at:end + 1]
+            parts.append(S(x + [k_sg], 128 * len(ds) + 24, signs, signs, F.Relu, 0.0, -1.0, accum_out=first))
+            named["r" + role[s]] = parts[-1]
+        for i, d in enumerate(here):
+            out = T.c2[:, r(3 * s + i)]
+            if (s, d) in ways:
+                signs = T.sg2[:, PART2 * s + 128 * i:PART2 * s + 128 * i + 128]
+                x = named["s" + role[s] + role[d]] = S([has, have[d]], 128, signs, T.sb[:, r(d)], F.Sign, mine, -1.0)
+                x = V([x], 64, ts, out, signs, 0.0, None, A.is_le if d < s else A.is_lt)
             else:
-                x = S(deps, 128 * n, T.sg2[:, at], src, F.Sign, mine, -1.0)
-            if way == "s":
-                x = V([x], 64 * n, ts, T.c2[:, at], T.sg2[:, at], 0.0, 0.5, A.is_le if d < s else A.is_lt, A.subtract)
-            if way == "c":
-                k = 1.0 if s else -1.0
-                x = S([x], 128 * n + 24, T.c2[:, at], T.sg2[:, at], F.Relu, 0.0, k, accum_out=T.acc2[:, s:s + 1])
-                named["relu"] = x
-                base = "top" if s else "p"
-                pz2.append(V([x] + made[base], 1, ts, T.pz2[:, s:s + 1], T.acc2[:, s:s + 1], -k, col[base],
-                             A.mult, A.add))
-            done.append(x)
-        if way != "c":
-            fin[s] = V(done + made["mid"], 96, scan, T.z2[:, r(s, 192)], T.c2[:, 384 * s:384 * s + 192],
-                       T.c2[:, 384 * s + 192:384 * s + 384], col["mid"], A.add, A.add)
-    a, b = min(fin), max(fin) + 1
-    pz2.append(V(list(fin.values()), 4, ts, T.pz2[:, a:b], T.z2[:, 192 * a + 191:192 * b:192], 256, None, A.add))
-    gm, lm = make_list(pz2, "2", OPT["many"][1])
+                x = V([has, have[d]], 128, ts, out, T.sb[:, r(d)], mine, None, A.is_ge if d < s else A.is_gt)
+            named["c" + role[s] + role[d]] = x
+            parts.append(x)
+        n = 128 * len(here)
+        if here:
+            pz2.append(total(parts, T.z2, s, T.c2, 384 * s + n, n, first))
+        else:
+            pz2.append(V(parts, 1, cp, T.z2[:, 4 * HALF - 4 + s:4 * HALF - 3 + s], first))
+        named["z" + role[s]] = pz2[s]
+    x = [named["c" + role[s] + "o"] for s in others if (s, rank) not in ways]
+    named.update(zip(("early", "earlyb"), x))
+    lm, _ = make_list(pz2, "2", places[1], free)
 
-    ic = [S([in_i, nbo, mn], 16, T.inn[64:128, h:512:32], T.rn[64:128, :], F.Copy) for h in (0, 16)]
-    iw = V(ic, 256, vec.transpose, T.iw[64:128, :], T.inn[64:128, :])
-    ql = by_list(gm + [k_band, k_gm], PICK * 16, ts, T.q2[:], T.gm2[:, 0:48].indirect(band_list), col["uncut"], 256,
-                 A.add, A.add)
-    ig = S([ql, iw, mi] + made["bias"], PICK * 128, T.gid[:], T.iw[:, 0:512].indirect(T.q2[:, 0:8]), F.Identity,
+    ic = S([in_i, nbo, mn], 16, T.inn[64:128, 0:512:32], T.rn[64:128, :], F.Copy)
+    iw = [V([ic, mi], 128, vec.transpose, T.iw[64:128, r(h, 256)], T.inn[64:128, r(h, 256)]) for h in range(2)]
+    ig = S(lm + iw + [mi] + made["bias"], PICK * 512, T.gid[:], T.iw[:, 0:512].indirect(T.lw2[:, 0:32]), F.Identity,
            col["bias"], fixed=65)
-    dma("a", [ig], LOAD, T.ids[:, :], T.gid[0:128:16, :], "dst")
-    named.update(iw=iw, ql=ql, ig=ig, ic=ic[0], icb=ic[1], lm=lm[0], lmb=lm[-1], pz2=pz2[-1], gm2=gm[0])
+    dma("a", [ig], LOAD, T.ids[:, :], T.gid[0:128:64, :], "dst")
+    named.update(iw=iw[0], iwb=iw[1], ig=ig, ic=ic)
 
     for k, n in OPT["bands"]:
         of, at = T.lw2[:, 8 * k:8 * (k + n)], slice(128 * k, 128 * (k + n))
-        a = pick("v", lm + [oq, in_c], 128 * n, T.fq[:, at].bitcast(U32), T.lq[:, 0:512].bitcast(U32).indirect(of))
-        b = pick("a", lm + [ow, in_p], 128 * n, T.fp[:, at], T.lp[:, 0:512].indirect(of))
+        a = pick("v", lm + [oq] + in_c, 128 * n, T.fq[:, at].bitcast(U32), T.lq[:, 0:512].bitcast(U32).indirect(of))
+        b = pick("a", lm + [ow] + in_p, 128 * n, T.fp[:, at], T.lp[:, 0:512].indirect(of))
         named.update({"a%d" % k: a, "b%d" % k: b})
         for j in range(k, k + n):
             x = P([a, b, qw[j]], 128, bank(j), T.wq[:, r(j)], T.ws[:, r(j)], T.fq[:, r(j)], T.fp[:, r(j)])
@@ -426,10 +487,12 @@ def rank_program(g, core, T, topo):
             dma(OPT["st"][j], [x], LOAD + 200, T.y[:, r(j)], T.ysb[:, r(j)], "dst")
 
     for rule in OPT["order"]:
-        rule = [named[n] for n in rule.split()]
+        rule = [named[n] for n in rule.split() if n in named]
         for a, b in zip(rule, rule[1:]):
             if a is not b:
                 b["after"].append(a)
+    for n, s in named.items():
+        s["name"] = n
     _arrange(steps)
     order = {q: sorted((s for s in steps if s["q"] == q), key=lambda s: s["at"]) for q in queues}
     for q in queues:

@@ -19,47 +19,56 @@ SCRATCH = {
     "zoff": _sb(8, "uint16"), "flip": _sb(144, "bfloat16"), "reset": _sb(128, "bfloat16"),
     "de": _sb(66, "int32"), "de2": _sb(72, "int32"),
     "da": _sb(64, "bfloat16"), "db": _sb(64, "bfloat16"), "d0": _sb(512, "bfloat16"),
-    "col": _sb(16, "float32"), "lf": _sb(38, "int32"), "lu": _sb(44, "uint16"),
+    "col": _sb(16, "float32"), "lf": _sb(12, "int32"), "lu": _sb(16, "uint16"),
     "idv0": _sb(64, "bfloat16"), "idv": _sb(64, "bfloat16"),
     "ss": _sb(512, "float32"), "vc": _sb(4, "float32"), "sg": _sb(512, "bfloat16"), "sgb": _sb(2048, "bfloat16"),
     "acc": _sb(8, "float32"), "eq": _sb(576, "bfloat16"), "sgc": _sb(1152, "bfloat16"),
     "cb": _sb(4 * PART, "bfloat16"), "t3": _sb(32, "float32"),
     "sl": _sb(64, "float32"), "so": _sb(512, "float32"), "tr": _sb(384, "float32"),
-    "pa": _sb(24, "float32"), "gm": _sb(32, "float32"), "nb": _sb(16, "float32"), "et": _sb(436, "float16"),
-    "rs": _sb(24, "float32"), "rr": _sb(128, "float32"), "bx": _sb(384, "float32"), "bo": _sb(128, "float32"),
+    "pa": _sb(24, "float32"), "gm": _sb(128, "float32"), "nb": _sb(16, "float32"), "et": _sb(436, "float16"),
+    "pb": _sb(8, "float32"), "rq": _sb(128, "float32"), "vn": _sb(16, "float32"),
+    "rs": _sb(16, "float32"), "rr": _sb(128, "float32"), "bx": _sb(384, "float32"), "bo": _sb(128, "float32"),
     "sb": _sb(512, "float32"), "v1": _sb(16, "float32"), "vo": _sb(16, "float32"),
     "sg2": _sb(4 * PART2, "bfloat16"), "c2": _sb(1536, "bfloat16"),
-    "acc2": _sb(4, "float32"), "rn": _sb(16, "float32"),
-    "inn": _sb(512, "bfloat16"), "iw": _sb(512, "bfloat16"), "gid": _sb(512, "float32"),
+    "acc2": _sb(4, "float32"), "rn": _sb(4, "float32"),
+    "iw": _sb(512, "float32"), "gid": _sb(512, "float32"),
     "ysb": _sb(512, "float32"),
     "ps": ("psum", [128, 4096], "float32"),
 }
 for _k in ("1", "2"):
     SCRATCH.update({"z" + _k: _sb(4 * HALF, "uint16"), "wi" + _k: _sb(512, "bfloat16"), "wx" + _k: _sb(512, "float16"),
                     "ez" + _k: _sb(288, "uint16"), "lw" + _k: _sb(32, "uint16")})
-SEMAPHORES = ["v", "a", "t", "q", "du", "dx0", "dx1", "dx2", "dx3", "dw", "dst",
-              "rem_s", "rem_c", "rem_p", "rem_i", "loc"]
+SEMAPHORES = ["v", "a", "t", "q", "du", "dx0", "dx1", "dx2", "dx3", "dw0", "dw1", "dn", "dst",
+              "rem_s", "rem_n", "rem_c", "rem_p", "rem_i", "loc"]
 
 WAIT = 215
 CYCLE, CALL, ACT, SLOW, GSLOW = 0.83, 0, 65, 1.0, 1.0
 ROUNDS = 0
+LONG = 1e9
 SLACK = 0
-LOAD, RATE, FIRST, HOP = 1000, 500, 1000, 1300
+LOAD, RATE, FIRST, HOP, NEAR = 1000, 500, 1000, 1300, 250
 OPT = {"loads": ((0, 1), (1, 2), (2, 3), (3, 4)), "twin": (2, 3),
        "count": (((1, 2, "k"), (2, 3, "t"), (3, 4, "c")), ((0, 1, "K"), (2, 3, "t"), (3, 4, "c")),
                  ((0, 2, "K"), (3, 4, "t")), ((0, 3, "K"), (3, 4, "T"))), "col": "vvv",
-       "few": 4, "merge": ("aos nbc nac", "noc nac nbc", "aoc boc abc", "aoc boc noc"), "ycopy": "vvvv", "vo": "a", "sl3": "a", "split": 1,
-       "gather": "vaa", "v1": "v", "bands": ((0, 1), (1, 1), (2, 1), (3, 1)), "st": "yyyy",
+       "signs": 3, "few": 4, "puts": (1, 1), "merge": ("aos abc oac", "noc nac oac", "aoc abc bnc", "aoc abc bnc"), "ycopy": "vvvv", "vo": "a", "sl3": "k", "split": 1,
+       "gather": "vaa", "v1": "va", "bands": ((0, 1), (1, 1), (2, 1), (3, 1)), "stores": (1, 1, 1, 1),
+       "ranks": (("ga cbo tb ta cno cnb tn cba cao cob cbn cna can con zn zb za zo", "gb vn gn sao sab soa ra ro"),
+                 ("ga cbo cao ta tb tn cba cab con can cbn cnb cob zb za zn zo", "gb vn gn sno sna soa rn ro"),
+                 ("ga cbo tb ta tn cno cob coa cnb con cna can cba zn zo za zb", "gb gn vn sao sab sbn ra rb"),
+                 ("ga cbo tb ta tn cno cob coa cnb con cna can cba zn zo za zb", "gb gn vn sao sab sbn ra rb")),
        "order": (
-           "m0 m1 k_low mz ones half b_quad da db k_group k_et k_etb qu d64 k_etc k_lu qx0 ub k_id qx1 k_twice col0",
-           "col0 b_pair qx2 col1 e10 k_pair qx3 eq0 col2 e01 e20 e02 eq1 e30 own0 eq2 eq3 e33 own1 own2 own3 t3 e23 e12",
-           "e12 z3 z0 z2 z1 k_eight b_mine k_bias so put1 tr trb diag1 low0 low1 low2 turn1a turn1b turn1c turn1d",
-           "turn1d qw0 k_mine join1 joinb1 back1a back1b back1c back1d qw1 gm pqf pqn to oq l2a l2 v1 ga",
-           "ga early tn ta earlyb tb",
-           "za qw2", "zb qw2", "zn qw2", "zo qw2 put2 qw3 diag2 iw turn2a turn2b turn2c turn2d iwb join2",
-           "ms d128 ubs d256 keep0 sign0 keep1 sign1 keep2 sign2 s03 s13 sum0 sum1 sl sl3 d512 keep3 m2 mn",
-           "mn go nb ppf ppn vo nbo gn gb", "ra ic", "rb ic", "rn ic", "ro ic ow",
-           "out_i out_cf out_pf out_cn out_pn")}
+           "m0 ones m1 k_low mz half da db k_group k_et k_etb d64 k_etc k_eight b_mine b_pair qu k_pair qx0 ub qx1 k_id",
+           "k_id k_lu col0 qx2 col1 e10 qx3 e01 col2 eq0 e20 e12 own0 eq1 e30 eq2 e33 eq3 own2 e23 own1 own3 e02 z2 z3",
+           "z3 z0 z1 qw0 k_mine so put1 trf diag1 lowf0 lowf1 lowf2 trn",
+           "trn turn1a turn1b turn1c turn1d lown0 lown1 lown2 join1 joinb1 alla allb back1a back1b back1c back1d",
+           "back1d qw1 pqf gm to l2a l2 v1 ga",
+           "a0 a1 a2 a3 y0 y1 y2 y3 y3b", "b0 b1 b2 b3 ig",
+           "za pqn", "zb pqn", "zn pqn", "zo pqn put2 oq diag2 oqb turn2a turn2b turn2c turn2d qw2 join2",
+           "back2a back2b back2c back2d qw3 a0",
+           "ms d128 ubs d256 keep0 keep1 sign0 sign1 keep2 sign2 s03 s13 keep3 sum0 sum1 sl d512 m2",
+           "pv0 row0 row1 pv1 pv2 row2 twin2 pv3 row3 twin3",
+           "m2 go ppf nb vo gb", "ra ppn", "rb ppn", "rn ppn", "ro ppn ow owb",
+           "out_cf out_pf out_i out_pn out_cn")}
 
 
 def _routes(core, cores, topo):
@@ -160,16 +169,15 @@ def rank_program(g, core, T, topo):
         tr = []
         for d, src, dst in pieces:
             rid, pid, _ = topo.addr(cores[d])
-            engines = routes[cores[d]][:FEW] if sem == "rem_s" else routes[cores[d]]
-            sides = dict(srcs=src, dsts=[dst], alu_op=3) if isinstance(src, list) else dict(src=src, dst=dst)
+            engines = routes[cores[d]][:FEW] if sem in ("rem_s", "rem_n") else routes[cores[d]]
             tr.append(RemoteDMATransfer(dst_ids=[DstId(rid=rid, pnc=pid)],
                                         dma_engine_mask=sum(1 << e for e in engines),
-                                        remote_sem=T.sem[sem], **sides))
+                                        remote_sem=T.sem[sem], src=src, dst=dst))
             counts["loc"] = counts.get("loc", 0) + len(engines)
         call = step("q", deps, busy, lambda: g.remote_dma_fused(tr, local_sem=T.sem.loc), sem=("loc", None), after=after)
-        n = [len(_routes(c, cores, topo)[core]) for c in cores if c != core]
-        n = sum(min(k, FEW) for k in n) if sem == "rem_s" else sum(n)
-        return call, step(None, [call], 0, None, late, (sem, n))
+        n = [len(_routes(cores[d], cores, topo)[core][:FEW if sem in ("rem_s", "rem_n") else None])
+             for d in {"rem_s": far, "rem_n": near}.get(sem, others)]
+        return call, step(None, [call], 0, None, late, (sem, sum(n)))
 
     vec = g.vector
     cp, ts, tt, scan = vec.tensor_copy, vec.tensor_scalar, vec.tensor_tensor, vec.tensor_tensor_scan
@@ -194,22 +202,17 @@ def rank_program(g, core, T, topo):
 
     near = [d for d in others if topo.chip(cores[d]) == topo.chip(core)]
     far = [d for d in others if d not in near]
-    spans = []
-    for i, d in enumerate(others):
-        if spans and spans[-1][1] + spans[-1][2] == d:
-            spans[-1][2] += 1
-        else:
-            spans.append([i, d, 1])
 
     du = dma("a", [], LOAD, T.ut[:, 0:8], T.u[:, 0:8], "du")
     dx, last = [], [du]
     for i, (a, b) in enumerate(OPT["loads"]):
         last = [dma("ya"[i & 1], [], LOAD + RATE * b, T.xt[:, 512 * a:512 * b], T.x[:, 512 * a:512 * b], "dx%d" % i,
                     after=last if i else [])]
-        dx.append(last[0])
-    dw = dma("y", [], LOAD + RATE * 8, T.wt[:], T.w[:], "dw", after=dx)
+        dx += last * (b - a)
+    dw = [dma("y", [], LOAD + RATE * 6, T.wt[:, 0:1024], T.w[:, 0:1024], "dw0", after=dx),
+          dma("y", [], LOAD + RATE * 2, T.wt[:, 1024:2048], T.w[:, 1024:2048], "dw1", after=dx)]
 
-    names = "p eight bias group twice".split()
+    names = "p eight group".split()
     col = {n: T.col[:, i:i + 1] for i, n in enumerate(names)}
     k_p = iota(T.de[:, 0:64], 64, [[0, 4], [-1, 16]], 2048, 1, False)
     made = {"p": [iota(col["p"], 1, [[0, 1]], 0, 1, after=[k_p])]}
@@ -232,27 +235,23 @@ def rank_program(g, core, T, topo):
     for n in (64, 128, 256):
         kd = named["d%d" % (2 * n)] = S([kd], n, T.d0[:, n:2 * n], T.d0[:, 0:n], F.Copy)
     made["group"] = [V([low] + made["p"], 1, ts, col["group"], p15, -1, col["p"], A.mult, A.add)]
-    made["twice"] = [V([low], 1, ts, col["twice"], p15, 2, None, A.mult)]
-    made["bias"] = [V(made["p"], 1, ts, col["bias"], col["p"], 64, 256, A.is_ge, A.mult)]
     x = named["ones"] = fill(T.flip[:, 16:144], 64, 1.0)
     half = named["half"] = fill(T.flip[:, 15:16], 1, 0.5)
     mark = step("q", [x], GSLOW * (170 + 2 * CYCLE * 128), lambda: g.affine_select(
         T.flip[:, 16:144], T.flip[:, 16:144], [[-1, 128]], A.not_equal, -1.0, 0, 1), after=[k_p])
     k_id = V([iota(T.idv0[:], 64, [[128, 4], [1, 16]], -256, 0, after=[mark])] + made["group"], 32, ts, T.idv[:],
              T.idv0[:], col["group"], None, A.add)
-    x = [iota(T.lf[:, 0:4], 4, [[128, 4]], 0, 1, False, [mark]),
-         iota(T.lf[:, 4:36], 32, [[2, 16], [0, 2]], 1, 0, False, [mark]),
-         V([k_p], 1, ts, T.lf[:, 36:37], T.de[:, 0:1], 31, None, A.bitwise_and, kind="plain")]
+    x = [iota(T.lf[:, 0:4], 4, [[128, 4]], 0, 1, False, [k_p]),
+         iota(T.lf[:, 4:12], 8, [[2, 4], [0, 2]], 1, 0, False, [k_p])]
     k_re = step("q", [mark], GSLOW * (170 + 2 * CYCLE * 128), lambda: g.affine_select(
-        T.reset[:], T.flip[:, 16:144], [[-1, 128]], A.not_equal, 0.0, 0, 1), after=x[:2])
-    k_lu = V(x, 37, cp, T.lu[:, 0:37], T.lf[:, 0:37])
-    named["b_quad"] = x[2]
-    quad_list, mine_list, pair_list = (T.lu[:, n:n + 1] for n in (36, 38, 40))
+        T.reset[:], T.flip[:, 16:144], [[-1, 128]], A.not_equal, 0.0, 0, 1), after=x)
+    k_lu = V(x, 12, cp, T.lu[:, 0:12], T.lf[:])
+    mine_list, pair_list = (T.lu[:, n:n + 1] for n in (12, 14))
     made["eight"] = [V([low], 1, ts, col["eight"], p15, 8, 1, A.mult, A.add)]
     x, v = bits(66, 96, 4)
     k_mine = V([x] + made["eight"], 1, ts, mine_list, v, col["eight"], None, A.add)
-    z, v = bits(70, 16, 4)
-    k_pair = V([z] + made["twice"], 1, ts, pair_list, v, col["twice"], None, A.add)
+    z, v = bits(70, 112, 4)
+    k_pair = V([z] + made["eight"], 1, ts, pair_list, v, col["eight"], -1, A.add, A.add)
     named.update({"k_" + n: made[n][0] for n in made})
     named.update(k_mine=k_mine, k_pair=k_pair, b_mine=x, b_pair=z, k_lu=k_lu, k_id=k_id, k_low=low, k_re=k_re)
     mw = {"1": fill(T.wi1[:], 256, -256.0)}
@@ -262,39 +261,33 @@ def rank_program(g, core, T, topo):
             V([mw["1"]], 72, ts, T.et[32:64, 144:288], T.wi1[32:64, 0:144], 0.0, None, A.mult)]
     k_et.append(V(k_et[:1], 1, ts, T.et[0:32, 146:153:2], T.wi1[0:32, 0:4], -3.0, None, A.mult))
     named.update(k_et=k_et[0], k_etb=k_et[1], k_etc=k_et[2])
-    k_eq = iota(T.eq[:, 15:432:144], 3, [[0, 3]], 0, 0, after=[mark])
+    k_eq = iota(T.eq[:, 15:576:144], 4, [[0, 4]], 0, 0, after=[mark])
     k_cb = iota(T.cb[:, PART - 1:4 * PART:PART], 4, [[0, 4]], 64, 0, after=[k_re])
-    k_rr = iota(T.rr[:, 24:128], 104, [[0, 104]], 0, 0, after=[k_cb])
-    k_sg = iota(T.sg2[:, PART2 - 1:4 * PART2:PART2], 4, [[0, 4]], 0, -1, after=[k_rr])
+    k_rr = iota(T.rr[:, 16:128], 112, [[0, 112]], 0, 0, after=[k_cb])
+    k_rq = iota(T.rq[:, 8:128], 120, [[0, 120]], 0, 0, after=[k_rr])
+    k_gm = iota(T.gm[:, 32:128], 96, [[0, 96]], 0, 0, after=[k_rq])
+    k_sg = iota(T.sg2[:, PART2 - 1:4 * PART2:PART2], 4, [[0, 4]], 0, -1, after=[k_gm])
     mi = iota(T.iw[:], 512, [[1, 4], [0, 128]], 0, 0, after=[k_sg])
     mw["2"] = named["m2"] = S([kd], 512, T.wi2[:], T.d0[:], F.Identity, -256.0, 0.0)
-    mn = named["mn"] = S([kd], 512, T.inn[64:128, :], T.d0[64:128, :], F.Copy)
 
     qu = quantize([m0, du], 128, T.uq[:], T.us[:], T.ut[:])
     ub = pick("v", [qu, mz], 128, T.ubq[:, 0:128].bitcast(U32), T.uq[:, 0:128].bitcast(U32).indirect(T.zoff[:, 0:8]))
     ubs = pick("a", [qu, mz], 128, T.ubs[:, 0:128], T.us[:, 0:128].indirect(T.zoff[:, 0:8]))
-    qw = [quantize([dw], 128, T.wq[:, r(k)], T.ws[:, r(k)], T.wt[:, r(k, 512)]) for k in range(4)]
+    qw = [quantize([dw[k // 2]], 128, T.wq[:, r(k)], T.ws[:, r(k)], T.wt[:, r(k, 512)]) for k in range(4)]
 
     pv, vcol, rows, kept, twin = {}, {}, [], [], {}
     for c in range(4):
         qx = quantize([dx[c]], 128, T.xq[:, r(c)], T.xs[:, r(c)], T.xt[:, r(c, 512)])
         mine = T.xq[:, r(c)], T.xs[:, r(c)]
-        if c < 3:
-            pv[c] = P([qx, qu], 128, bank(4 + c), *mine, T.uq[:], T.us[:])
-            if OPT["col"][c] == "v":
-                vcol[c] = V([pv[c]], 1, cp, T.vc[:, c:c + 1], bank(4 + c, 1))
-            else:
-                vcol[c] = S([pv[c]], 1, T.vc[:, c:c + 1], bank(4 + c, 1), F.Copy)
-            named["col%d" % c] = vcol[c]
-        else:
-            pv[c] = P([qx, ub, ubs], 128, bank(4 + c), *mine, T.ubq[:], T.ubs[:])
+        pv[c] = P([qx, qu], 128, bank(4 + c), *mine, T.uq[:], T.us[:])
+        if c < OPT["signs"]:
+            vcol[c] = named["col%d" % c] = V([pv[c]], 1, cp, T.vc[:, c:c + 1], bank(4 + c, 1))
         rows.append(P([qx, ub, ubs], 128, bank(c), T.ubq[:], T.ubs[:], *mine))
-        rows[c]["after"].append(pv[c])
         kept.append(S([rows[c]], 128, T.ss[:, r(c)], bank(c), F.Copy))
         named["keep%d" % c] = kept[c]
         named.update({"qx%d" % c: qx, "row%d" % c: rows[c], "pv%d" % c: pv[c]})
         if c in OPT["twin"]:
-            twin[c] = P([qx, ub, ubs, vcol[3 - c]], 128, bank(7 - c), T.ubq[:], T.ubs[:], *mine)
+            twin[c] = named["twin%d" % c] = P([qx, ub, ubs, vcol[c - 2]], 128, bank(2 + c), T.ubq[:], T.ubs[:], *mine)
             twin[c]["after"].append(rows[c])
 
     def ahead(c, lo, hi, way, at):
@@ -305,11 +298,11 @@ def rank_program(g, core, T, topo):
             y = S([rows[lo], vcol[c]], n, signs, bank(lo), F.Sign, T.vc[:, c:c + 1], -1.0)
             named["s%d%d" % (c, lo)] = y
             return V([y], n / 2, ts, out, signs, 0.0, None, A.is_lt if up else A.is_le)
-        dep, src = (kept[lo:hi], T.ss[:, 128 * lo:128 * hi]) if way in "kK" else ([twin[lo]], bank(7 - lo))
+        dep, src = (kept[lo:hi], T.ss[:, 128 * lo:128 * hi]) if way in "kK" else ([twin[lo]], bank(2 + lo))
         has, v = (vcol[c], T.vc[:, c:c + 1]) if way in "kt" else (pv[c], bank(4 + c, 1))
         y = V(dep + [has], n, ts, out, src, v, None, A.is_gt if up else A.is_ge)
-        if way in "KT" and 3 - c in twin:
-            twin[3 - c]["deps"].append(y)
+        if way in "KT" and c + 2 in twin:
+            twin[c + 2]["deps"].append(y)
         return y
 
     def total(deps, out, c, src, stop, n, first):
@@ -322,7 +315,7 @@ def rank_program(g, core, T, topo):
         ways = OPT["count"][c]
         n = 128 * sum(hi - lo for lo, hi, way in ways if way != "c")
         at, e = PART * (c + 1) - 1 - n, 144 * c + 16
-        if c < 3:
+        if c < OPT["signs"]:
             x = S([rows[c], vcol[c]], 128 + 24, T.sg[:, r(c)], bank(c), F.Sign, T.vc[:, c:c + 1], -1.0,
                   accum_out=T.acc[:, c:c + 1])
             named["sign%d" % c] = x
@@ -331,7 +324,7 @@ def rank_program(g, core, T, topo):
                     T.acc[:, c:c + 1], A.mult, A.subtract)
             first = 0.0
         else:
-            x = V([twin[c], pv[c]], 128, ts, T.eq[:, e:e + 128], bank(7 - c), bank(4 + c, 1), None, A.is_equal)
+            x = V([twin[c], pv[c]], 128, ts, T.eq[:, e:e + 128], bank(2 + c), bank(4 + c, 1), None, A.is_equal)
             own = V([x, k_re], 64, scan, T.cb[:, at - 128:at], T.reset[:], T.eq[:, e:e + 128], 0.0, A.mult, A.subtract)
             first = -64.0
         parts = [own, k_cb]
@@ -352,18 +345,17 @@ def rank_program(g, core, T, topo):
         pz.append(total(parts, T.z1, c, T.cb, PART * (c + 1), n + 2, first))
         named["z%d" % c] = pz[c]
     places = [T["z" + k][:, 4 * HALF - 4:4 * HALF] for k in "12"]
-    if OPT["sl3"] == "k":
-        sl = [pick("a", [k_lu] + kept, 64, T.sl[:], T.ss[:, 0:512].indirect(T.lu[:, 0:4]))]
-    else:
-        t3 = V([pv[3]], 32, vec.transpose, T.t3[:], bank(7, 32))
-        sl = [pick("a", [k_lu] + kept[:3], 48, T.sl[:, 0:48], T.ss[:, 0:384].indirect(T.lu[:, 0:3])),
-              pick(OPT["sl3"], [k_lu, t3], 16, T.sl[:, 48:64], T.t3[:, 0:32].indirect(quad_list))]
-        named.update(t3=t3, sl3=sl[1])
+    sl = [pick("a", [k_lu] + kept, 64, T.sl[:], T.ss[:, 0:512].indirect(T.lu[:, 0:4]))]
     named["sl"] = sl[0]
 
     def make_list(deps, k, places, free):
         wi, wx, ez, lw = (T[n + k] for n in ("wi", "wx", "ez", "lw"))
-        put = by_list(deps + [k_id, mw[k]], PUT * 64, cp, wi[:, 0:512].indirect(places), T.idv[:])
+        put, n = None, OPT["puts"][k == "2"]
+        for i in range(n):
+            at = 4 * HALF - 4 + 4 // n * i
+            put = named["put%s%s" % (k, "a" * (i < n - 1))] = by_list(
+                deps + [k_id, mw[k]] + [put] * i, PUT * 64 / n, cp, wi[:, 0:512].indirect(T["z" + k][:, at:at + 4 // n]),
+                T.idv[:, r(i, 64 // n)])
         diag = V([put, kd], 256, scan, wx[:], wi[:], T.d0[:], -2048.0, A.max, A.add)
         turn = [V([diag] + free, 16, vec.transpose, T.et[0:64, at + 2 * h:at + 2 * h + 288:9], wx[r(h, 64), 15:512:16])
                 for at in (145, 5) for h in range(2)]
@@ -375,36 +367,47 @@ def rank_program(g, core, T, topo):
         return back, join
 
     so = by_list(pz + sl + [ms], PUT * 64, cp, T.so[:, 0:512].indirect(places[0]), T.sl[:])
-    tr = [V([so], 128 * n, vec.transpose, T.tr[:, 128 * i:128 * (i + n)], T.so[:, 128 * d:128 * (d + n)])
-          for i, d, n in spans]
-    low = [V(tr, 24, scan, T.pa[to:to + n, :], T.tr[a:a + n, 0:384:16], T.tr[a + 64:a + 64 + n, 0:384:16], 1e29,
-             A.min, A.min, kind="across") for to, a, n in ((0, 0, 64), (64, 32, 32), (96, 0, 32))]
-    out_s, in_s = send(low, [(d, T.pa[:, r(i, 8)], T.rs[:, r(rank - (rank > d), 8)]) for i, d in enumerate(others)],
-                       "rem_s", FIRST, HOP)
-    named.update(so=so, trb=tr[-1], tr=tr[0], ub=ub, qu=qu, ubs=ubs, ms=ms, out_s=out_s)
-    named.update({"low%d" % k: x for k, x in enumerate(low)})
+    in_s, out_s = [], None
+    for n, ds, at in (("f", far, 0), ("n", near, len(far))):
+        a, b = 128 * at, 128 * (at + len(ds))
+        tr = V([so], b - a, vec.transpose, T.tr[:, a:b], T.so[:, 128 * ds[0]:128 * ds[-1] + 128])
+        low = [V([tr], 16, scan, T.pa[to:to + k, a // 16:b // 16], T.tr[p:p + k, a:b:16], T.tr[p + 64:p + 64 + k, a:b:16],
+                 1e29, A.min, A.min, kind="across") for to, p, k in ((0, 0, 64), (64, 32, 32), (96, 0, 32))]
+        named.update({"low%s%d" % (n, k): x for k, x in enumerate(low)})
+        if n == "f":
+            out_s, x = send(low, [(d, T.pa[:, r(i, 8)], T.rs[:, r(near[0] < rank, 8)]) for i, d in enumerate(ds)],
+                            "rem_s", FIRST, HOP)
+        else:
+            low = [V(low, 16, tt, T.pb[r(h, 64), :], T.pa[0:64, 16:24], T.pa[64:128, 16:24], A.min, kind="across")
+                   for h in range(2)]
+            named.update(alla=low[0], allb=low[1])
+            out_s, x = send(low, [(ds[0], T.pb[:], T.rq[:, 0:8])], "rem_n", 200, HOP - NEAR, after=[out_s])
+        in_s.append(x)
+        named.update({"tr" + n: tr, "out_s" + n: out_s})
+    named.update(so=so, ub=ub, qu=qu, ubs=ubs, ms=ms)
     named.update({"qw%d" % k: qw[k] for k in range(4)})
     lw, free = make_list(pz + [ms] + k_et, "1", places[0], k_et)
 
-    pq, pp, in_c, in_p, sent = {}, {}, [], [], [out_s]
+    pq, pp, in_c, in_p = {}, {}, [], []
     for n, ds, at in (("f", far, 0), ("n", near, 128 * len(far))):
         of, at = T.lw1[:, 8 * ds[0]:8 * ds[-1] + 8], slice(at, at + 128 * len(ds))
         w = 128 * len(ds)
         pq[n] = pick("v", lw, w, T.sq[:, at].bitcast(U32), T.xq[:, 0:512].bitcast(U32).indirect(of))
         pp[n] = pick("a", lw, w, T.sp[:, at], T.xs[:, 0:512].indirect(of))
         named.update({"pq" + n: pq[n], "pp" + n: pp[n]})
-    gm = V(lw, 32, ts, T.gm[:], T.lw1[:], -256, None, A.add)
-    nb = pick("a", [gm, k_pair], 16, T.nb[:], T.gm[:, 0:32].indirect(pair_list))
-    out_i, in_i = send([nb], [(d, T.nb[:, r(d, 4)], T.rn[:, r(rank, 4)]) for d in others], "rem_i", 200, HOP,
+    dw[1]["deps"].append(pp["f"])
+    gm = V(lw, 32, cp, T.gm[:, 0:32], T.lw1[:])
+    nb = pick("a", [gm, k_pair, k_gm], 16, T.nb[:], T.gm[:, 0:128].indirect(pair_list))
+    out_i, in_i = send([nb], [(d, T.nb[:, d:d + 1], T.rn[:, rank:rank + 1]) for d in others], "rem_i", 200, HOP,
                        after=[out_s])
-    for ns, hops in ((("f", 2), ("n", 1)) if OPT["split"] else (("fn", 2),)):
-        ds = [(i, d) for i, d in enumerate(far + near) if "fn"[d in near] in ns]
-        a, b = send([pq[n] for n in ns], [(d, T.sq[:, r(i)].bitcast(U8), T.lq[:, r(rank)].bitcast(U8)) for i, d in ds],
-                    "rem_c", 200, hops * HOP, after=sent[-1:])
-        c, e = send([pp[n] for n in ns], [(d, T.sp[:, r(i)], T.lp[:, r(rank)]) for i, d in ds], "rem_p", 200,
-                    (hops + 0.5) * HOP, after=[a])
-        in_c, in_p, sent = in_c + [b], in_p + [e], sent + [a, c]
-        named.update({"out_c" + ns[0]: a, "out_p" + ns[0]: c})
+    for n, hops in (("f", 2), ("n", 1)):
+        ds = [(i, d) for i, d in enumerate(far + near) if "fn"[d in near] == n]
+        a, b = send([pq[n]], [(d, T.sq[:, r(i)].bitcast(U8), T.lq[:, r(rank)].bitcast(U8)) for i, d in ds],
+                    "rem_c", 200, hops * HOP, after=[out_s])
+        c, e = send([pp[n]], [(d, T.sp[:, r(i)], T.lp[:, r(rank)]) for i, d in ds], "rem_p", 200, hops * HOP,
+                    after=[out_s])
+        in_c, in_p = in_c + [b], in_p + [e]
+        named.update({"out_c" + n: a, "out_p" + n: c})
     named.update(out_i=out_i, nb=nb, gm=gm)
 
     of = T.lw1[:, r(rank, 8)]
@@ -412,28 +415,32 @@ def rank_program(g, core, T, topo):
     bo = V([have[rank]], 128, vec.transpose, T.bo[:], T.sb[:, r(rank)])
     named.update(go=have[rank], to=bo)
     vo = pick(OPT["vo"], [bo, k_lu], 16, T.vo[:], T.bo[:, 0:128].indirect(T.lu[:, 0:1]))
-    oq = pick("v", lw, 128, T.lq[:, r(rank)].bitcast(U32), T.xq[:, 0:512].bitcast(U32).indirect(of))
-    ow = pick("a", lw, 128, T.lp[:, r(rank)], T.xs[:, 0:512].indirect(of))
-    nbo = S([nb], 4, T.rn[:, r(rank, 4)], T.nb[:, r(rank, 4)], F.Copy)
+    oq, ow = [], []
+    for h in range(2):
+        of, at = T.lw1[:, r(2 * rank + h, 4)], r(2 * rank + h, 64)
+        oq.append(pick("v", lw, 64, T.lq[:, at].bitcast(U32), T.xq[:, 0:512].bitcast(U32).indirect(of)))
+        ow.append(pick("a", lw, 64, T.lp[:, at], T.xs[:, 0:512].indirect(of)))
 
-    rr, whole = [V([in_s], 48, tt, T.rr[r(h, 64), 0:24], T.rs[0:64, :], T.rs[64:128, :], A.min, kind="across")
-                 for h in range(2)], T.rr
-    named["l2a"] = rr[0]
-    v1 = pick(OPT["v1"], rr + [k_mine, k_rr], 16, T.v1[:], whole[:, 0:128].indirect(mine_list))
+    rr = [V(in_s[:1], 32, tt, T.rr[r(h, 64), 0:16], T.rs[0:64, :], T.rs[64:128, :], A.min, kind="across")
+          for h in range(2)]
+    v1 = pick(OPT["v1"][0], rr + [k_mine, k_rr], 16, T.v1[:], T.rr[:, 0:128].indirect(mine_list))
+    vn = pick(OPT["v1"][1], [in_s[1], k_mine, k_rq], 16, T.vn[:], T.rq[:, 0:128].indirect(mine_list))
     role = dict(zip(far + near + [rank], "abno"))
-    for i, d in enumerate(others):
-        x = pick(OPT["gather"]["abn".index(role[d])], rr + [k_lu], 128, T.bx[:, r(i)],
-                 whole[:, 0:24].indirect(T.lu[:, 4 + 8 * i:12 + 8 * i]))
+    for i, d in enumerate(far + near):
+        has, src = (in_s[1:], T.rq[:, 0:8]) if d in near else (rr, T.rr[:, r(i, 8)])
+        x = pick(OPT["gather"][i], has + [k_lu], 128, T.bx[:, r(i)], src.indirect(T.lu[:, 4:12]))
         have[d] = V([x], 128, vec.transpose, T.sb[:, r(d)], T.bx[:, r(i)])
         named.update({"g" + role[d]: x, "t" + role[d]: have[d]})
-    named.update(oq=oq, ow=ow, nbo=nbo, l2=rr[-1], v1=v1, vo=vo)
+    named.update(oq=oq[0], oqb=oq[1], ow=ow[0], owb=ow[1], l2a=rr[0], l2=rr[1], v1=v1, vn=vn, vo=vo)
+    token = {rank: (vo, T.vo[:, 0:1]), near[0]: (vn, T.vn[:, 0:1])}
+    token.update({d: (v1, T.v1[:, i:i + 1]) for i, d in enumerate(far)})
 
     who = {n: d for d, n in role.items()}
     ways = OPT["merge"][rank] if len(OPT["merge"]) == N else OPT["merge"][0]
     ways = {(who[w[0]], who[w[1]]): w[2] for w in ways.split()}
     pz2 = []
     for s in range(N):
-        has, mine = (vo, T.vo[:, 0:1]) if s == rank else (v1, T.v1[:, r(others.index(s), 1)])
+        has, mine = token[s]
         ds = [d for d in range(s + 1, N) if ways.get((s, d)) == "c"]
         here = [d for d in range(N) if d != s and d not in ds]
         parts, first, end = list(made["p"]), col["p"], PART2 * (s + 1) - 1
@@ -461,32 +468,30 @@ def rank_program(g, core, T, topo):
         else:
             pz2.append(V(parts, 1, cp, T.z2[:, 4 * HALF - 4 + s:4 * HALF - 3 + s], first))
         named["z" + role[s]] = pz2[s]
-    x = [named["c" + role[s] + "o"] for s in others if (s, rank) not in ways]
-    named.update(zip(("early", "earlyb"), x))
     lm, _ = make_list(pz2, "2", places[1], free)
 
-    ic = S([in_i, nbo, mn], 16, T.inn[64:128, 0:512:32], T.rn[64:128, :], F.Copy)
-    iw = [V([ic, mi], 128, vec.transpose, T.iw[64:128, r(h, 256)], T.inn[64:128, r(h, 256)]) for h in range(2)]
-    ig = S(lm + iw + [mi] + made["bias"], PICK * 512, T.gid[:], T.iw[:, 0:512].indirect(T.lw2[:, 0:32]), F.Identity,
-           col["bias"], fixed=65)
+    iw = [dma("y", [mi, nb if s == rank else in_i], LOAD, T.iw[64:65, r(s)], (T.nb if s == rank else T.rn)[:, s:s + 1],
+              "dn") for s in [rank] + others]
+    for a, b in zip(iw, iw[1:]):
+        b["after"].append(a)
+        a["sem"] = iw[-1]["sem"]
+    ig = named["ig"] = pick("a", lm + iw, 512, T.gid[:], T.iw[:, 0:512].indirect(T.lw2[:, 0:32]))
     dma("a", [ig], LOAD, T.ids[:, :], T.gid[0:128:64, :], "dst")
-    named.update(iw=iw[0], iwb=iw[1], ig=ig, ic=ic)
 
     for k, n in OPT["bands"]:
         of, at = T.lw2[:, 8 * k:8 * (k + n)], slice(128 * k, 128 * (k + n))
-        a = pick("v", lm + [oq] + in_c, 128 * n, T.fq[:, at].bitcast(U32), T.lq[:, 0:512].bitcast(U32).indirect(of))
-        b = pick("a", lm + [ow] + in_p, 128 * n, T.fp[:, at], T.lp[:, 0:512].indirect(of))
+        a = pick("v", lm + oq + in_c, 128 * n, T.fq[:, at].bitcast(U32), T.lq[:, 0:512].bitcast(U32).indirect(of))
+        b = pick("a", lm + ow + in_p, 128 * n, T.fp[:, at], T.lp[:, 0:512].indirect(of))
         named.update({"a%d" % k: a, "b%d" % k: b})
         for j in range(k, k + n):
             x = P([a, b, qw[j]], 128, bank(j), T.wq[:, r(j)], T.ws[:, r(j)], T.fq[:, r(j)], T.fp[:, r(j)])
-            if OPT["ycopy"][j] == "v":
-                x = V([x], 128, cp, T.ysb[:, r(j)], bank(j))
-            else:
-                x = S([x], 128, T.ysb[:, r(j)], bank(j), F.Copy)
-            named["y%d" % j] = x
-            dma(OPT["st"][j], [x], LOAD + 200, T.y[:, r(j)], T.ysb[:, r(j)], "dst")
+            w = 128 // OPT["stores"][j]
+            for i in range(OPT["stores"][j]):
+                at = slice(128 * j + w * i, 128 * j + w * i + w)
+                y = named["y%d%s" % (j, "b" * i)] = V([x], w, cp, T.ysb[:, at], bank(j, w, w * i))
+                dma("y", [y], LOAD + 1.6 * w, T.y[:, at], T.ysb[:, at], "dst")
 
-    for rule in OPT["order"]:
+    for rule in OPT["order"] + OPT["ranks"][rank]:
         rule = [named[n] for n in rule.split() if n in named]
         for a, b in zip(rule, rule[1:]):
             if a is not b:
@@ -500,22 +505,31 @@ def rank_program(g, core, T, topo):
             if s["sem"] is None:
                 counts[q] = counts.get(q, 0) + 1
                 s["sem"] = (q, counts[q])
+    seen, across = {q: {} for q in queues}, []
+    for s in sorted(steps, key=lambda s: (s["at"], s["n"])):
+        q = s["q"]
+        wants = list(s["deps"])
+        if s["kind"] == "across":
+            across = [s]
+        elif q == "v" and s["kind"] == "":
+            wants += across
+        s["waits"] = []
+        for d in sorted(wants, key=lambda d: -d["end"]) if q else []:
+            if seen[q].get(d["sem"][0], 0) < d["sem"][1]:
+                if d["sem"][0] == d["q"]:
+                    d = max([d] + [e for e in order[d["q"]] if e["sem"][0] == d["q"] and e["end"] + LONG <= s["at"]],
+                            key=lambda e: e["sem"][1])
+                s["waits"].append(d["sem"])
+                for sem, n in [d["sem"]] + list(d["knows"].items()):
+                    seen[q][sem] = max(seen[q].get(sem, 0), n)
+        s["knows"] = dict(seen[q]) if q else {}
     for q, E in queues.items():
-        seen = {}
-
         def need(tokens):
             for sem, n in tokens:
-                if seen.get(sem, 0) < n:
-                    E.wait_ge(T.sem[sem], n)
-                    seen[sem] = n
+                E.wait_ge(T.sem[sem], n)
 
-        across = []
         for s in order[q]:
-            if s["kind"] == "across":
-                across = [s["sem"]]
-            elif s["kind"] == "":
-                need(across)
-            need(sorted((d["sem"] for d in s["deps"]), key=lambda t: (t[0], -t[1])))
+            need(s["waits"])
             done = s["call"]()
             if s["sem"][1] is not None:
                 done.then_inc(T.sem[s["sem"][0]], 1 if s["sem"][0] == q else 16)

from concourse.bass import DstId, RemoteDMATransfer
from concourse.mybir import dt, AluOpType as A, ActivationFunctionType as F

N, CH = 4, 128
X4 = "float8_e4m3fn_x4"
PART, PART2, HALF = 656, 400, 272


def _sb(n, d):
    return ("sbuf", [128, n], d)


SCRATCH = {
    "xt": _sb(2048, "bfloat16"), "wt": _sb(2048, "bfloat16"), "ut": _sb(512, "bfloat16"),
    "xq": _sb(512, X4), "xs": _sb(512, "uint8"), "wq": _sb(512, X4), "ws": _sb(512, "uint8"),
    "uq": _sb(128, X4), "us": _sb(128, "uint8"), "ubq": _sb(128, X4), "ubs": _sb(128, "uint8"),
    "sq": _sb(384, X4), "sp": _sb(384, "uint8"), "lq": _sb(512, X4), "lp": _sb(512, "uint8"),
    "fq": _sb(512, X4), "fp": _sb(512, "uint8"),
    "zoff": _sb(8, "uint16"), "flip": _sb(144, "bfloat16"), "reset": _sb(128, "bfloat16"),
    "de": _sb(66, "int32"), "de2": _sb(72, "int32"),
    "da": _sb(64, "bfloat16"), "db": _sb(64, "bfloat16"), "d0": _sb(512, "bfloat16"),
    "col": _sb(16, "float32"), "lf": _sb(12, "int32"), "lu": _sb(16, "uint16"),
    "idv0": _sb(64, "bfloat16"), "idv": _sb(64, "bfloat16"),
    "ss": _sb(512, "float32"), "vc": _sb(4, "float32"), "sg": _sb(512, "bfloat16"), "sgb": _sb(2048, "bfloat16"),
    "acc": _sb(8, "float32"), "eq": _sb(576, "bfloat16"), "sgc": _sb(1152, "bfloat16"),
    "cb": _sb(4 * PART, "bfloat16"), "t3": _sb(32, "float32"),
    "sl": _sb(64, "float32"), "so": _sb(512, "float32"), "tr": _sb(384, "float32"),
    "pa": _sb(24, "float32"), "gm": _sb(128, "float32"), "nb": _sb(16, "float32"), "et": _sb(436, "float16"),
    "pb": _sb(8, "float32"), "rq": _sb(128, "float32"), "vn": _sb(16, "float32"),
    "rs": _sb(16, "float32"), "rr": _sb(128, "float32"), "bx": _sb(384, "float32"), "bo": _sb(128, "float32"),
    "sb": _sb(512, "float32"), "v1": _sb(16, "float32"), "vo": _sb(16, "float32"),
    "sg2": _sb(4 * PART2, "bfloat16"), "c2": _sb(1536, "bfloat16"),
    "acc2": _sb(4, "float32"), "rn": _sb(4, "float32"),
    "iw": _sb(512, "float32"), "gid": _sb(512, "float32"),
    "ysb": _sb(512, "float32"),
    "ps": ("psum", [128, 4096], "float32"),
}
for _k in ("1", "2"):
    SCRATCH.update({"z" + _k: _sb(4 * HALF, "uint16"), "wi" + _k: _sb(512, "bfloat16"), "wx" + _k: _sb(512, "float16"),
                    "ez" + _k: _sb(288, "uint16"), "lw" + _k: _sb(32, "uint16")})
SEMAPHORES = ["v", "a", "t", "q", "du", "dx0", "dx1", "dx2", "dx3", "dw0", "dw1", "dn", "dst",
              "rem_s", "rem_n", "rem_c", "rem_p", "rem_i", "loc"]

WAIT = 215
CYCLE, CALL, ACT, SLOW, GSLOW = 0.83, 0, 65, 1.0, 1.0
ROUNDS = 0
LONG = 1e9
SLACK = 0
LOAD, RATE, FIRST, HOP, NEAR = 1000, 500, 1000, 1300, 250
OPT = {"loads": ((0, 1), (1, 2), (2, 3), (3, 4)), "twin": (2, 3),
       "count": (((1, 2, "k"), (2, 3, "t"), (3, 4, "c")), ((0, 1, "K"), (2, 3, "t"), (3, 4, "c")),
                 ((0, 2, "K"), (3, 4, "t")), ((0, 3, "K"), (3, 4, "T"))), "col": "vvv",
       "signs": 3, "few": 4, "puts": (1, 1), "merge": ("aos abc oac", "noc nac oac", "aoc abc bnc", "aoc abc bnc"), "ycopy": "vvvv", "vo": "a", "sl3": "k", "split": 1,
       "gather": "vaa", "v1": "va", "bands": ((0, 1), (1, 1), (2, 1), (3, 1)), "stores": (1, 1, 1, 1),
       "ranks": (("ga cbo tb ta cno cnb tn cba cao cob cbn cna can con zn zb za zo", "gb vn gn sao sab soa ra ro"),
                 ("ga cbo cao ta tb tn cba cab con can cbn cnb cob zb za zn zo", "gb vn gn sno sna soa rn ro"),
                 ("ga cbo tb ta tn cno cob coa cnb con cna can cba zn zo za zb", "gb gn vn sao sab sbn ra rb"),
                 ("ga cbo tb ta tn cno cob coa cnb con cna can cba zn zo za zb", "gb gn vn sao sab sbn ra rb")),
       "order": (
           "m0 ones m1 k_low mz half da db k_group k_et k_etb d64 k_etc k_eight b_mine b_pair qu k_pair qx0 ub qx1 k_id",
           "k_id k_lu col0 qx2 col1 e10 qx3 e01 col2 eq0 e20 e12 own0 eq1 e30 eq2 e33 eq3 own2 e23 own1 own3 e02 z2 z3",
           "z3 z0 z1 qw0 k_mine so put1 trf diag1 lowf0 lowf1 lowf2 trn",
           "trn turn1a turn1b turn1c turn1d lown0 lown1 lown2 join1 joinb1 alla allb back1a back1b back1c back1d",
           "back1d qw1 pqf gm to l2a l2 v1 ga",
           "a0 a1 a2 a3 y0 y1 y2 y3 y3b", "b0 b1 b2 b3 ig",
           "za pqn", "zb pqn", "zn pqn", "zo pqn put2 oq diag2 oqb turn2a turn2b turn2c turn2d qw2 join2",
           "back2a back2b back2c back2d qw3 a0",
           "ms d128 ubs d256 keep0 keep1 sign0 sign1 keep2 sign2 s03 s13 keep3 sum0 sum1 sl d512 m2",
           "pv0 row0 row1 pv1 pv2 row2 twin2 pv3 row3 twin3",
           "m2 go ppf nb vo gb", "ra ppn", "rb ppn", "rn ppn", "ro ppn ow owb",
           "out_cf out_pf out_i out_pn out_cn")}


def _routes(core, cores, topo):
    far = [c for c in cores if c != core and topo.chip(c) != topo.chip(core)]
    near = [c for c in cores if c != core and topo.chip(c) == topo.chip(core)]
    out, used = {}, set()
    for i, c in enumerate(far):
        e = topo.engines(core, c)
        k = 1
        while 2 * k * len(far) <= len(e):
            k *= 2
        out[c] = e[i * k:i * k + k]
        used.update(out[c])
    for i, c in enumerate(near):
        e = [n for n in topo.engines(core, c) if n not in used]
        k = 1
        while 2 * k * len(near) <= len(e):
            k *= 2
        out[c] = e[i * k:i * k + k]
    return out


def _arrange(steps):
    later = [[] for s in steps]
    for i, s in enumerate(steps):
        s["n"] = i
    for s in steps:
        for d in s["deps"]:
            later[d["n"]].append((s, WAIT + d["late"]))
        for d in s["after"]:
            later[d["n"]].append((s, 0))

    def chain(s):
        if not s["chain"]:
            s["chain"] = s["busy"] + 1 + max([s["late"]] + [w + chain(n) for n, w in later[s["n"]]])
        return s["chain"]

    def place(key, back):
        taken, first, second = {}, "" if back else "across", "across" if back else ""
        for s in sorted(steps, key=key):
            if back:
                t = max([s["late"]] + [n["left"] + w for n, w in later[s["n"]]])
            else:
                t = max([0] + [d["end"] + WAIT for d in s["deps"]] + [d["at"] + d["busy"] for d in s["after"]])
            if s["q"]:
                for a, b, kind in sorted(taken.setdefault(s["q"], [])):
                    if t < a and t + s["busy"] - SLACK + WAIT * (s["kind"] == first and kind == second) <= a:
                        break
                    t = max(t, b + WAIT * (kind == first and s["kind"] == second))
                taken[s["q"]].append((t, t + s["busy"], s["kind"]))
            if back:
                s["left"] = t + s["busy"] + 1
            else:
                s["at"], s["end"] = t, t + s["busy"] + s["late"]

    place(lambda s: -chain(s), False)
    for _ in range(ROUNDS):
        place(lambda s: (-s["at"] - s["busy"], chain(s)), True)
        place(lambda s: (-s["left"], -chain(s)), False)


def rank_program(g, core, T, topo):
    rank = T.rank_of(core)
    if rank is None:
        return
    cores = T.cores
    others = [d for d in range(N) if d != rank]
    routes = _routes(core, cores, topo)
    FEW = OPT["few"]
    U32, U8 = dt.uint32, dt.uint8
    queues = {"v": g.vector, "a": g.scalar, "t": g.tensor, "q": g, "y": g.sync}
    steps, counts, named = [], {}, {}

    def step(q, deps, busy, call, late=0, sem=None, after=(), kind=""):
        s = {"q": q, "deps": list(deps), "after": list(after), "busy": busy, "late": late, "call": call, "sem": sem,
             "chain": 0, "kind": kind}
        steps.append(s)
        return s

    def V(deps, n, call, *a, kind=""):
        return step("v", deps, CALL + CYCLE * max(n, 64), lambda: call(*a), kind=kind)

    def S(deps, n, *a, fixed=ACT, **k):
        return step("a", deps, fixed + CYCLE * n, lambda: g.scalar.activation(*a, **k))

    def P(deps, n, *a):
        return step("t", deps, SLOW * CYCLE * (n + 16), lambda: g.tensor.matmul_mx(*a, True, True), 120)

    def iota(out, n, pattern, base, mult, small=True, after=()):
        return step("q", [], GSLOW * (130 + 2 * CYCLE * n),
                    lambda: g.iota(out, pattern, base, mult, allow_small_or_imprecise_dtypes=small), after=after)

    def dma(q, deps, late, out, in_, sem, after=()):
        counts[sem] = counts.get(sem, 0) + 16
        return step(q, deps, 50, lambda: queues[q].dma_start(out, in_), late, (sem, counts[sem]), after)

    def send(deps, pieces, sem, busy, late, after=()):
        tr = []
        for d, src, dst in pieces:
            rid, pid, _ = topo.addr(cores[d])
            engines = routes[cores[d]][:FEW] if sem in ("rem_s", "rem_n") else routes[cores[d]]
            tr.append(RemoteDMATransfer(dst_ids=[DstId(rid=rid, pnc=pid)],
                                        dma_engine_mask=sum(1 << e for e in engines),
                                        remote_sem=T.sem[sem], src=src, dst=dst))
            counts["loc"] = counts.get("loc", 0) + len(engines)
        call = step("q", deps, busy, lambda: g.remote_dma_fused(tr, local_sem=T.sem.loc), sem=("loc", None), after=after)
        n = [len(_routes(cores[d], cores, topo)[core][:FEW if sem in ("rem_s", "rem_n") else None])
             for d in {"rem_s": far, "rem_n": near}.get(sem, others)]
        return call, step(None, [call], 0, None, late, (sem, sum(n)))

    vec = g.vector
    cp, ts, tt, scan = vec.tensor_copy, vec.tensor_scalar, vec.tensor_tensor, vec.tensor_tensor_scan
    PICK, PUT = 1.5, 3.0

    def r(c, w=128):
        return slice(w * c, w * c + w)

    def by_list(deps, n, call, *a):
        return step("v", deps, 50 + CYCLE * n, lambda: call(*a))

    def pick(q, deps, n, out, src):
        if q == "v":
            return by_list(deps, PICK * n, cp, out, src)
        return S(deps, PICK * n, out, src, F.Copy, fixed=65)

    def quantize(deps, n, *a):
        return step("v", deps, 12 + 0.88 * n, lambda: vec.quantize_mx(*a))

    def bank(b, n=128, a=0):
        return T.ps[:, 512 * b + a:512 * b + a + n]

    near = [d for d in others if topo.chip(cores[d]) == topo.chip(core)]
    far = [d for d in others if d not in near]

    du = dma("a", [], LOAD, T.ut[:, 0:8], T.u[:, 0:8], "du")
    dx, last = [], [du]
    for i, (a, b) in enumerate(OPT["loads"]):
        last = [dma("ya"[i & 1], [], LOAD + RATE * b, T.xt[:, 512 * a:512 * b], T.x[:, 512 * a:512 * b], "dx%d" % i,
                    after=last if i else [])]
        dx += last * (b - a)
    dw = [dma("y", [], LOAD + RATE * 6, T.wt[:, 0:1024], T.w[:, 0:1024], "dw0", after=dx),
          dma("y", [], LOAD + RATE * 2, T.wt[:, 1024:2048], T.w[:, 1024:2048], "dw1", after=dx)]

    names = "p eight group".split()
    col = {n: T.col[:, i:i + 1] for i, n in enumerate(names)}
    k_p = iota(T.de[:, 0:64], 64, [[0, 4], [-1, 16]], 2048, 1, False)
    made = {"p": [iota(col["p"], 1, [[0, 1]], 0, 1, after=[k_p])]}

    def fill(out, n, c):
        return V([], n, vec.memset, out, c, kind="plain")

    def bits(at, a, b):
        return V([k_p], 1, ts, T.de2[:, at:at + 1], T.de[:, 0:1], a, b, A.bitwise_and, A.logical_shift_right,
                 kind="plain"), T.de2[:, at:at + 1]

    m0 = fill(T.ut[:, 8:512], 252, 0.0)
    mz = fill(T.zoff[:], 8, 0)
    low = V([k_p], 64, ts, T.de2[:, 0:64], T.de[:, 0:64], 15, None, A.bitwise_and, kind="plain")
    p15 = T.de2[:, 0:1]
    x = [V([low], 64, ts, out[:], T.de2[:, 0:64], at, k, A.is_equal, A.mult)
         for out, at, k in ((T.da, 0, 768), (T.db, 1, -1280))]
    kd = V(x, 128, tt, T.d0[:, 0:64], T.da[:], T.db[:], A.add)
    named.update(m0=m0, mz=mz, da=x[0], db=x[1], d64=kd)
    for n in (64, 128, 256):
        kd = named["d%d" % (2 * n)] = S([kd], n, T.d0[:, n:2 * n], T.d0[:, 0:n], F.Copy)
    made["group"] = [V([low] + made["p"], 1, ts, col["group"], p15, -1, col["p"], A.mult, A.add)]
    x = named["ones"] = fill(T.flip[:, 16:144], 64, 1.0)
    half = named["half"] = fill(T.flip[:, 15:16], 1, 0.5)
    mark = step("q", [x], GSLOW * (170 + 2 * CYCLE * 128), lambda: g.affine_select(
        T.flip[:, 16:144], T.flip[:, 16:144], [[-1, 128]], A.not_equal, -1.0, 0, 1), after=[k_p])
    k_id = V([iota(T.idv0[:], 64, [[128, 4], [1, 16]], -256, 0, after=[mark])] + made["group"], 32, ts, T.idv[:],
             T.idv0[:], col["group"], None, A.add)
    x = [iota(T.lf[:, 0:4], 4, [[128, 4]], 0, 1, False, [k_p]),
         iota(T.lf[:, 4:12], 8, [[2, 4], [0, 2]], 1, 0, False, [k_p])]
    k_re = step("q", [mark], GSLOW * (170 + 2 * CYCLE * 128), lambda: g.affine_select(
        T.reset[:], T.flip[:, 16:144], [[-1, 128]], A.not_equal, 0.0, 0, 1), after=x)
    k_lu = V(x, 12, cp, T.lu[:, 0:12], T.lf[:])
    mine_list, pair_list = (T.lu[:, n:n + 1] for n in (12, 14))
    made["eight"] = [V([low], 1, ts, col["eight"], p15, 8, 1, A.mult, A.add)]
    x, v = bits(66, 96, 4)
    k_mine = V([x] + made["eight"], 1, ts, mine_list, v, col["eight"], None, A.add)
    z, v = bits(70, 112, 4)
    k_pair = V([z] + made["eight"], 1, ts, pair_list, v, col["eight"], -1, A.add, A.add)
    named.update({"k_" + n: made[n][0] for n in made})
    named.update(k_mine=k_mine, k_pair=k_pair, b_mine=x, b_pair=z, k_lu=k_lu, k_id=k_id, k_low=low, k_re=k_re)
    mw = {"1": fill(T.wi1[:], 256, -256.0)}
    named["m1"] = mw["1"]
    ms = S([mw["1"]], 512, T.so[:], T.wi1[:], F.Copy, 0.0, -1e26)
    k_et = [V([mw["1"]], 72, ts, T.et[0:32, 144:288], T.wi1[0:32, 0:144], 2.0, None, A.mult),
            V([mw["1"]], 72, ts, T.et[32:64, 144:288], T.wi1[32:64, 0:144], 0.0, None, A.mult)]
    k_et.append(V(k_et[:1], 1, ts, T.et[0:32, 146:153:2], T.wi1[0:32, 0:4], -3.0, None, A.mult))
    named.update(k_et=k_et[0], k_etb=k_et[1], k_etc=k_et[2])
    k_eq = iota(T.eq[:, 15:576:144], 4, [[0, 4]], 0, 0, after=[mark])
    k_cb = iota(T.cb[:, PART - 1:4 * PART:PART], 4, [[0, 4]], 64, 0, after=[k_re])
    k_rr = iota(T.rr[:, 16:128], 112, [[0, 112]], 0, 0, after=[k_cb])
    k_rq = iota(T.rq[:, 8:128], 120, [[0, 120]], 0, 0, after=[k_rr])
    k_gm = iota(T.gm[:, 32:128], 96, [[0, 96]], 0, 0, after=[k_rq])
    k_sg = iota(T.sg2[:, PART2 - 1:4 * PART2:PART2], 4, [[0, 4]], 0, -1, after=[k_gm])
    mi = iota(T.iw[:], 512, [[1, 4], [0, 128]], 0, 0, after=[k_sg])
    mw["2"] = named["m2"] = S([kd], 512, T.wi2[:], T.d0[:], F.Identity, -256.0, 0.0)

    qu = quantize([m0, du], 128, T.uq[:], T.us[:], T.ut[:])
    ub = pick("v", [qu, mz], 128, T.ubq[:, 0:128].bitcast(U32), T.uq[:, 0:128].bitcast(U32).indirect(T.zoff[:, 0:8]))
    ubs = pick("a", [qu, mz], 128, T.ubs[:, 0:128], T.us[:, 0:128].indirect(T.zoff[:, 0:8]))
    qw = [quantize([dw[k // 2]], 128, T.wq[:, r(k)], T.ws[:, r(k)], T.wt[:, r(k, 512)]) for k in range(4)]

    pv, vcol, rows, kept, twin = {}, {}, [], [], {}
    for c in range(4):
        qx = quantize([dx[c]], 128, T.xq[:, r(c)], T.xs[:, r(c)], T.xt[:, r(c, 512)])
        mine = T.xq[:, r(c)], T.xs[:, r(c)]
        pv[c] = P([qx, qu], 128, bank(4 + c), *mine, T.uq[:], T.us[:])
        if c < OPT["signs"]:
            vcol[c] = named["col%d" % c] = V([pv[c]], 1, cp, T.vc[:, c:c + 1], bank(4 + c, 1))
        rows.append(P([qx, ub, ubs], 128, bank(c), T.ubq[:], T.ubs[:], *mine))
        kept.append(S([rows[c]], 128, T.ss[:, r(c)], bank(c), F.Copy))
        named["keep%d" % c] = kept[c]
        named.update({"qx%d" % c: qx, "row%d" % c: rows[c], "pv%d" % c: pv[c]})
        if c in OPT["twin"]:
            twin[c] = named["twin%d" % c] = P([qx, ub, ubs, vcol[c - 2]], 128, bank(2 + c), T.ubq[:], T.ubs[:], *mine)
            twin[c]["after"].append(rows[c])

    def ahead(c, lo, hi, way, at):
        n, up = 128 * (hi - lo), lo > c
        out = T.cb[:, at:at + n]
        if way == "s":
            signs = T.sgb[:, r(4 * c + lo)]
            y = S([rows[lo], vcol[c]], n, signs, bank(lo), F.Sign, T.vc[:, c:c + 1], -1.0)
            named["s%d%d" % (c, lo)] = y
            return V([y], n / 2, ts, out, signs, 0.0, None, A.is_lt if up else A.is_le)
        dep, src = (kept[lo:hi], T.ss[:, 128 * lo:128 * hi]) if way in "kK" else ([twin[lo]], bank(2 + lo))
        has, v = (vcol[c], T.vc[:, c:c + 1]) if way in "kt" else (pv[c], bank(4 + c, 1))
        y = V(dep + [has], n, ts, out, src, v, None, A.is_gt if up else A.is_ge)
        if way in "KT" and c + 2 in twin:
            twin[c + 2]["deps"].append(y)
        return y

    def total(deps, out, c, src, stop, n, first):
        h = n // 2
        return V(deps, h / 2, scan, out[:, 4 * (HALF - h) + c:4 * HALF:4], src[:, stop - n:stop - h],
                 src[:, stop - h:stop], first, A.add, A.add)

    pz = []
    for c in range(4):
        ways = OPT["count"][c]
        n = 128 * sum(hi - lo for lo, hi, way in ways if way != "c")
        at, e = PART * (c + 1) - 1 - n, 144 * c + 16
        if c < OPT["signs"]:
            x = S([rows[c], vcol[c]], 128 + 24, T.sg[:, r(c)], bank(c), F.Sign, T.vc[:, c:c + 1], -1.0,
                  accum_out=T.acc[:, c:c + 1])
            named["sign%d" % c] = x
            x = V([x], 64, ts, T.eq[:, e:e + 128], T.sg[:, r(c)], 0.0, 0.5, A.is_equal, A.mult)
            own = V([x, mark, half, k_eq], 65, scan, T.cb[:, at - 129:at], T.flip[:, 15:144], T.eq[:, e - 1:e + 128],
                    T.acc[:, c:c + 1], A.mult, A.subtract)
            first = 0.0
        else:
            x = V([twin[c], pv[c]], 128, ts, T.eq[:, e:e + 128], bank(2 + c), bank(4 + c, 1), None, A.is_equal)
            own = V([x, k_re], 64, scan, T.cb[:, at - 128:at], T.reset[:], T.eq[:, e:e + 128], 0.0, A.mult, A.subtract)
            first = -64.0
        parts = [own, k_cb]
        named.update({"eq%d" % c: x, "own%d" % c: own})
        for lo, hi, way in ways:
            if way != "c":
                parts.append(ahead(c, lo, hi, way, at))
                named["e%d%d" % (c, lo)] = parts[-1]
                at += 128 * (hi - lo)
        los = [lo for lo, hi, way in ways if way == "c"]
        if los:
            x = [S([rows[lo], vcol[c]], 128, T.sgc[:, r(3 * c + i)], bank(lo), F.Sign, T.vc[:, c:c + 1], -1.0)
                 for i, lo in enumerate(los)]
            named.update({"s%d%d" % (c, lo): y for lo, y in zip(los, x)})
            first, signs = T.acc[:, 4 + c:5 + c], T.sgc[:, 384 * c:384 * c + 128 * len(los)]
            parts.append(S(x, 128 * len(los) + 24, signs, signs, F.Relu, 0.0, -1.0, accum_out=first))
            named["sum%d" % c] = parts[-1]
        pz.append(total(parts, T.z1, c, T.cb, PART * (c + 1), n + 2, first))
        named["z%d" % c] = pz[c]
    places = [T["z" + k][:, 4 * HALF - 4:4 * HALF] for k in "12"]
    sl = [pick("a", [k_lu] + kept, 64, T.sl[:], T.ss[:, 0:512].indirect(T.lu[:, 0:4]))]
    named["sl"] = sl[0]

    def make_list(deps, k, places, free):
        wi, wx, ez, lw = (T[n + k] for n in ("wi", "wx", "ez", "lw"))
        put, n = None, OPT["puts"][k == "2"]
        for i in range(n):
            at = 4 * HALF - 4 + 4 // n * i
            put = named["put%s%s" % (k, "a" * (i < n - 1))] = by_list(
                deps + [k_id, mw[k]] + [put] * i, PUT * 64 / n, cp, wi[:, 0:512].indirect(T["z" + k][:, at:at + 4 // n]),
                T.idv[:, r(i, 64 // n)])
        diag = V([put, kd], 256, scan, wx[:], wi[:], T.d0[:], -2048.0, A.max, A.add)
        turn = [V([diag] + free, 16, vec.transpose, T.et[0:64, at + 2 * h:at + 2 * h + 288:9], wx[r(h, 64), 15:512:16])
                for at in (145, 5) for h in range(2)]
        join = [V(turn, 72, scan, ez[0:32, r(h, 144)], T.et[0:32, 144:288], T.et[32:64, 144:288], 0.0, A.add, A.max,
                  kind="across") for h in range(2)]
        back = [V(join, 16, vec.transpose, lw[r(a, 32), :], ez[0:32, 8:288:9]) for a in range(4)]
        named.update({"put" + k: put, "diag" + k: diag, "join" + k: join[0], "joinb" + k: join[1]})
        named.update({n + k + "abcd"[a]: x[a] for n, x in (("turn", turn), ("back", back)) for a in range(4)})
        return back, join

    so = by_list(pz + sl + [ms], PUT * 64, cp, T.so[:, 0:512].indirect(places[0]), T.sl[:])
    in_s, out_s = [], None
    for n, ds, at in (("f", far, 0), ("n", near, len(far))):
        a, b = 128 * at, 128 * (at + len(ds))
        tr = V([so], b - a, vec.transpose, T.tr[:, a:b], T.so[:, 128 * ds[0]:128 * ds[-1] + 128])
        low = [V([tr], 16, scan, T.pa[to:to + k, a // 16:b // 16], T.tr[p:p + k, a:b:16], T.tr[p + 64:p + 64 + k, a:b:16],
                 1e29, A.min, A.min, kind="across") for to, p, k in ((0, 0, 64), (64, 32, 32), (96, 0, 32))]
        named.update({"low%s%d" % (n, k): x for k, x in enumerate(low)})
        if n == "f":
            out_s, x = send(low, [(d, T.pa[:, r(i, 8)], T.rs[:, r(near[0] < rank, 8)]) for i, d in enumerate(ds)],
                            "rem_s", FIRST, HOP)
        else:
            low = [V(low, 16, tt, T.pb[r(h, 64), :], T.pa[0:64, 16:24], T.pa[64:128, 16:24], A.min, kind="across")
                   for h in range(2)]
            named.update(alla=low[0], allb=low[1])
            out_s, x = send(low, [(ds[0], T.pb[:], T.rq[:, 0:8])], "rem_n", 200, HOP - NEAR, after=[out_s])
        in_s.append(x)
        named.update({"tr" + n: tr, "out_s" + n: out_s})
    named.update(so=so, ub=ub, qu=qu, ubs=ubs, ms=ms)
    named.update({"qw%d" % k: qw[k] for k in range(4)})
    lw, free = make_list(pz + [ms] + k_et, "1", places[0], k_et)

    pq, pp, in_c, in_p = {}, {}, [], []
    for n, ds, at in (("f", far, 0), ("n", near, 128 * len(far))):
        of, at = T.lw1[:, 8 * ds[0]:8 * ds[-1] + 8], slice(at, at + 128 * len(ds))
        w = 128 * len(ds)
        pq[n] = pick("v", lw, w, T.sq[:, at].bitcast(U32), T.xq[:, 0:512].bitcast(U32).indirect(of))
        pp[n] = pick("a", lw, w, T.sp[:, at], T.xs[:, 0:512].indirect(of))
        named.update({"pq" + n: pq[n], "pp" + n: pp[n]})
    dw[1]["deps"].append(pp["f"])
    gm = V(lw, 32, cp, T.gm[:, 0:32], T.lw1[:])
    nb = pick("a", [gm, k_pair, k_gm], 16, T.nb[:], T.gm[:, 0:128].indirect(pair_list))
    out_i, in_i = send([nb], [(d, T.nb[:, d:d + 1], T.rn[:, rank:rank + 1]) for d in others], "rem_i", 200, HOP,
                       after=[out_s])
    for n, hops in (("f", 2), ("n", 1)):
        ds = [(i, d) for i, d in enumerate(far + near) if "fn"[d in near] == n]
        a, b = send([pq[n]], [(d, T.sq[:, r(i)].bitcast(U8), T.lq[:, r(rank)].bitcast(U8)) for i, d in ds],
                    "rem_c", 200, hops * HOP, after=[out_s])
        c, e = send([pp[n]], [(d, T.sp[:, r(i)], T.lp[:, r(rank)]) for i, d in ds], "rem_p", 200, hops * HOP,
                    after=[out_s])
        in_c, in_p = in_c + [b], in_p + [e]
        named.update({"out_c" + n: a, "out_p" + n: c})
    named.update(out_i=out_i, nb=nb, gm=gm)

    of = T.lw1[:, r(rank, 8)]
    have = {rank: pick("a", lw + kept, 128, T.sb[:, r(rank)], T.ss[:, 0:512].indirect(of))}
    bo = V([have[rank]], 128, vec.transpose, T.bo[:], T.sb[:, r(rank)])
    named.update(go=have[rank], to=bo)
    vo = pick(OPT["vo"], [bo, k_lu], 16, T.vo[:], T.bo[:, 0:128].indirect(T.lu[:, 0:1]))
    oq, ow = [], []
    for h in range(2):
        of, at = T.lw1[:, r(2 * rank + h, 4)], r(2 * rank + h, 64)
        oq.append(pick("v", lw, 64, T.lq[:, at].bitcast(U32), T.xq[:, 0:512].bitcast(U32).indirect(of)))
        ow.append(pick("a", lw, 64, T.lp[:, at], T.xs[:, 0:512].indirect(of)))

    rr = [V(in_s[:1], 32, tt, T.rr[r(h, 64), 0:16], T.rs[0:64, :], T.rs[64:128, :], A.min, kind="across")
          for h in range(2)]
    v1 = pick(OPT["v1"][0], rr + [k_mine, k_rr], 16, T.v1[:], T.rr[:, 0:128].indirect(mine_list))
    vn = pick(OPT["v1"][1], [in_s[1], k_mine, k_rq], 16, T.vn[:], T.rq[:, 0:128].indirect(mine_list))
    role = dict(zip(far + near + [rank], "abno"))
    for i, d in enumerate(far + near):
        has, src = (in_s[1:], T.rq[:, 0:8]) if d in near else (rr, T.rr[:, r(i, 8)])
        x = pick(OPT["gather"][i], has + [k_lu], 128, T.bx[:, r(i)], src.indirect(T.lu[:, 4:12]))
        have[d] = V([x], 128, vec.transpose, T.sb[:, r(d)], T.bx[:, r(i)])
        named.update({"g" + role[d]: x, "t" + role[d]: have[d]})
    named.update(oq=oq[0], oqb=oq[1], ow=ow[0], owb=ow[1], l2a=rr[0], l2=rr[1], v1=v1, vn=vn, vo=vo)
    token = {rank: (vo, T.vo[:, 0:1]), near[0]: (vn, T.vn[:, 0:1])}
    token.update({d: (v1, T.v1[:, i:i + 1]) for i, d in enumerate(far)})

    who = {n: d for d, n in role.items()}
    ways = OPT["merge"][rank] if len(OPT["merge"]) == N else OPT["merge"][0]
    ways = {(who[w[0]], who[w[1]]): w[2] for w in ways.split()}
    pz2 = []
    for s in range(N):
        has, mine = token[s]
        ds = [d for d in range(s + 1, N) if ways.get((s, d)) == "c"]
        here = [d for d in range(N) if d != s and d not in ds]
        parts, first, end = list(made["p"]), col["p"], PART2 * (s + 1) - 1
        if ds:
            at = end - 128 * len(ds)
            x = [S([has, have[d]], 128, T.sg2[:, at + 128 * i:at + 128 * i + 128], T.sb[:, r(d)], F.Sign, mine, -1.0)
                 for i, d in enumerate(ds)]
            named.update({"s" + role[s] + role[d]: y for d, y in zip(ds, x)})
            first, signs = T.acc2[:, s:s + 1], T.sg2[:, at:end + 1]
            parts.append(S(x + [k_sg], 128 * len(ds) + 24, signs, signs, F.Relu, 0.0, -1.0, accum_out=first))
            named["r" + role[s]] = parts[-1]
        for i, d in enumerate(here):
            out = T.c2[:, r(3 * s + i)]
            if (s, d) in ways:
                signs = T.sg2[:, PART2 * s + 128 * i:PART2 * s + 128 * i + 128]
                x = named["s" + role[s] + role[d]] = S([has, have[d]], 128, signs, T.sb[:, r(d)], F.Sign, mine, -1.0)
                x = V([x], 64, ts, out, signs, 0.0, None, A.is_le if d < s else A.is_lt)
            else:
                x = V([has, have[d]], 128, ts, out, T.sb[:, r(d)], mine, None, A.is_ge if d < s else A.is_gt)
            named["c" + role[s] + role[d]] = x
            parts.append(x)
        n = 128 * len(here)
        if here:
            pz2.append(total(parts, T.z2, s, T.c2, 384 * s + n, n, first))
        else:
            pz2.append(V(parts, 1, cp, T.z2[:, 4 * HALF - 4 + s:4 * HALF - 3 + s], first))
        named["z" + role[s]] = pz2[s]
    lm, _ = make_list(pz2, "2", places[1], free)

    iw = [dma("y", [mi, nb if s == rank else in_i], LOAD, T.iw[64:65, r(s)], (T.nb if s == rank else T.rn)[:, s:s + 1],
              "dn") for s in [rank] + others]
    for a, b in zip(iw, iw[1:]):
        b["after"].append(a)
        a["sem"] = iw[-1]["sem"]
    ig = named["ig"] = pick("a", lm + iw, 512, T.gid[:], T.iw[:, 0:512].indirect(T.lw2[:, 0:32]))
    dma("a", [ig], LOAD, T.ids[:, :], T.gid[0:128:64, :], "dst")

    for k, n in OPT["bands"]:
        of, at = T.lw2[:, 8 * k:8 * (k + n)], slice(128 * k, 128 * (k + n))
        a = pick("v", lm + oq + in_c, 128 * n, T.fq[:, at].bitcast(U32), T.lq[:, 0:512].bitcast(U32).indirect(of))
        b = pick("a", lm + ow + in_p, 128 * n, T.fp[:, at], T.lp[:, 0:512].indirect(of))
        named.update({"a%d" % k: a, "b%d" % k: b})
        for j in range(k, k + n):
            x = P([a, b, qw[j]], 128, bank(j), T.wq[:, r(j)], T.ws[:, r(j)], T.fq[:, r(j)], T.fp[:, r(j)])
            w = 128 // OPT["stores"][j]
            for i in range(OPT["stores"][j]):
                at = slice(128 * j + w * i, 128 * j + w * i + w)
                y = named["y%d%s" % (j, "b" * i)] = V([x], w, cp, T.ysb[:, at], bank(j, w, w * i))
                dma("y", [y], LOAD + 1.6 * w, T.y[:, at], T.ysb[:, at], "dst")

    for rule in OPT["order"] + OPT["ranks"][rank]:
        rule = [named[n] for n in rule.split() if n in named]
        for a, b in zip(rule, rule[1:]):
            if a is not b:
                b["after"].append(a)
    for n, s in named.items():
        s["name"] = n
    _arrange(steps)
    order = {q: sorted((s for s in steps if s["q"] == q), key=lambda s: s["at"]) for q in queues}
    for q in queues:
        for s in order[q]:
            if s["sem"] is None:
                counts[q] = counts.get(q, 0) + 1
                s["sem"] = (q, counts[q])
    seen, across = {q: {} for q in queues}, []
    for s in sorted(steps, key=lambda s: (s["at"], s["n"])):
        q = s["q"]
        wants = list(s["deps"])
        if s["kind"] == "across":
            across = [s]
        elif q == "v" and s["kind"] == "":
            wants += across
        s["waits"] = []
        for d in sorted(wants, key=lambda d: -d["end"]) if q else []:
            if seen[q].get(d["sem"][0], 0) < d["sem"][1]:
                if d["sem"][0] == d["q"]:
                    d = max([d] + [e for e in order[d["q"]] if e["sem"][0] == d["q"] and e["end"] + LONG <= s["at"]],
                            key=lambda e: e["sem"][1])
                s["waits"].append(d["sem"])
                for sem, n in [d["sem"]] + list(d["knows"].items()):
                    seen[q][sem] = max(seen[q].get(sem, 0), n)
        s["knows"] = dict(seen[q]) if q else {}
    for q, E in queues.items():
        def need(tokens):
            for sem, n in tokens:
                E.wait_ge(T.sem[sem], n)

        for s in order[q]:
            need(s["waits"])
            done = s["call"]()
            if s["sem"][1] is not None:
                done.then_inc(T.sem[s["sem"][0]], 1 if s["sem"][0] == q else 16)
        if q == "y":
            need([("dst", counts["dst"])])
        if q == "q":
            need([(sem, counts[sem]) for sem in ("loc", "v", "a", "t", "q")])
